import numpy as np
import ml_dtypes


def mxq(x, axis, fmt="e4m3"):
    dtype, down = {"e4m3": (ml_dtypes.float8_e4m3fn, 7), "e5m2": (ml_dtypes.float8_e5m2, 14)}[fmt]
    v = np.moveaxis(np.asarray(x, np.float32).astype(ml_dtypes.bfloat16).astype(np.float64), axis, -1)
    blocks = v.reshape(v.shape[:-1] + (-1, 32))
    amax = np.abs(blocks).max(-1, keepdims=True)
    byte = np.maximum(np.where(amax > 0, np.frexp(amax)[1] - 1 + 127, 0) - down, 1)
    scale = np.exp2(byte - 127.0)
    codes = (blocks / scale).astype(np.float32).astype(dtype).astype(np.float64)
    return np.moveaxis((codes * scale).reshape(v.shape), -1, axis)


WIDE = False


def mx_kscale(k):
    if not WIDE:
        return np.ones(k)
    levels = np.array([10, -10, 5, -5, 0])
    if k % 512:
        return np.exp2(np.random.permutation(np.resize(levels, k // 32))).repeat(32)
    a = np.empty((k // 512, 16))
    for p in range(k // 512):
        a[p, :8] = np.random.permutation(np.resize(levels, 8))
        for g in range(8):
            far = levels[np.abs(levels - a[p, g]) >= 10]
            a[p, g + 8] = far[np.random.randint(len(far))]
    return np.exp2(a.ravel()).repeat(32)


BF16 = ml_dtypes.bfloat16


def bf(x):
    return np.asarray(x, np.float32).astype(BF16)


def f64(x):
    return np.asarray(x).astype(np.float64)


H, T, E, L, S, DV = 2, 4096, 512, 128, 384, 256
N = L + S


def _softmax_last(x):
    m = np.max(x, axis=-1, keepdims=True)
    p = np.exp(x - m)
    return p / np.sum(p, axis=-1, keepdims=True)


def draw0():
    s, t = mx_kscale(E), mx_kscale(N)
    root_n = np.sqrt(N)
    return {"q": bf(np.random.standard_normal((H, T, E)) * 2.0 * s),
            "k": bf(np.random.standard_normal((H, N, E)) / s),
            "v": bf(np.random.standard_normal((H, N, DV)) * 4.0 / root_n / t[:, None]),
            "gate": bf(np.random.uniform(0.5, 1.5, H)),
            "c": bf(np.random.standard_normal((H, N)) * root_n * t)}


def core(q, k, v, gate, c):
    qq = mxq(f64(q), 2, "e4m3")
    kq = mxq(f64(k), 2, "e4m3")
    z = (qq @ kq.transpose(0, 2, 1)) / np.sqrt(E)
    ap = _softmax_last(z[:, :, :L])
    at = _softmax_last(z[:, :, L:])
    gp = np.tanh(f64(gate))[:, None, None] * ap
    a = np.concatenate([gp, at], axis=-1)
    b = a * f64(c)[:, None, :]
    return mxq(b, 2, "e4m3") @ mxq(f64(v), 1, "e4m3")


def e4m3fn_bytes(y):
    return np.clip(np.asarray(y, np.float64), -448.0, 448.0).astype(np.float32).astype(ml_dtypes.float8_e4m3fn).view(np.uint8)


def e4m3fn_values(b):
    return np.asarray(b, np.uint8).view(ml_dtypes.float8_e4m3fn).astype(np.float64)


def setup_inputs():
    d = draw0()
    x0 = np.asarray(d['q']).astype(np.float64)
    s = (np.max(np.abs(x0), axis=(0, 1), keepdims=True) / 448.0).astype(np.float32)
    out = {}
    for k, v in d.items():
        if k == 'q':
            out['q_bytes'] = e4m3fn_bytes(x0 / s.astype(np.float64))
            out['q_scale'] = s
        else:
            out[k] = v
    return out


def reference(q_bytes, q_scale, k, v, gate, c):
    return core(e4m3fn_values(q_bytes) * q_scale.astype(np.float64), k, v, gate, c)

@@ -1,0 +1,385 @@
+from contextlib import ExitStack
+
+import concourse.mybir as mybir
+from concourse.masks import make_identity
+
+H, T, E, L, S, DV = 2, 4096, 512, 128, 384, 256
+N = L + S
+P = 128
+FLOPS = 2 * H * T * N * (E + DV)
+
+F32 = mybir.dt.float32
+BF16 = mybir.dt.bfloat16
+U32 = mybir.dt.uint32
+U8 = mybir.dt.uint8
+FP8 = mybir.dt.float8_e4m3fn
+FP8X4 = mybir.dt.float8_e4m3fn_x4
+ALU = mybir.AluOpType
+ACTF = mybir.ActivationFunctionType
+AX = mybir.AxisListType
+
+TILES = 2
+PAIR = TILES * P
+PAIRS_PER_HEAD = T // PAIR
+PAIRS = H * PAIRS_PER_HEAD
+ROOT = 512.0 ** -0.5
+LEAD = 4
+SEG = ((0, 64), (64, 256))
+
+
+def tile_llamaadaptergatedpromptattention_t_kernel(tc, q_bytes, q_scale, k, v, gate, c, out):
+    nc = tc.nc
+    with ExitStack() as ctx:
+        keep = ctx.enter_context(tc.tile_pool(name="keep", bufs=1))
+        work = ctx.enter_context(tc.tile_pool(name="work", bufs=6))
+        psum = ctx.enter_context(tc.psum_pool(name="psum", bufs=1))
+        ctx.enter_context(tc.manual_schedule())
+
+        ident = keep.tile([P, P], F32)
+        make_identity(nc, ident[:])
+
+        q_raw = keep.tile([P, PAIRS * TILES * E], U8, align_bytes=64)
+        qs = keep.tile([P, E], F32, align_bytes=64)
+        k_raw = keep.tile([P, H, 4, E], BF16, align_bytes=64)
+        v_raw = keep.tile([P, H, 4, DV], BF16, align_bytes=64)
+        c_raw = keep.tile([P, H, N], BF16, align_bytes=64)
+        g_raw = keep.tile([P, H], BF16, align_bytes=64)
+        q_view = q_bytes.rearrange("h (j p i) e -> p (h j) (i e)", p=P, i=TILES)
+        out_view = out.rearrange("h (j p i) d -> (h j) p i d", p=P, i=TILES)
+        row = TILES * E
+
+        def load_q(a, b):
+            nc.sync.dma_start(
+                out=q_raw[:, a * row : b * row].rearrange("p (j x) -> p j x", x=row),
+                in_=q_view[:, a:b, :],
+            )
+
+        load_q(0, 1)
+        nc.sync.dma_start(out=qs[:], in_=q_scale.rearrange("a b e -> (a b e)").partition_broadcast(P))
+        load_q(1, 2)
+        nc.sync.dma_start(out=k_raw[:, 0, :, :], in_=k[0].rearrange("(r j) e -> r j e", j=4))
+        load_q(2, 4)
+        nc.sync.dma_start(out=g_raw[:], in_=gate.partition_broadcast(P))
+        nc.sync.dma_start(out=c_raw[:].rearrange("p h n -> p (h n)"), in_=c.rearrange("h n -> (h n)").partition_broadcast(P))
+        load_q(4, 8)
+        nc.sync.dma_start(out=v_raw[:, 0, :, :], in_=v[0].rearrange("(p t) d -> p t d", t=4))
+        nc.sync.dma_start(out=k_raw[:, 1, :, :], in_=k[1].rearrange("(r j) e -> r j e", j=4))
+        nc.sync.dma_start(out=v_raw[:, 1, :, :], in_=v[1].rearrange("(p t) d -> p t d", t=4))
+        load_q(8, 16)
+        load_q(16, 24)
+        load_q(24, 32)
+
+        tg = keep.tile([P, H], F32)
+        gain = keep.tile([P, H, 2, 256], F32, align_bytes=64)
+        k_codes = keep.tile([P, H, N], U32, align_bytes=64)
+        k_scales = keep.tile([P, H, N], U8, align_bytes=64)
+        v_codes = keep.tile([P, H, DV], U32, align_bytes=64)
+        v_scales = keep.tile([P, H, DV], U8, align_bytes=64)
+
+        def k_transposes(h, w, bank):
+            ps = psum.tile([P, 2, 2, P], F32, name=bank, bufs=1)
+            for e in range(2):
+                words = k_raw[:, h, 2 * w + e, :].bitcast(F32)
+                for u in range(2):
+                    nc.tensor.transpose(ps[:, e, u, :], words[:, u : 256 : 2], ident[:])
+            return ps
+
+        def k_copy(h, w, ps, kg, engine):
+            engine(
+                out=kg[:, w].bitcast(F32).rearrange("p (r e u) -> p r e u", e=2, u=2),
+                in_=ps[:].rearrange("p e u r -> p r e u"),
+            )
+
+        def k_quant(h, kg):
+            nc.vector.quantize_mx(
+                out=k_codes[:, h, :].bitcast(FP8X4),
+                scales=k_scales[:, h, :],
+                in_=kg[:].rearrange("p w x -> p (w x)"),
+            )
+
+        def v_group(h):
+            vg = keep.tile([P, DV, 4], BF16, align_bytes=64, name="v_grouped%d" % h)
+            nc.vector.tensor_copy(out=vg[:], in_=v_raw[:, h].rearrange("p t d -> p d t"))
+            return vg
+
+        def v_quant(h, vg):
+            nc.vector.quantize_mx(
+                out=v_codes[:, h, :].bitcast(FP8X4),
+                scales=v_scales[:, h, :],
+                in_=vg[:].rearrange("p d t -> p (d t)"),
+            )
+
+        def gains(h):
+            src = c_raw[:, h, :].rearrange("p (x u e) -> p u x e", u=2, e=2)
+            dst = gain[:, h].rearrange("p u (x e) -> p u x e", e=2)
+            nc.scalar.activation(
+                out=dst[:, :, 0:32, :], in_=src[:, :, 0:32, :], func=ACTF.Copy, scale=tg[:, h : h + 1]
+            )
+            nc.scalar.copy(out=dst[:, :, 32:128, :], in_=src[:, :, 32:128, :])
+
+        live = {}
+
+        def gain_flip(h):
+            ps = psum.tile([P, 4, P], F32, name="flip_q", bufs=1)
+            flat = gain[:, h].rearrange("p u x -> p (u x)")
+            for g in range(4):
+                nc.tensor.transpose(ps[:, g, :], flat[:, g * P : (g + 1) * P], ident[:])
+            gt = keep.tile([P, 4, P], F32, name="gain_turned%d" % h)
+            nc.scalar.copy(out=gt[:], in_=ps[:])
+            live["gt", h] = gt
+
+        def gain_to_psum(h):
+            cp = psum.tile([P, 2, 256], F32, name="c", bufs=1)
+            flat = cp[:].rearrange("p u x -> p (u x)")
+            for g in range(4):
+                nc.tensor.transpose(flat[:, g * P : (g + 1) * P], live["gt", h][:, g, :], ident[:])
+            live["c", h] = cp
+
+        def cast_q(j):
+            if j < LEAD:
+                return
+            qc = work.tile([P, E], BF16, align_bytes=64, name="q_cast")
+            nc.scalar.copy(out=qc[:], in_=q_raw[:, j * row + E : (j + 1) * row].bitcast(FP8))
+            live["cast", j] = qc
+
+        def scale_q0(j):
+            for i in range(TILES if j < LEAD else 1):
+                qb = work.tile([P, E], BF16, align_bytes=64, name="q_plain%d" % i)
+                a = j * row + i * E
+                nc.vector.tensor_tensor(out=qb[:], in0=q_raw[:, a : a + E].bitcast(FP8), in1=qs[:], op=ALU.mult)
+                live["qb", j, i] = qb
+
+        def hold(j):
+            held = work.tile([P, 1], U32, name="held")
+            nc.gpsimd.tensor_copy(out=held[:], in_=live["qc", j][0][:, 0:1])
+
+        def scale_q1(j):
+            if j < LEAD:
+                return
+            qb = work.tile([P, E], BF16, align_bytes=64, name="q_plain1")
+            nc.gpsimd.tensor_tensor(out=qb[:], in0=live["cast", j][:], in1=qs[:], op=ALU.mult)
+            live["qb", j, 1] = qb
+
+        def flip_q(j):
+            ps = psum.tile([P, 2, 2, P], F32, name="flip_q", bufs=1)
+            for i in range(TILES):
+                words = live["qb", j, i][:].bitcast(F32)
+                for u in range(2):
+                    nc.tensor.transpose(ps[:, i, u, :], words[:, u : 256 : 2], ident[:])
+            live["tq", j] = ps
+
+        def copy_q(j):
+            qg = work.tile([P, PAIR * 4], BF16, align_bytes=64, name="q_grouped")
+            nc.scalar.copy(
+                out=qg[:].bitcast(F32).rearrange("p (i r u) -> p i r u", i=TILES, u=2),
+                in_=live["tq", j][:].rearrange("p i u r -> p i r u"),
+            )
+            live["qg", j] = qg
+
+        def quant_q(j):
+            codes = work.tile([P, PAIR], U32, align_bytes=64, name="q_codes")
+            scales = work.tile([P, PAIR], U8, align_bytes=64, name="q_scales")
+            nc.vector.quantize_mx(out=codes[:].bitcast(FP8X4), scales=scales[:], in_=live["qg", j][:])
+            live["qc", j] = (codes, scales)
+
+        def scores(j):
+            h = j // PAIRS_PER_HEAD
+            codes, scales = live["qc", j]
+            for i in range(TILES):
+                z = psum.tile([P, 2, 256], F32, name="z", bufs=4)
+                nc.tensor.matmul_mx(
+                    out=z[:].rearrange("p u x -> p (u x)"),
+                    lhsT=codes[:, i * P : (i + 1) * P].bitcast(FP8X4),
+                    lhsT_scale=scales[:, i * P : (i + 1) * P],
+                    rhs=k_codes[:, h, :].bitcast(FP8X4),
+                    rhs_scale=k_scales[:, h, :],
+                    start=True,
+                    stop=True,
+                )
+                live["z", j, i] = z
+
+        def maxima(j, i):
+            if ("m", j) not in live:
+                live["m", j] = work.tile([P, 2 * TILES], F32, name="row_max")
+            m = live["m", j]
+            for s, (a, b) in enumerate(SEG):
+                nc.vector.tensor_reduce(
+                    out=m[:, 2 * i + s : 2 * i + s + 1], in_=live["z", j, i][:, :, a:b], axis=AX.XY, op=ALU.max
+                )
+
+        def biases(j):
+            nb = work.tile([P, 2 * TILES], F32, name="neg_max")
+            nc.gpsimd.tensor_scalar(
+                out=nb[:], in0=live["m", j][:], scalar1=-ROOT, scalar2=1.0, op0=ALU.mult, op1=ALU.mult
+            )
+            live["nb", j] = nb
+
+        def exps(j, i):
+            if ("sums", j) not in live:
+                live["sums", j] = work.tile([P, 2 * TILES], F32, name="row_sum")
+            sums = live["sums", j]
+            nb = live["nb", j]
+            ex = work.tile([P, 2, 256], F32, align_bytes=64, name="ex%d" % i)
+            for s, (a, b) in enumerate(SEG):
+                col = slice(2 * i + s, 2 * i + s + 1)
+                nc.scalar.activation(
+                    out=ex[:, :, a:b], in_=live["z", j, i][:, :, a:b], func=ACTF.Exp,
+                    bias=nb[:, col], scale=ROOT, accum_out=sums[:, col],
+                )
+            live["ex", j, i] = ex
+
+        def recips(j):
+            r = work.tile([P, 2 * TILES], F32, name="recip")
+            nc.vector.reciprocal(out=r[:], in_=live["sums", j][:])
+            live["r", j] = r
+
+        def norms(j, i):
+            h = j // PAIRS_PER_HEAD
+            bb = work.tile([P, 2, 256], BF16, align_bytes=64, name="b_plain%d" % i)
+            for s, (a, b) in enumerate(SEG):
+                nc.vector.scalar_tensor_tensor(
+                    out=bb[:, :, a:b], in0=live["ex", j, i][:, :, a:b],
+                    scalar=live["r", j][:, 2 * i + s : 2 * i + s + 1],
+                    in1=live["c", h][:, :, a:b], op0=ALU.mult, op1=ALU.mult,
+                )
+            live["bb", j, i] = bb
+
+        def flip_b(j):
+            ps = psum.tile([P, 2, 2, P], F32, name="flip_b", bufs=1)
+            for i in range(TILES):
+                words = live["bb", j, i][:].rearrange("p u x -> p (u x)").bitcast(F32)
+                for u in range(2):
+                    nc.tensor.transpose(ps[:, i, u, :], words[:, 128 * u : 128 * (u + 1)], ident[:])
+            live["tb", j] = ps
+
+        def copy_b(j):
+            bg = work.tile([P, PAIR * 4], BF16, align_bytes=64, name="b_grouped")
+            nc.scalar.copy(
+                out=bg[:].bitcast(F32).rearrange("p (i r u) -> p i r u", i=TILES, u=2),
+                in_=live["tb", j][:].rearrange("p i u r -> p i r u"),
+            )
+            live["bg", j] = bg
+
+        def quant_b(j):
+            codes = work.tile([P, PAIR], U32, align_bytes=64, name="b_codes")
+            scales = work.tile([P, PAIR], U8, align_bytes=64, name="b_scales")
+            nc.vector.quantize_mx(out=codes[:].bitcast(FP8X4), scales=scales[:], in_=live["bg", j][:])
+            live["bc", j] = (codes, scales)
+
+        def outputs(j):
+            h = j // PAIRS_PER_HEAD
+            codes, scales = live["bc", j]
+            o = psum.tile([P, TILES, DV], F32, name="o", bufs=1)
+            for i in range(TILES):
+                nc.tensor.matmul_mx(
+                    out=o[:, i, :],
+                    lhsT=codes[:, i * P : (i + 1) * P].bitcast(FP8X4),
+                    lhsT_scale=scales[:, i * P : (i + 1) * P],
+                    rhs=v_codes[:, h, :].bitcast(FP8X4),
+                    rhs_scale=v_scales[:, h, :],
+                    start=True,
+                    stop=True,
+                )
+            live["o", j] = o
+
+        def copy_o(j):
+            y = work.tile([P, TILES, DV], F32, align_bytes=64, name="y")
+            nc.scalar.copy(out=y[:], in_=live["o", j][:])
+            nc.sync.dma_start(out=out_view[j], in_=y[:])
+
+        def head_prep(h, part, state):
+            if part == 0:
+                state["kg"] = keep.tile([P, 2, 1024], BF16, align_bytes=64, name="k_grouped%d" % h)
+                ps = k_transposes(h, 0, "flip_b" if h == 0 else "flip_q")
+                k_copy(h, 0, ps, state["kg"], nc.scalar.copy)
+            elif part == 1:
+                ps = k_transposes(h, 1, "o" if h == 0 else "flip_q")
+                k_copy(h, 1, ps, state["kg"], nc.scalar.copy)
+            elif part == 2:
+                k_quant(h, state["kg"])
+            elif part == 3:
+                state["vg"] = v_group(h)
+                if h == 0:
+                    v_quant(h, state["vg"])
+            elif part == 4:
+                gains(h)
+
+        warm = keep.tile([P, 1], F32)
+        nc.scalar.activation(out=warm[:], in_=ident[:, 0:1], func=ACTF.Exp)
+        h0, h1 = {}, {}
+
+        def ok(j):
+            return 0 <= j < PAIRS
+
+        def mid(i):
+            if i == -1:
+                gain_flip(0)
+                gain_to_psum(0)
+            if i in (4, 5):
+                head_prep(1, i - 4, h1)
+            if i == 6:
+                head_prep(1, 2, h1)
+            if i == 7:
+                head_prep(1, 3, h1)
+            if i == 8:
+                gains(1)
+                v_quant(1, h1["vg"])
+            if i == 10:
+                gain_flip(1)
+
+        for i in range(-7, PAIRS + 3):
+            if i == PAIRS_PER_HEAD + 2:
+                gain_to_psum(1)
+            if ok(i + 7):
+                cast_q(i + 7)
+            if ok(i + 1):
+                biases(i + 1)
+            if ok(i + 4):
+                flip_q(i + 4)
+            if ok(i - 2):
+                norms(i - 2, 0)
+            if ok(i - 2):
+                norms(i - 2, 1)
+            if ok(i + 2):
+                scores(i + 2)
+            if ok(i + 4):
+                copy_q(i + 4)
+            mid(i)
+            if ok(i - 3):
+                quant_b(i - 3)
+            if ok(i - 2):
+                flip_b(i - 2)
+            if ok(i - 1):
+                recips(i - 1)
+            if ok(i - 3):
+                outputs(i - 3)
+            if ok(i + 3):
+                quant_q(i + 3)
+            if ok(i + 7):
+                scale_q0(i + 7)
+            if ok(i + 2):
+                maxima(i + 2, 1)
+            if ok(i + 3):
+                hold(i + 3)
+            if ok(i + 1):
+                exps(i + 1, 1)
+            if ok(i + 1):
+                exps(i + 1, 0)
+            if ok(i - 2):
+                copy_b(i - 2)
+            if ok(i + 2):
+                maxima(i + 2, 0)
+            if ok(i + 6):
+                scale_q1(i + 6)
+            if ok(i - 3):
+                copy_o(i - 3)
+            if i == -7:
+                head_prep(0, 0, h0)
+                head_prep(0, 1, h0)
+            if i == -6:
+                head_prep(0, 2, h0)
+            if i == -4:
+                nc.scalar.activation(out=tg[:], in_=g_raw[:], func=ACTF.Tanh)
+                head_prep(0, 4, h0)
+            if i == -1:
+                head_prep(0, 3, h0)

@@ -20,167 +20,215 @@ AX = mybir.AxisListType
 
 TILES = 2
 PAIR = TILES * P
+ROW = TILES * E
 PAIRS_PER_HEAD = T // PAIR
 PAIRS = H * PAIRS_PER_HEAD
 ROOT = 512.0 ** -0.5
-LEAD = 4
+LEAD = 5
+DIRECT = 256
+WIDEN_V = 384
+STAGES = 3
+Q_TO_B = 5
+TAIL = PAIRS - 3
 SEG = ((0, 64), (64, 256))
+Q_LOADS = ((0, 1), (1, 2), (2, 4), (4, 8), (8, 16), (16, 24), (24, 32))
 
 
 def tile_llamaadaptergatedpromptattention_t_kernel(tc, q_bytes, q_scale, k, v, gate, c, out):
     nc = tc.nc
     with ExitStack() as ctx:
         keep = ctx.enter_context(tc.tile_pool(name="keep", bufs=1))
-        work = ctx.enter_context(tc.tile_pool(name="work", bufs=6))
+        work = ctx.enter_context(tc.tile_pool(name="work", bufs=3))
         psum = ctx.enter_context(tc.psum_pool(name="psum", bufs=1))
         ctx.enter_context(tc.manual_schedule())
 
         ident = keep.tile([P, P], F32)
         make_identity(nc, ident[:])
 
-        q_raw = keep.tile([P, PAIRS * TILES * E], U8, align_bytes=64)
-        qs = keep.tile([P, E], F32, align_bytes=64)
-        k_raw = keep.tile([P, H, 4, E], BF16, align_bytes=64)
-        v_raw = keep.tile([P, H, 4, DV], BF16, align_bytes=64)
-        c_raw = keep.tile([P, H, N], BF16, align_bytes=64)
-        g_raw = keep.tile([P, H], BF16, align_bytes=64)
         q_view = q_bytes.rearrange("h (j p i) e -> p (h j) (i e)", p=P, i=TILES)
         out_view = out.rearrange("h (j p i) d -> (h j) p i d", p=P, i=TILES)
-        row = TILES * E
+        q_raw = {}
 
         def load_q(a, b):
-            nc.sync.dma_start(
-                out=q_raw[:, a * row : b * row].rearrange("p (j x) -> p j x", x=row),
-                in_=q_view[:, a:b, :],
-            )
+            raw = keep.tile([P, (b - a) * ROW], U8, align_bytes=64, name="q_raw%d" % a)
+            nc.sync.dma_start(out=raw[:].rearrange("p (j x) -> p j x", x=ROW), in_=q_view[:, a:b, :])
+            for j in range(a, b):
+                q_raw[j] = raw[:, (j - a) * ROW : (j - a + 1) * ROW]
 
-        load_q(0, 1)
-        nc.sync.dma_start(out=qs[:], in_=q_scale.rearrange("a b e -> (a b e)").partition_broadcast(P))
-        load_q(1, 2)
-        nc.sync.dma_start(out=k_raw[:, 0, :, :], in_=k[0].rearrange("(r j) e -> r j e", j=4))
-        load_q(2, 4)
+        def load_rows(src, width, name):
+            raw = keep.tile([P, 4 * width], BF16, align_bytes=64, name=name)
+            nc.sync.dma_start(out=raw[:], in_=src.rearrange("(p t) x -> p (t x)", t=4))
+            return raw
+
+        scale_cols = keep.tile([P, 4], F32)
+        c_cols = keep.tile([P, H, 4], BF16)
+        g_raw = keep.tile([P, H], BF16)
+        k_raw = {}
+
+        def load_keys(half):
+            h, w = divmod(half, 2)
+            raw = keep.tile([P, 2 * E], BF16, align_bytes=64, name="k_raw%d" % half)
+            nc.sync.dma_start(out=raw[:], in_=k[h].rearrange("(p w e) x -> w p (e x)", w=2, e=2)[w])
+            k_raw[half] = raw
+
+        nc.sync.dma_start(out=scale_cols[:], in_=q_scale.rearrange("a b (p t) -> p (a b t)", t=4))
+        load_keys(0)
+        load_q(*Q_LOADS[0])
+        load_keys(1)
+        load_q(*Q_LOADS[1])
         nc.sync.dma_start(out=g_raw[:], in_=gate.partition_broadcast(P))
-        nc.sync.dma_start(out=c_raw[:].rearrange("p h n -> p (h n)"), in_=c.rearrange("h n -> (h n)").partition_broadcast(P))
-        load_q(4, 8)
-        nc.sync.dma_start(out=v_raw[:, 0, :, :], in_=v[0].rearrange("(p t) d -> p t d", t=4))
-        nc.sync.dma_start(out=k_raw[:, 1, :, :], in_=k[1].rearrange("(r j) e -> r j e", j=4))
-        nc.sync.dma_start(out=v_raw[:, 1, :, :], in_=v[1].rearrange("(p t) d -> p t d", t=4))
-        load_q(8, 16)
-        load_q(16, 24)
-        load_q(24, 32)
+        nc.sync.dma_start(out=c_cols[:], in_=c.rearrange("h (p t) -> p h t", t=4))
+        load_q(*Q_LOADS[2])
+        load_q(*Q_LOADS[3])
+        load_keys(2)
+        load_keys(3)
+        v_raw = [load_rows(v[h], DV, "v_raw%d" % h) for h in range(H)]
+        for a, b in Q_LOADS[4:]:
+            load_q(a, b)
 
-        tg = keep.tile([P, H], F32)
-        gain = keep.tile([P, H, 2, 256], F32, align_bytes=64)
+        scales2 = keep.tile([P, ROW], F32, align_bytes=64)
+        gain_cols = keep.tile([P, H, 4], F32)
+        tanh_gate = keep.tile([P, H], F32)
         k_codes = keep.tile([P, H, N], U32, align_bytes=64)
         k_scales = keep.tile([P, H, N], U8, align_bytes=64)
         v_codes = keep.tile([P, H, DV], U32, align_bytes=64)
         v_scales = keep.tile([P, H, DV], U8, align_bytes=64)
+        stage = [keep.tile([P, 2 * ROW], BF16, align_bytes=64, name="stage%d" % n) for n in range(STAGES)]
 
-        def k_transposes(h, w, bank):
-            ps = psum.tile([P, 2, 2, P], F32, name=bank, bufs=1)
-            for e in range(2):
-                words = k_raw[:, h, 2 * w + e, :].bitcast(F32)
-                for u in range(2):
-                    nc.tensor.transpose(ps[:, e, u, :], words[:, u : 256 : 2], ident[:])
-            return ps
+        def q_stage(j):
+            return stage[j % STAGES][:, 0:ROW]
 
-        def k_copy(h, w, ps, kg, engine):
-            engine(
-                out=kg[:, w].bitcast(F32).rearrange("p (r e u) -> p r e u", e=2, u=2),
-                in_=ps[:].rearrange("p e u r -> p r e u"),
-            )
-
-        def k_quant(h, kg):
-            nc.vector.quantize_mx(
-                out=k_codes[:, h, :].bitcast(FP8X4),
-                scales=k_scales[:, h, :],
-                in_=kg[:].rearrange("p w x -> p (w x)"),
-            )
-
-        def v_group(h):
-            vg = keep.tile([P, DV, 4], BF16, align_bytes=64, name="v_grouped%d" % h)
-            nc.vector.tensor_copy(out=vg[:], in_=v_raw[:, h].rearrange("p t d -> p d t"))
-            return vg
-
-        def v_quant(h, vg):
-            nc.vector.quantize_mx(
-                out=v_codes[:, h, :].bitcast(FP8X4),
-                scales=v_scales[:, h, :],
-                in_=vg[:].rearrange("p d t -> p (d t)"),
-            )
-
-        def gains(h):
-            src = c_raw[:, h, :].rearrange("p (x u e) -> p u x e", u=2, e=2)
-            dst = gain[:, h].rearrange("p u (x e) -> p u x e", e=2)
-            nc.scalar.activation(
-                out=dst[:, :, 0:32, :], in_=src[:, :, 0:32, :], func=ACTF.Copy, scale=tg[:, h : h + 1]
-            )
-            nc.scalar.copy(out=dst[:, :, 32:128, :], in_=src[:, :, 32:128, :])
+        def b_stage(j):
+            return stage[(j + Q_TO_B) % STAGES][:, ROW : 2 * ROW]
 
         live = {}
 
-        def gain_flip(h):
-            ps = psum.tile([P, 4, P], F32, name="flip_q", bufs=1)
-            flat = gain[:, h].rearrange("p u x -> p (u x)")
-            for g in range(4):
-                nc.tensor.transpose(ps[:, g, :], flat[:, g * P : (g + 1) * P], ident[:])
-            gt = keep.tile([P, 4, P], F32, name="gain_turned%d" % h)
-            nc.scalar.copy(out=gt[:], in_=ps[:])
-            live["gt", h] = gt
-
-        def gain_to_psum(h):
-            cp = psum.tile([P, 2, 256], F32, name="c", bufs=1)
-            flat = cp[:].rearrange("p u x -> p (u x)")
-            for g in range(4):
-                nc.tensor.transpose(flat[:, g * P : (g + 1) * P], live["gt", h][:, g, :], ident[:])
-            live["c", h] = cp
-
-        def cast_q(j):
-            if j < LEAD:
-                return
-            qc = work.tile([P, E], BF16, align_bytes=64, name="q_cast")
-            nc.scalar.copy(out=qc[:], in_=q_raw[:, j * row + E : (j + 1) * row].bitcast(FP8))
-            live["cast", j] = qc
-
-        def scale_q0(j):
-            for i in range(TILES if j < LEAD else 1):
-                qb = work.tile([P, E], BF16, align_bytes=64, name="q_plain%d" % i)
-                a = j * row + i * E
-                nc.vector.tensor_tensor(out=qb[:], in0=q_raw[:, a : a + E].bitcast(FP8), in1=qs[:], op=ALU.mult)
-                live["qb", j, i] = qb
-
-        def hold(j):
-            held = work.tile([P, 1], U32, name="held")
-            nc.gpsimd.tensor_copy(out=held[:], in_=live["qc", j][0][:, 0:1])
-
-        def scale_q1(j):
-            if j < LEAD:
-                return
-            qb = work.tile([P, E], BF16, align_bytes=64, name="q_plain1")
-            nc.gpsimd.tensor_tensor(out=qb[:], in0=live["cast", j][:], in1=qs[:], op=ALU.mult)
-            live["qb", j, 1] = qb
-
-        def flip_q(j):
-            ps = psum.tile([P, 2, 2, P], F32, name="flip_q", bufs=1)
+        def spread_scales():
+            ps = psum.tile([P, 4, P], F32, name="z", bufs=4)
+            for t in range(4):
+                nc.tensor.transpose(ps[:, t, :], scale_cols[:, t : t + 1].to_broadcast([P, P]), ident[:])
             for i in range(TILES):
-                words = live["qb", j, i][:].bitcast(F32)
+                nc.scalar.copy(
+                    out=scales2[:, i * E : (i + 1) * E].rearrange("m (p t) -> m p t", t=4),
+                    in_=ps[:].rearrange("m t p -> m p t"),
+                )
+
+        def make_gains(unused):
+            nc.scalar.activation(out=tanh_gate[:], in_=g_raw[:], func=ACTF.Tanh)
+            nc.scalar.copy(out=gain_cols[:], in_=c_cols[:])
+            for h in range(H):
+                nc.scalar.activation(
+                    out=gain_cols[0:32, h, :], in_=c_cols[0:32, h, :], func=ACTF.Copy,
+                    scale=tanh_gate[0:32, h : h + 1],
+                )
+
+        def spread_gains(h):
+            ps = psum.tile([P, 2, P, 2], F32, name="gain", bufs=1)
+            for t in range(4):
+                nc.tensor.transpose(
+                    ps[:, t // 2, :, t % 2], gain_cols[:, h, t : t + 1].to_broadcast([P, P]), ident[:]
+                )
+            live["gain", h] = ps[:].rearrange("m u p e -> m u (p e)")
+
+        def turn_keys(half):
+            h, w = divmod(half, 2)
+            if w == 0:
+                live["kg", h] = keep.tile([P, 2, 4 * 2 * P], BF16, align_bytes=64, name="k_grouped%d" % h)
+            ps = psum.tile([P, 2, 2, P], F32, name="turn_b" if half == 0 else "o", bufs=1)
+            for e in range(2):
+                words = k_raw[half][:, e * E : (e + 1) * E].bitcast(F32)
                 for u in range(2):
-                    nc.tensor.transpose(ps[:, i, u, :], words[:, u : 256 : 2], ident[:])
-            live["tq", j] = ps
+                    nc.tensor.transpose(ps[:, e, u, :], words[:, u : 256 : 2], ident[:])
+            live["tk", half] = ps
+
+        def copy_keys(half):
+            h, w = divmod(half, 2)
+            nc.scalar.copy(
+                out=live["kg", h][:, w].bitcast(F32).rearrange("p (r e u) -> p r e u", e=2, u=2),
+                in_=live["tk", half][:].rearrange("p e u r -> p r e u"),
+            )
+
+        def quant_keys(half):
+            h, w = divmod(half, 2)
+            cols = slice(256 * w, 256 * (w + 1))
+            nc.vector.quantize_mx(
+                out=k_codes[:, h, cols].bitcast(FP8X4), scales=k_scales[:, h, cols], in_=live["kg", h][:, w, :]
+            )
+
+        def group_values(h):
+            grouped = keep.tile([P, DV, 4], BF16, align_bytes=64, name="v_grouped%d" % h)
+            nc.scalar.copy(out=grouped[:], in_=v_raw[h][:].rearrange("p (t d) -> p d t", t=4))
+            live["vg", h] = grouped
+
+        def quant_values(h):
+            nc.vector.quantize_mx(
+                out=v_codes[:, h, :].bitcast(FP8X4), scales=v_scales[:, h, :],
+                in_=live["vg", h][:].rearrange("p d t -> p (d t)"),
+            )
+
+        def wide(j):
+            if ("wide", j) not in live:
+                live["wide", j] = work.tile([P, ROW], BF16, align_bytes=64, name="q_wide")
+            return live["wide", j]
+
+        def split(j):
+            return DIRECT if j == LEAD else DIRECT + WIDEN_V
+
+        def widen_scalar(j):
+            if j >= LEAD:
+                a = split(j)
+                nc.scalar.copy(out=wide(j)[:, a:ROW], in_=q_raw[j][:, a:ROW].bitcast(FP8))
+
+        def widen_vector(j):
+            if j > LEAD:
+                b = split(j)
+                nc.vector.tensor_copy(out=wide(j)[:, DIRECT:b], in_=q_raw[j][:, DIRECT:b].bitcast(FP8))
+
+        def scale_vector(j):
+            spans = ((0, E), (E, ROW)) if j < LEAD else ((0, DIRECT),)
+            for a, b in spans:
+                nc.vector.tensor_tensor(
+                    out=q_stage(j)[:, a:b], in0=q_raw[j][:, a:b].bitcast(FP8), in1=scales2[:, a:b], op=ALU.mult
+                )
+
+        def scale_gpsimd(j):
+            if j >= LEAD:
+                nc.gpsimd.tensor_tensor(
+                    out=q_stage(j)[:, DIRECT:ROW], in0=wide(j)[:, DIRECT:ROW], in1=scales2[:, DIRECT:ROW],
+                    op=ALU.mult,
+                )
+
+        def turn(src, bank):
+            ps = psum.tile([P, TILES, 2, P], F32, name=bank, bufs=1)
+            for i in range(TILES):
+                for u in range(2):
+                    nc.tensor.transpose(ps[:, i, u, :], src(i, u), ident[:])
+            return ps
+
+        def copy_turned(dst, ps, copy=nc.scalar.copy):
+            copy(
+                out=dst.bitcast(F32).rearrange("p (i r u) -> p i r u", i=TILES, u=2),
+                in_=ps[:].rearrange("p i u r -> p i r u"),
+            )
+
+        def quantise(j):
+            a = 0 if j < PAIRS else 1
+            b = 2 if j >= Q_TO_B else 1
+            codes = work.tile([P, 2 * PAIR], U32, align_bytes=64, name="codes")
+            scales = work.tile([P, 2 * PAIR], U8, align_bytes=64, name="scales")
+            nc.vector.quantize_mx(
+                out=codes[:, a * PAIR : b * PAIR].bitcast(FP8X4), scales=scales[:, a * PAIR : b * PAIR],
+                in_=stage[j % STAGES][:, a * ROW : b * ROW],
+            )
+            live["qc", j] = (codes[:, 0:PAIR], scales[:, 0:PAIR])
+            live["bc", j - Q_TO_B] = (codes[:, PAIR : 2 * PAIR], scales[:, PAIR : 2 * PAIR])
+
+        def turn_q(j):
+            words = q_stage(j).bitcast(F32)
+            live["tq", j] = turn(lambda i, u: words[:, 256 * i + u : 256 * (i + 1) : 2], {1: "gain", 2: "turn_b"}.get(j, "turn_q"))
 
         def copy_q(j):
-            qg = work.tile([P, PAIR * 4], BF16, align_bytes=64, name="q_grouped")
-            nc.scalar.copy(
-                out=qg[:].bitcast(F32).rearrange("p (i r u) -> p i r u", i=TILES, u=2),
-                in_=live["tq", j][:].rearrange("p i u r -> p i r u"),
-            )
-            live["qg", j] = qg
-
-        def quant_q(j):
-            codes = work.tile([P, PAIR], U32, align_bytes=64, name="q_codes")
-            scales = work.tile([P, PAIR], U8, align_bytes=64, name="q_scales")
-            nc.vector.quantize_mx(out=codes[:].bitcast(FP8X4), scales=scales[:], in_=live["qg", j][:])
-            live["qc", j] = (codes, scales)
+            copy_turned(q_stage(j), live["tq", j], nc.vector.tensor_copy if j == 3 else nc.scalar.copy)
 
         def scores(j):
             h = j // PAIRS_PER_HEAD
@@ -198,78 +246,64 @@ def tile_llamaadaptergatedpromptattention_t_kernel(tc, q_bytes, q_scale, k, v, g
                 )
                 live["z", j, i] = z
 
-        def maxima(j, i):
-            if ("m", j) not in live:
-                live["m", j] = work.tile([P, 2 * TILES], F32, name="row_max")
-            m = live["m", j]
-            for s, (a, b) in enumerate(SEG):
-                nc.vector.tensor_reduce(
-                    out=m[:, 2 * i + s : 2 * i + s + 1], in_=live["z", j, i][:, :, a:b], axis=AX.XY, op=ALU.max
-                )
+        def maxima(j):
+            m = work.tile([P, 2 * TILES], F32, name="row_max")
+            for i in range(TILES):
+                for s, (a, b) in enumerate(SEG):
+                    nc.vector.tensor_reduce(
+                        out=m[:, 2 * i + s : 2 * i + s + 1], in_=live["z", j, i][:, :, a:b], axis=AX.XY, op=ALU.max
+                    )
+            live["m", j] = m
 
         def biases(j):
             nb = work.tile([P, 2 * TILES], F32, name="neg_max")
-            nc.gpsimd.tensor_scalar(
-                out=nb[:], in0=live["m", j][:], scalar1=-ROOT, scalar2=1.0, op0=ALU.mult, op1=ALU.mult
-            )
+            nc.scalar.activation(out=nb[:], in_=live["m", j][:], func=ACTF.Copy, scale=-ROOT)
             live["nb", j] = nb
 
-        def exps(j, i):
-            if ("sums", j) not in live:
-                live["sums", j] = work.tile([P, 2 * TILES], F32, name="row_sum")
-            sums = live["sums", j]
-            nb = live["nb", j]
-            ex = work.tile([P, 2, 256], F32, align_bytes=64, name="ex%d" % i)
-            for s, (a, b) in enumerate(SEG):
-                col = slice(2 * i + s, 2 * i + s + 1)
-                nc.scalar.activation(
-                    out=ex[:, :, a:b], in_=live["z", j, i][:, :, a:b], func=ACTF.Exp,
-                    bias=nb[:, col], scale=ROOT, accum_out=sums[:, col],
-                )
-            live["ex", j, i] = ex
+        def exps(j):
+            sums = work.tile([P, 2 * TILES], F32, name="row_sum")
+            for i in range(TILES):
+                ex = work.tile([P, 2, 256], F32, align_bytes=64, name="ex%d" % i)
+                for s, (a, b) in enumerate(SEG):
+                    col = slice(2 * i + s, 2 * i + s + 1)
+                    nc.scalar.activation(
+                        out=ex[:, :, a:b], in_=live["z", j, i][:, :, a:b], func=ACTF.Exp,
+                        bias=live["nb", j][:, col], scale=ROOT, accum_out=sums[:, col],
+                    )
+                live["ex", j, i] = ex
+            live["sums", j] = sums
 
         def recips(j):
             r = work.tile([P, 2 * TILES], F32, name="recip")
             nc.vector.reciprocal(out=r[:], in_=live["sums", j][:])
             live["r", j] = r
 
-        def norms(j, i):
+        def weights(j):
             h = j // PAIRS_PER_HEAD
-            bb = work.tile([P, 2, 256], BF16, align_bytes=64, name="b_plain%d" % i)
-            for s, (a, b) in enumerate(SEG):
-                nc.vector.scalar_tensor_tensor(
-                    out=bb[:, :, a:b], in0=live["ex", j, i][:, :, a:b],
-                    scalar=live["r", j][:, 2 * i + s : 2 * i + s + 1],
-                    in1=live["c", h][:, :, a:b], op0=ALU.mult, op1=ALU.mult,
-                )
-            live["bb", j, i] = bb
-
-        def flip_b(j):
-            ps = psum.tile([P, 2, 2, P], F32, name="flip_b", bufs=1)
             for i in range(TILES):
-                words = live["bb", j, i][:].rearrange("p u x -> p (u x)").bitcast(F32)
-                for u in range(2):
-                    nc.tensor.transpose(ps[:, i, u, :], words[:, 128 * u : 128 * (u + 1)], ident[:])
-            live["tb", j] = ps
+                bb = work.tile([P, 2, 256], BF16, align_bytes=64, name="b_plain%d" % i)
+                for s, (a, b) in enumerate(SEG):
+                    nc.vector.scalar_tensor_tensor(
+                        out=bb[:, :, a:b], in0=live["ex", j, i][:, :, a:b],
+                        scalar=live["r", j][:, 2 * i + s : 2 * i + s + 1],
+                        in1=live["gain", h][:, :, a:b], op0=ALU.mult, op1=ALU.mult,
+                    )
+                live["bb", j, i] = bb[:].rearrange("p u x -> p (u x)").bitcast(F32)
+
+        def turn_b(j):
+            bank = "turn_q" if j >= TAIL - 1 and j % 2 == 0 else "turn_b"
+            live["tb", j] = turn(lambda i, u: live["bb", j, i][:, P * u : P * (u + 1)], bank)
 
         def copy_b(j):
-            bg = work.tile([P, PAIR * 4], BF16, align_bytes=64, name="b_grouped")
-            nc.scalar.copy(
-                out=bg[:].bitcast(F32).rearrange("p (i r u) -> p i r u", i=TILES, u=2),
-                in_=live["tb", j][:].rearrange("p i u r -> p i r u"),
-            )
-            live["bg", j] = bg
-
-        def quant_b(j):
-            codes = work.tile([P, PAIR], U32, align_bytes=64, name="b_codes")
-            scales = work.tile([P, PAIR], U8, align_bytes=64, name="b_scales")
-            nc.vector.quantize_mx(out=codes[:].bitcast(FP8X4), scales=scales[:], in_=live["bg", j][:])
-            live["bc", j] = (codes, scales)
+            copy_turned(b_stage(j), live["tb", j])
 
         def outputs(j):
             h = j // PAIRS_PER_HEAD
             codes, scales = live["bc", j]
-            o = psum.tile([P, TILES, DV], F32, name="o", bufs=1)
+            if j >= TAIL - 1:
+                o = psum.tile([P, TILES, DV], F32, name="z", bufs=4)
+            else:
+                o = psum.tile([P, TILES, DV], F32, name="o", bufs=1)
             for i in range(TILES):
                 nc.tensor.matmul_mx(
                     out=o[:, i, :],
@@ -283,103 +317,57 @@ def tile_llamaadaptergatedpromptattention_t_kernel(tc, q_bytes, q_scale, k, v, g
             live["o", j] = o
 
         def copy_o(j):
-            y = work.tile([P, TILES, DV], F32, align_bytes=64, name="y")
-            nc.scalar.copy(out=y[:], in_=live["o", j][:])
+            y = work.tile([P, TILES, DV], F32, align_bytes=64, name="y", bufs=5)
+            copy = nc.vector.tensor_copy if j in (PAIRS - 3, PAIRS - 2) else nc.scalar.copy
+            copy(out=y[:], in_=live["o", j][:])
             nc.sync.dma_start(out=out_view[j], in_=y[:])
 
-        def head_prep(h, part, state):
-            if part == 0:
-                state["kg"] = keep.tile([P, 2, 1024], BF16, align_bytes=64, name="k_grouped%d" % h)
-                ps = k_transposes(h, 0, "flip_b" if h == 0 else "flip_q")
-                k_copy(h, 0, ps, state["kg"], nc.scalar.copy)
-            elif part == 1:
-                ps = k_transposes(h, 1, "o" if h == 0 else "flip_q")
-                k_copy(h, 1, ps, state["kg"], nc.scalar.copy)
-            elif part == 2:
-                k_quant(h, state["kg"])
-            elif part == 3:
-                state["vg"] = v_group(h)
-                if h == 0:
-                    v_quant(h, state["vg"])
-            elif part == 4:
-                gains(h)
-
-        warm = keep.tile([P, 1], F32)
-        nc.scalar.activation(out=warm[:], in_=ident[:, 0:1], func=ACTF.Exp)
-        h0, h1 = {}, {}
-
-        def ok(j):
-            return 0 <= j < PAIRS
-
-        def mid(i):
-            if i == -1:
-                gain_flip(0)
-                gain_to_psum(0)
-            if i in (4, 5):
-                head_prep(1, i - 4, h1)
-            if i == 6:
-                head_prep(1, 2, h1)
-            if i == 7:
-                head_prep(1, 3, h1)
-            if i == 8:
-                gains(1)
-                v_quant(1, h1["vg"])
-            if i == 10:
-                gain_flip(1)
-
-        for i in range(-7, PAIRS + 3):
-            if i == PAIRS_PER_HEAD + 2:
-                gain_to_psum(1)
-            if ok(i + 7):
-                cast_q(i + 7)
-            if ok(i + 1):
-                biases(i + 1)
-            if ok(i + 4):
-                flip_q(i + 4)
-            if ok(i - 2):
-                norms(i - 2, 0)
-            if ok(i - 2):
-                norms(i - 2, 1)
-            if ok(i + 2):
-                scores(i + 2)
-            if ok(i + 4):
-                copy_q(i + 4)
-            mid(i)
-            if ok(i - 3):
-                quant_b(i - 3)
-            if ok(i - 2):
-                flip_b(i - 2)
-            if ok(i - 1):
-                recips(i - 1)
-            if ok(i - 3):
-                outputs(i - 3)
-            if ok(i + 3):
-                quant_q(i + 3)
-            if ok(i + 7):
-                scale_q0(i + 7)
-            if ok(i + 2):
-                maxima(i + 2, 1)
-            if ok(i + 3):
-                hold(i + 3)
-            if ok(i + 1):
-                exps(i + 1, 1)
-            if ok(i + 1):
-                exps(i + 1, 0)
-            if ok(i - 2):
-                copy_b(i - 2)
-            if ok(i + 2):
-                maxima(i + 2, 0)
-            if ok(i + 6):
-                scale_q1(i + 6)
-            if ok(i - 3):
-                copy_o(i - 3)
-            if i == -7:
-                head_prep(0, 0, h0)
-                head_prep(0, 1, h0)
-            if i == -6:
-                head_prep(0, 2, h0)
-            if i == -4:
-                nc.scalar.activation(out=tg[:], in_=g_raw[:], func=ACTF.Tanh)
-                head_prep(0, 4, h0)
-            if i == -1:
-                head_prep(0, 3, h0)
+        step = (
+            (quantise, 2), (scale_gpsimd, 5), (exps, 0), (scores, 2), (weights, -1), (copy_o, -4), (outputs, -3),
+            (copy_q, 3), (turn_q, 4), (maxima, 1), (copy_b, -2), (turn_b, -1), (recips, 0),
+            (biases, 1), (widen_scalar, 6), (widen_vector, 6), (scale_vector, 5),
+        )
+        head = (
+            (turn_keys, 0), (copy_keys, 0), (turn_keys, 1), (copy_keys, 1),
+            (scale_vector, 0), (turn_q, 0), (scale_vector, 1), (turn_q, 1), (copy_q, 0), (quant_keys, 0), (quant_keys, 1), (quantise, 0),
+            (copy_q, 1), (scores, 0), (scale_vector, 2), (turn_q, 2), (quantise, 1), (make_gains, 0), (widen_scalar, 5), (maxima, 0),
+            (copy_q, 2), (biases, 0), (scores, 1), (scale_vector, 3), (turn_q, 3), (spread_gains, 0), (scale_vector, 4),
+        )
+        in_place_of = {
+            (outputs, -3): ((turn_keys, 2),),
+            (outputs, -2): ((turn_keys, 3),),
+            (copy_o, -4): ((group_values, 0),),
+            (copy_o, -3): ((copy_keys, 2),),
+            (copy_o, -2): ((copy_keys, 3),),
+            (copy_b, -1): ((group_values, 1),),
+        }
+        before_step = {
+            1: ((quant_values, 0),),
+            2: ((quant_keys, 2),),
+            3: ((quant_keys, 3),),
+            4: ((quant_values, 1),),
+            PAIRS_PER_HEAD + 1: ((spread_gains, 1),),
+        }
+        t = TAIL
+        qb = Q_TO_B
+        tail = (
+            (quantise, t + 2), (exps, t), (scores, t + 2), (maxima, t + 1), (copy_o, t - 4), (outputs, t - 3), (biases, t + 1),
+            (weights, t - 1), (copy_b, t - 2), (turn_b, t - 1), (exps, t + 1), (recips, t), (quantise, t - 2 + qb),
+            (maxima, t + 2), (copy_o, t - 3), (outputs, t - 2), (copy_b, t - 1), (biases, t + 2), (weights, t), (turn_b, t),
+            (exps, t + 2), (quantise, t - 1 + qb), (outputs, t - 1), (recips, t + 1), (copy_b, t), (weights, t + 1), (turn_b, t + 1),
+            (copy_o, t - 2), (recips, t + 2), (quantise, t + qb), (outputs, t), (copy_b, t + 1), (weights, t + 2), (turn_b, t + 2), (copy_o, t - 1),
+            (quantise, t + 1 + qb), (outputs, t + 1), (copy_b, t + 2), (copy_o, t), (quantise, t + 2 + qb), (outputs, t + 2), (copy_o, t + 1), (copy_o, t + 2),
+        )
+        spread_scales()
+        for stage_fn, j in head:
+            stage_fn(j)
+        for s in range(TAIL):
+            for extra, h in before_step.get(s, ()):
+                extra(h)
+            for stage_fn, lead in step:
+                if 0 <= s + lead < PAIRS:
+                    stage_fn(s + lead)
+                for extra, h in in_place_of.get((stage_fn, s + lead), ()):
+                    extra(h)
+        for stage_fn, j in tail:
+            stage_fn(j)

@@ -24,12 +24,14 @@ ROW = TILES * E
 PAIRS_PER_HEAD = T // PAIR
 PAIRS = H * PAIRS_PER_HEAD
 ROOT = 512.0 ** -0.5
-LEAD = 5
-DIRECT = 256
-WIDEN_V = 384
-STAGES = 3
+LEAD = 4
+DIRECT = 160
+O_SCALAR = 352
+STAGES = 2
 Q_TO_B = 5
 TAIL = PAIRS - 3
+SHARED_O = PAIRS - 8
+BOTH = (0, 1)
 SEG = ((0, 64), (64, 256))
 Q_LOADS = ((0, 1), (1, 2), (2, 4), (4, 8), (8, 16), (16, 24), (24, 32))
 
@@ -99,6 +101,8 @@ def tile_llamaadaptergatedpromptattention_t_kernel(tc, q_bytes, q_scale, k, v, g
             return stage[j % STAGES][:, 0:ROW]
 
         def b_stage(j):
+            if j > TAIL:
+                return q_stage(j)
             return stage[(j + Q_TO_B) % STAGES][:, ROW : 2 * ROW]
 
         live = {}
@@ -134,7 +138,7 @@ def tile_llamaadaptergatedpromptattention_t_kernel(tc, q_bytes, q_scale, k, v, g
             h, w = divmod(half, 2)
             if w == 0:
                 live["kg", h] = keep.tile([P, 2, 4 * 2 * P], BF16, align_bytes=64, name="k_grouped%d" % h)
-            ps = psum.tile([P, 2, 2, P], F32, name="turn_b" if half == 0 else "o", bufs=1)
+            ps = psum.tile([P, 2, 2, P], F32, name="turn_b" if half in (0, 3) else "o", bufs=1)
             for e in range(2):
                 words = k_raw[half][:, e * E : (e + 1) * E].bitcast(F32)
                 for u in range(2):
@@ -143,7 +147,8 @@ def tile_llamaadaptergatedpromptattention_t_kernel(tc, q_bytes, q_scale, k, v, g
 
         def copy_keys(half):
             h, w = divmod(half, 2)
-            nc.scalar.copy(
+            copy = nc.vector.tensor_copy if half >= 2 else nc.scalar.copy
+            copy(
                 out=live["kg", h][:, w].bitcast(F32).rearrange("p (r e u) -> p r e u", e=2, u=2),
                 in_=live["tk", half][:].rearrange("p e u r -> p r e u"),
             )
@@ -155,10 +160,15 @@ def tile_llamaadaptergatedpromptattention_t_kernel(tc, q_bytes, q_scale, k, v, g
                 out=k_codes[:, h, cols].bitcast(FP8X4), scales=k_scales[:, h, cols], in_=live["kg", h][:, w, :]
             )
 
-        def group_values(h):
-            grouped = keep.tile([P, DV, 4], BF16, align_bytes=64, name="v_grouped%d" % h)
-            nc.scalar.copy(out=grouped[:], in_=v_raw[h][:].rearrange("p (t d) -> p d t", t=4))
-            live["vg", h] = grouped
+        def group_values(half):
+            h, w = divmod(half, 2)
+            if w == 0:
+                live["vg", h] = keep.tile([P, DV, 4], BF16, align_bytes=64, name="v_grouped%d" % h)
+            cols = slice(w * P, (w + 1) * P)
+            nc.scalar.copy(
+                out=live["vg", h][:, cols, :].rearrange("p (c i) t -> p c t i", i=4),
+                in_=v_raw[h][:].rearrange("p (t d) -> p t d", t=4)[:, :, cols].rearrange("p t (c i) -> p c t i", i=4),
+            )
 
         def quant_values(h):
             nc.vector.quantize_mx(
@@ -171,18 +181,9 @@ def tile_llamaadaptergatedpromptattention_t_kernel(tc, q_bytes, q_scale, k, v, g
                 live["wide", j] = work.tile([P, ROW], BF16, align_bytes=64, name="q_wide")
             return live["wide", j]
 
-        def split(j):
-            return DIRECT if j == LEAD else DIRECT + WIDEN_V
-
-        def widen_scalar(j):
+        def widen(j):
             if j >= LEAD:
-                a = split(j)
-                nc.scalar.copy(out=wide(j)[:, a:ROW], in_=q_raw[j][:, a:ROW].bitcast(FP8))
-
-        def widen_vector(j):
-            if j > LEAD:
-                b = split(j)
-                nc.vector.tensor_copy(out=wide(j)[:, DIRECT:b], in_=q_raw[j][:, DIRECT:b].bitcast(FP8))
+                nc.scalar.copy(out=wide(j)[:, DIRECT:ROW], in_=q_raw[j][:, DIRECT:ROW].bitcast(FP8))
 
         def scale_vector(j):
             spans = ((0, E), (E, ROW)) if j < LEAD else ((0, DIRECT),)
@@ -198,27 +199,26 @@ def tile_llamaadaptergatedpromptattention_t_kernel(tc, q_bytes, q_scale, k, v, g
                     op=ALU.mult,
                 )
 
-        def turn(src, bank):
-            ps = psum.tile([P, TILES, 2, P], F32, name=bank, bufs=1)
-            for i in range(TILES):
+        def turn(src, bank, tiles=BOTH):
+            ps = psum.tile([P, len(tiles), 2, P], F32, name=bank, bufs=1)
+            for n, i in enumerate(tiles):
                 for u in range(2):
-                    nc.tensor.transpose(ps[:, i, u, :], src(i, u), ident[:])
+                    nc.tensor.transpose(ps[:, n, u, :], src(i, u), ident[:])
             return ps
 
-        def copy_turned(dst, ps, copy=nc.scalar.copy):
-            copy(
-                out=dst.bitcast(F32).rearrange("p (i r u) -> p i r u", i=TILES, u=2),
+        def copy_turned(dst, ps):
+            nc.scalar.copy(
+                out=dst.bitcast(F32).rearrange("p (i r u) -> p i r u", r=P, u=2),
                 in_=ps[:].rearrange("p i u r -> p i r u"),
             )
 
         def quantise(j):
-            a = 0 if j < PAIRS else 1
             b = 2 if j >= Q_TO_B else 1
             codes = work.tile([P, 2 * PAIR], U32, align_bytes=64, name="codes")
             scales = work.tile([P, 2 * PAIR], U8, align_bytes=64, name="scales")
             nc.vector.quantize_mx(
-                out=codes[:, a * PAIR : b * PAIR].bitcast(FP8X4), scales=scales[:, a * PAIR : b * PAIR],
-                in_=stage[j % STAGES][:, a * ROW : b * ROW],
+                out=codes[:, 0 : b * PAIR].bitcast(FP8X4), scales=scales[:, 0 : b * PAIR],
+                in_=stage[j % STAGES][:, 0 : b * ROW],
             )
             live["qc", j] = (codes[:, 0:PAIR], scales[:, 0:PAIR])
             live["bc", j - Q_TO_B] = (codes[:, PAIR : 2 * PAIR], scales[:, PAIR : 2 * PAIR])
@@ -228,7 +228,7 @@ def tile_llamaadaptergatedpromptattention_t_kernel(tc, q_bytes, q_scale, k, v, g
             live["tq", j] = turn(lambda i, u: words[:, 256 * i + u : 256 * (i + 1) : 2], {1: "gain", 2: "turn_b"}.get(j, "turn_q"))
 
         def copy_q(j):
-            copy_turned(q_stage(j), live["tq", j], nc.vector.tensor_copy if j == 3 else nc.scalar.copy)
+            copy_turned(q_stage(j), live["tq", j])
 
         def scores(j):
             h = j // PAIRS_PER_HEAD
@@ -273,40 +273,52 @@ def tile_llamaadaptergatedpromptattention_t_kernel(tc, q_bytes, q_scale, k, v, g
                 live["ex", j, i] = ex
             live["sums", j] = sums
 
-        def recips(j):
+        def recips(j, tiles=BOTH):
+            cols = slice(2 * tiles[0], 2 * tiles[-1] + 2)
             r = work.tile([P, 2 * TILES], F32, name="recip")
-            nc.vector.reciprocal(out=r[:], in_=live["sums", j][:])
-            live["r", j] = r
+            nc.vector.reciprocal(out=r[:, cols], in_=live["sums", j][:, cols])
+            for i in tiles:
+                live["r", j, i] = r
 
-        def weights(j):
+        def weights(j, tiles=BOTH):
             h = j // PAIRS_PER_HEAD
-            for i in range(TILES):
+            for i in tiles:
                 bb = work.tile([P, 2, 256], BF16, align_bytes=64, name="b_plain%d" % i)
                 for s, (a, b) in enumerate(SEG):
                     nc.vector.scalar_tensor_tensor(
                         out=bb[:, :, a:b], in0=live["ex", j, i][:, :, a:b],
-                        scalar=live["r", j][:, 2 * i + s : 2 * i + s + 1],
+                        scalar=live["r", j, i][:, 2 * i + s : 2 * i + s + 1],
                         in1=live["gain", h][:, :, a:b], op0=ALU.mult, op1=ALU.mult,
                     )
                 live["bb", j, i] = bb[:].rearrange("p u x -> p (u x)").bitcast(F32)
 
-        def turn_b(j):
-            bank = "turn_q" if j >= TAIL - 1 and j % 2 == 0 else "turn_b"
-            live["tb", j] = turn(lambda i, u: live["bb", j, i][:, P * u : P * (u + 1)], bank)
+        def turn_b(j, tiles=BOTH):
+            bank = "turn_q" if j >= TAIL - 1 and (j + tiles[0]) % 2 == 0 else "turn_b"
+            live["tb", j, tiles] = turn(lambda i, u: live["bb", j, i][:, P * u : P * (u + 1)], bank, tiles)
 
-        def copy_b(j):
-            copy_turned(b_stage(j), live["tb", j])
+        def copy_b(j, tiles=BOTH):
+            copy_turned(b_stage(j)[:, tiles[0] * E : (tiles[-1] + 1) * E], live["tb", j, tiles])
 
-        def outputs(j):
+        def quant_b(j, tiles=BOTH):
+            cols = slice(tiles[0] * P, (tiles[-1] + 1) * P)
+            codes = work.tile([P, 2 * PAIR], U32, align_bytes=64, name="codes")
+            scales = work.tile([P, 2 * PAIR], U8, align_bytes=64, name="scales")
+            nc.vector.quantize_mx(
+                out=codes[:, cols].bitcast(FP8X4), scales=scales[:, cols],
+                in_=b_stage(j)[:, tiles[0] * E : (tiles[-1] + 1) * E],
+            )
+            live["bc", j] = (codes, scales)
+
+        def outputs(j, tiles=BOTH):
             h = j // PAIRS_PER_HEAD
             codes, scales = live["bc", j]
             if j >= TAIL - 1:
-                o = psum.tile([P, TILES, DV], F32, name="z", bufs=4)
+                o = psum.tile([P, len(tiles) * DV], F32, name="z", bufs=4)
             else:
-                o = psum.tile([P, TILES, DV], F32, name="o", bufs=1)
-            for i in range(TILES):
+                o = psum.tile([P, len(tiles) * DV], F32, name="o", bufs=1)
+            for n, i in enumerate(tiles):
                 nc.tensor.matmul_mx(
-                    out=o[:, i, :],
+                    out=o[:, n * DV : (n + 1) * DV],
                     lhsT=codes[:, i * P : (i + 1) * P].bitcast(FP8X4),
                     lhsT_scale=scales[:, i * P : (i + 1) * P],
                     rhs=v_codes[:, h, :].bitcast(FP8X4),
@@ -314,49 +326,64 @@ def tile_llamaadaptergatedpromptattention_t_kernel(tc, q_bytes, q_scale, k, v, g
                     start=True,
                     stop=True,
                 )
-            live["o", j] = o
+            live["o", j, tiles] = o
 
-        def copy_o(j):
-            y = work.tile([P, TILES, DV], F32, align_bytes=64, name="y", bufs=5)
-            copy = nc.vector.tensor_copy if j in (PAIRS - 3, PAIRS - 2) else nc.scalar.copy
-            copy(out=y[:], in_=live["o", j][:])
-            nc.sync.dma_start(out=out_view[j], in_=y[:])
+        def result(j, tiles):
+            if ("y", j, tiles) not in live:
+                live["y", j, tiles] = work.tile([P, len(tiles) * DV], F32, align_bytes=64, name="y", bufs=5)
+            return live["y", j, tiles]
+
+        def copy_o_share(j):
+            if j < SHARED_O:
+                nc.vector.tensor_copy(out=result(j, BOTH)[:, O_SCALAR:], in_=live["o", j, BOTH][:, O_SCALAR:])
+
+        def copy_o(j, tiles=BOTH, copy=nc.scalar.copy):
+            b = O_SCALAR if j < SHARED_O else len(tiles) * DV
+            y = result(j, tiles)
+            copy(out=y[:, 0:b], in_=live["o", j, tiles][:, 0:b])
+            nc.sync.dma_start(
+                out=out_view[j][:, tiles[0] : tiles[-1] + 1, :], in_=y[:].rearrange("p (i d) -> p i d", d=DV)
+            )
+
+        def copy_o_vector(j, tiles=BOTH):
+            copy_o(j, tiles, nc.vector.tensor_copy)
 
         step = (
-            (quantise, 2), (scale_gpsimd, 5), (exps, 0), (scores, 2), (weights, -1), (copy_o, -4), (outputs, -3),
-            (copy_q, 3), (turn_q, 4), (maxima, 1), (copy_b, -2), (turn_b, -1), (recips, 0),
-            (biases, 1), (widen_scalar, 6), (widen_vector, 6), (scale_vector, 5),
+            (quantise, 2), (scale_gpsimd, 4), (turn_q, 3), (outputs, -3), (exps, 0), (scores, 2), (weights, -1),
+            (copy_q, 3), (maxima, 1), (copy_b, -2), (turn_b, -1), (copy_o_share, -3), (recips, 0),
+            (widen, 5), (biases, 1), (copy_o, -3), (scale_vector, 4),
         )
         head = (
             (turn_keys, 0), (copy_keys, 0), (turn_keys, 1), (copy_keys, 1),
             (scale_vector, 0), (turn_q, 0), (scale_vector, 1), (turn_q, 1), (copy_q, 0), (quant_keys, 0), (quant_keys, 1), (quantise, 0),
-            (copy_q, 1), (scores, 0), (scale_vector, 2), (turn_q, 2), (quantise, 1), (make_gains, 0), (widen_scalar, 5), (maxima, 0),
-            (copy_q, 2), (biases, 0), (scores, 1), (scale_vector, 3), (turn_q, 3), (spread_gains, 0), (scale_vector, 4),
+            (copy_q, 1), (scores, 0), (scale_vector, 2), (turn_q, 2), (quantise, 1), (make_gains, 0), (widen, 4), (maxima, 0),
+            (biases, 0), (copy_q, 2), (scores, 1), (spread_gains, 0), (turn_keys, 2), (scale_vector, 3),
         )
         in_place_of = {
-            (outputs, -3): ((turn_keys, 2),),
-            (outputs, -2): ((turn_keys, 3),),
-            (copy_o, -4): ((group_values, 0),),
-            (copy_o, -3): ((copy_keys, 2),),
-            (copy_o, -2): ((copy_keys, 3),),
-            (copy_b, -1): ((group_values, 1),),
+            (outputs, -3): ((turn_keys, 3),),
+            (weights, -1): ((copy_keys, 2), (copy_keys, 3)),
+            (copy_b, -2): ((group_values, 0),),
+            (copy_o, -3): ((group_values, 1),),
+            (copy_b, -1): ((group_values, 2),),
+            (copy_o, -2): ((group_values, 3),),
         }
         before_step = {
-            1: ((quant_values, 0),),
-            2: ((quant_keys, 2),),
+            1: ((quant_keys, 2),),
+            2: ((quant_values, 0),),
             3: ((quant_keys, 3),),
             4: ((quant_values, 1),),
             PAIRS_PER_HEAD + 1: ((spread_gains, 1),),
         }
         t = TAIL
-        qb = Q_TO_B
+        z = t + 2
         tail = (
-            (quantise, t + 2), (exps, t), (scores, t + 2), (maxima, t + 1), (copy_o, t - 4), (outputs, t - 3), (biases, t + 1),
-            (weights, t - 1), (copy_b, t - 2), (turn_b, t - 1), (exps, t + 1), (recips, t), (quantise, t - 2 + qb),
-            (maxima, t + 2), (copy_o, t - 3), (outputs, t - 2), (copy_b, t - 1), (biases, t + 2), (weights, t), (turn_b, t),
-            (exps, t + 2), (quantise, t - 1 + qb), (outputs, t - 1), (recips, t + 1), (copy_b, t), (weights, t + 1), (turn_b, t + 1),
-            (copy_o, t - 2), (recips, t + 2), (quantise, t + qb), (outputs, t), (copy_b, t + 1), (weights, t + 2), (turn_b, t + 2), (copy_o, t - 1),
-            (quantise, t + 1 + qb), (outputs, t + 1), (copy_b, t + 2), (copy_o, t), (quantise, t + 2 + qb), (outputs, t + 2), (copy_o, t + 1), (copy_o, t + 2),
+            (quantise, z), (exps, t), (scores, z), (outputs, t - 3), (maxima, t + 1), (biases, t + 1), (copy_b, t - 2),
+            (weights, t - 1), (turn_b, t - 1), (exps, t + 1), (recips, t), (maxima, z), (copy_o, t - 3), (biases, z), (copy_b, t - 1),
+            (weights, t), (turn_b, t), (exps, z), (recips, t + 1), (quant_b, t - 2), (outputs, t - 2),
+            (weights, t + 1), (copy_b, t), (turn_b, t + 1), (recips, z), (quant_b, t - 1), (outputs, t - 1), (copy_o, t - 2),
+            (weights, z, (0,)), (turn_b, z, (0,)), (copy_b, t + 1), (weights, z, (1,)), (turn_b, z, (1,)), (quant_b, t), (outputs, t),
+            (copy_o, t - 1), (copy_b, z, (0,)), (copy_b, z, (1,)), (quant_b, t + 1), (outputs, t + 1), (copy_o_vector, t), (quant_b, z, (0,)), (outputs, z, (0,)),
+            (quant_b, z, (1,)), (outputs, z, (1,)), (copy_o, t + 1), (copy_o_vector, z, (0,)), (copy_o, z, (1,)),
         )
         spread_scales()
         for stage_fn, j in head:
@@ -369,5 +396,5 @@ def tile_llamaadaptergatedpromptattention_t_kernel(tc, q_bytes, q_scale, k, v, g
                     stage_fn(s + lead)
                 for extra, h in in_place_of.get((stage_fn, s + lead), ()):
                     extra(h)
-        for stage_fn, j in tail:
-            stage_fn(j)
+        for stage_fn, *args in tail:
+            stage_fn(*args)

@@ -25,10 +25,11 @@ PAIRS_PER_HEAD = T // PAIR
 PAIRS = H * PAIRS_PER_HEAD
 ROOT = 512.0 ** -0.5
 LEAD = 4
-DIRECT = 160
-O_SCALAR = 352
-STAGES = 2
-Q_TO_B = 5
+DIRECT = 0
+DIRECT_EARLY = 224
+DIRECT_FIRST = 736
+O_SCALAR = 208
+B_TO_Q = 7
 TAIL = PAIRS - 3
 SHARED_O = PAIRS - 8
 BOTH = (0, 1)
@@ -95,15 +96,15 @@ def tile_llamaadaptergatedpromptattention_t_kernel(tc, q_bytes, q_scale, k, v, g
         k_scales = keep.tile([P, H, N], U8, align_bytes=64)
         v_codes = keep.tile([P, H, DV], U32, align_bytes=64)
         v_scales = keep.tile([P, H, DV], U8, align_bytes=64)
-        stage = [keep.tile([P, 2 * ROW], BF16, align_bytes=64, name="stage%d" % n) for n in range(STAGES)]
+        stage = [keep.tile([P, ROW], BF16, align_bytes=64, name="stage%d" % n) for n in range(3)]
 
         def q_stage(j):
-            return stage[j % STAGES][:, 0:ROW]
+            if 0 < j < B_TO_Q:
+                return stage[j % 2]
+            return stage[(B_TO_Q + 2 - j) % 3] if j else stage[2]
 
         def b_stage(j):
-            if j > TAIL:
-                return q_stage(j)
-            return stage[(j + Q_TO_B) % STAGES][:, ROW : 2 * ROW]
+            return q_stage(j + B_TO_Q)
 
         live = {}
 
@@ -111,11 +112,14 @@ def tile_llamaadaptergatedpromptattention_t_kernel(tc, q_bytes, q_scale, k, v, g
             ps = psum.tile([P, 4, P], F32, name="z", bufs=4)
             for t in range(4):
                 nc.tensor.transpose(ps[:, t, :], scale_cols[:, t : t + 1].to_broadcast([P, P]), ident[:])
-            for i in range(TILES):
+            for a, b in ((0, 64), (64, P)):
                 nc.scalar.copy(
-                    out=scales2[:, i * E : (i + 1) * E].rearrange("m (p t) -> m p t", t=4),
-                    in_=ps[:].rearrange("m t p -> m p t"),
+                    out=scales2[:, 4 * a : 4 * b].rearrange("m (p t) -> m p t", t=4),
+                    in_=ps[:, :, a:b].rearrange("m t p -> m p t"),
                 )
+
+        def repeat_scales(unused):
+            nc.scalar.copy(out=scales2[:, E:ROW], in_=scales2[:, 0:E])
 
         def make_gains(unused):
             nc.scalar.activation(out=tanh_gate[:], in_=g_raw[:], func=ACTF.Tanh)
@@ -181,23 +185,27 @@ def tile_llamaadaptergatedpromptattention_t_kernel(tc, q_bytes, q_scale, k, v, g
                 live["wide", j] = work.tile([P, ROW], BF16, align_bytes=64, name="q_wide")
             return live["wide", j]
 
-        def widen(j):
-            if j >= LEAD:
-                nc.scalar.copy(out=wide(j)[:, DIRECT:ROW], in_=q_raw[j][:, DIRECT:ROW].bitcast(FP8))
+        def direct(j):
+            return DIRECT_FIRST if j < LEAD else DIRECT_EARLY if j < B_TO_Q else DIRECT
 
-        def scale_vector(j):
-            spans = ((0, E), (E, ROW)) if j < LEAD else ((0, DIRECT),)
-            for a, b in spans:
-                nc.vector.tensor_tensor(
-                    out=q_stage(j)[:, a:b], in0=q_raw[j][:, a:b].bitcast(FP8), in1=scales2[:, a:b], op=ALU.mult
-                )
+        def widen(j):
+            a = direct(j)
+            nc.scalar.copy(out=wide(j)[:, a:ROW], in_=q_raw[j][:, a:ROW].bitcast(FP8))
+
+        def scale_vector(j, span=None):
+            a, b = span or (0, direct(j))
+            if a == b:
+                return
+            nc.vector.tensor_tensor(
+                out=q_stage(j)[:, a:b], in0=q_raw[j][:, a:b].bitcast(FP8), in1=scales2[:, a % E : a % E + b - a],
+                op=ALU.mult,
+            )
 
         def scale_gpsimd(j):
-            if j >= LEAD:
-                nc.gpsimd.tensor_tensor(
-                    out=q_stage(j)[:, DIRECT:ROW], in0=wide(j)[:, DIRECT:ROW], in1=scales2[:, DIRECT:ROW],
-                    op=ALU.mult,
-                )
+            a = direct(j)
+            nc.gpsimd.tensor_tensor(
+                out=q_stage(j)[:, a:ROW], in0=wide(j)[:, a:ROW], in1=scales2[:, a:ROW], op=ALU.mult
+            )
 
         def turn(src, bank, tiles=BOTH):
             ps = psum.tile([P, len(tiles), 2, P], F32, name=bank, bufs=1)
@@ -212,23 +220,18 @@ def tile_llamaadaptergatedpromptattention_t_kernel(tc, q_bytes, q_scale, k, v, g
                 in_=ps[:].rearrange("p i u r -> p i r u"),
             )
 
-        def quantise(j):
-            b = 2 if j >= Q_TO_B else 1
-            codes = work.tile([P, 2 * PAIR], U32, align_bytes=64, name="codes")
-            scales = work.tile([P, 2 * PAIR], U8, align_bytes=64, name="scales")
-            nc.vector.quantize_mx(
-                out=codes[:, 0 : b * PAIR].bitcast(FP8X4), scales=scales[:, 0 : b * PAIR],
-                in_=stage[j % STAGES][:, 0 : b * ROW],
-            )
-            live["qc", j] = (codes[:, 0:PAIR], scales[:, 0:PAIR])
-            live["bc", j - Q_TO_B] = (codes[:, PAIR : 2 * PAIR], scales[:, PAIR : 2 * PAIR])
+        def quant_q(j):
+            codes = work.tile([P, PAIR], U32, align_bytes=64, name="q_codes")
+            scales = work.tile([P, PAIR], U8, align_bytes=64, name="q_scales")
+            nc.vector.quantize_mx(out=codes[:].bitcast(FP8X4), scales=scales[:], in_=q_stage(j)[:])
+            live["qc", j] = (codes, scales)
 
         def turn_q(j):
-            words = q_stage(j).bitcast(F32)
+            words = q_stage(j)[:].bitcast(F32)
             live["tq", j] = turn(lambda i, u: words[:, 256 * i + u : 256 * (i + 1) : 2], {1: "gain", 2: "turn_b"}.get(j, "turn_q"))
 
         def copy_q(j):
-            copy_turned(q_stage(j), live["tq", j])
+            copy_turned(q_stage(j)[:], live["tq", j])
 
         def scores(j):
             h = j // PAIRS_PER_HEAD
@@ -301,8 +304,8 @@ def tile_llamaadaptergatedpromptattention_t_kernel(tc, q_bytes, q_scale, k, v, g
 
         def quant_b(j, tiles=BOTH):
             cols = slice(tiles[0] * P, (tiles[-1] + 1) * P)
-            codes = work.tile([P, 2 * PAIR], U32, align_bytes=64, name="codes")
-            scales = work.tile([P, 2 * PAIR], U8, align_bytes=64, name="scales")
+            codes = work.tile([P, PAIR], U32, align_bytes=64, name="b_codes")
+            scales = work.tile([P, PAIR], U8, align_bytes=64, name="b_scales")
             nc.vector.quantize_mx(
                 out=codes[:, cols].bitcast(FP8X4), scales=scales[:, cols],
                 in_=b_stage(j)[:, tiles[0] * E : (tiles[-1] + 1) * E],
@@ -349,21 +352,24 @@ def tile_llamaadaptergatedpromptattention_t_kernel(tc, q_bytes, q_scale, k, v, g
             copy_o(j, tiles, nc.vector.tensor_copy)
 
         step = (
-            (quantise, 2), (scale_gpsimd, 4), (turn_q, 3), (outputs, -3), (exps, 0), (scores, 2), (weights, -1),
-            (copy_q, 3), (maxima, 1), (copy_b, -2), (turn_b, -1), (copy_o_share, -3), (recips, 0),
-            (widen, 5), (biases, 1), (copy_o, -3), (scale_vector, 4),
+            (quant_b, -3), (quant_q, 2), (scale_gpsimd, 4), (turn_q, 3), (outputs, -3), (maxima, 1), (exps, 0), (scores, 2), (weights, -1),
+            (copy_q, 3), (biases, 1), (copy_b, -2), (turn_b, -1), (copy_o_share, -3), (recips, 0),
+            (widen, 5), (copy_o, -3), (scale_vector, 4),
         )
+        tile0, tile1 = (0, E), (E, ROW)
         head = (
             (turn_keys, 0), (copy_keys, 0), (turn_keys, 1), (copy_keys, 1),
-            (scale_vector, 0), (turn_q, 0), (scale_vector, 1), (turn_q, 1), (copy_q, 0), (quant_keys, 0), (quant_keys, 1), (quantise, 0),
-            (copy_q, 1), (scores, 0), (scale_vector, 2), (turn_q, 2), (quantise, 1), (make_gains, 0), (widen, 4), (maxima, 0),
-            (biases, 0), (copy_q, 2), (scores, 1), (spread_gains, 0), (turn_keys, 2), (scale_vector, 3),
+            (scale_vector, 0, (0, E // 2)), (scale_vector, 0, (E // 2, E)), (scale_vector, 0, tile1), (turn_q, 0),
+            (scale_vector, 1, tile0), (scale_vector, 1, tile1), (turn_q, 1), (copy_q, 0), (quant_keys, 0), (quant_keys, 1),
+            (quant_q, 0), (copy_q, 1), (repeat_scales, 0), (widen, 3), (scores, 0), (scale_vector, 2, tile0), (scale_vector, 2, tile1),
+            (turn_q, 2), (quant_q, 1), (scale_gpsimd, 3), (make_gains, 0), (widen, 4), (group_values, 0), (maxima, 0),
+            (biases, 0), (copy_q, 2), (scores, 1), (turn_keys, 2), (turn_keys, 3), (scale_vector, 3, tile0),
+            (scale_vector, 3, (E, DIRECT_FIRST)),
         )
         in_place_of = {
-            (outputs, -3): ((turn_keys, 3),),
+            (turn_b, -1): ((spread_gains, 0),),
             (weights, -1): ((copy_keys, 2), (copy_keys, 3)),
-            (copy_b, -2): ((group_values, 0),),
-            (copy_o, -3): ((group_values, 1),),
+            (copy_b, -2): ((group_values, 1),),
             (copy_b, -1): ((group_values, 2),),
             (copy_o, -2): ((group_values, 3),),
         }
@@ -372,28 +378,29 @@ def tile_llamaadaptergatedpromptattention_t_kernel(tc, q_bytes, q_scale, k, v, g
             2: ((quant_values, 0),),
             3: ((quant_keys, 3),),
             4: ((quant_values, 1),),
-            PAIRS_PER_HEAD + 1: ((spread_gains, 1),),
         }
         t = TAIL
         z = t + 2
         tail = (
-            (quantise, z), (exps, t), (scores, z), (outputs, t - 3), (maxima, t + 1), (biases, t + 1), (copy_b, t - 2),
+            (quant_b, t - 3), (quant_q, z), (exps, t), (scores, z), (outputs, t - 3), (maxima, t + 1), (biases, t + 1), (copy_b, t - 2),
             (weights, t - 1), (turn_b, t - 1), (exps, t + 1), (recips, t), (maxima, z), (copy_o, t - 3), (biases, z), (copy_b, t - 1),
             (weights, t), (turn_b, t), (exps, z), (recips, t + 1), (quant_b, t - 2), (outputs, t - 2),
             (weights, t + 1), (copy_b, t), (turn_b, t + 1), (recips, z), (quant_b, t - 1), (outputs, t - 1), (copy_o, t - 2),
-            (weights, z, (0,)), (turn_b, z, (0,)), (copy_b, t + 1), (weights, z, (1,)), (turn_b, z, (1,)), (quant_b, t), (outputs, t),
-            (copy_o, t - 1), (copy_b, z, (0,)), (copy_b, z, (1,)), (quant_b, t + 1), (outputs, t + 1), (copy_o_vector, t), (quant_b, z, (0,)), (outputs, z, (0,)),
+            (quant_b, t), (outputs, t), (weights, z, (0,)), (turn_b, z, (0,)), (copy_b, t + 1), (copy_o, t - 1), (weights, z, (1,)), (turn_b, z, (1,)),
+            (quant_b, t + 1), (outputs, t + 1), (copy_b, z, (0,)), (copy_o_vector, t), (copy_b, z, (1,)), (quant_b, z, (0,)), (outputs, z, (0,)),
             (quant_b, z, (1,)), (outputs, z, (1,)), (copy_o, t + 1), (copy_o_vector, z, (0,)), (copy_o, z, (1,)),
         )
         spread_scales()
-        for stage_fn, j in head:
-            stage_fn(j)
+        for stage_fn, *args in head:
+            stage_fn(*args)
         for s in range(TAIL):
             for extra, h in before_step.get(s, ()):
                 extra(h)
             for stage_fn, lead in step:
                 if 0 <= s + lead < PAIRS:
                     stage_fn(s + lead)
+                if (stage_fn, s + lead) == (turn_b, PAIRS_PER_HEAD - 1):
+                    spread_gains(1)
                 for extra, h in in_place_of.get((stage_fn, s + lead), ()):
                     extra(h)
         for stage_fn, *args in tail:

@@ -18,22 +18,26 @@ ALU = mybir.AluOpType
 ACTF = mybir.ActivationFunctionType
 AX = mybir.AxisListType
 
+PACK = 4
 TILES = 2
+BOTH = (0, 1)
 PAIR = TILES * P
 ROW = TILES * E
+WORDS = E // 2
 PAIRS_PER_HEAD = T // PAIR
 PAIRS = H * PAIRS_PER_HEAD
 ROOT = 512.0 ** -0.5
+PROMPT_ROWS = L // PACK
+SEGMENTS = ((0, 2 * PROMPT_ROWS), (2 * PROMPT_ROWS, N // 2))
+
 LEAD = 4
-DIRECT = 0
-DIRECT_EARLY = 224
-DIRECT_FIRST = 736
-O_SCALAR = 208
-B_TO_Q = 7
+LAG = 3
+B_TO_Q = LEAD + LAG
 TAIL = PAIRS - 3
-SHARED_O = PAIRS - 8
-BOTH = (0, 1)
-SEG = ((0, 64), (64, 256))
+VECTOR_COLUMNS_FIRST = 736
+VECTOR_COLUMNS_EARLY = 224
+OUT_COLUMNS_SCALAR = 208
+SHARED_OUT_PAIRS = PAIRS - LEAD - LAG - 1
 Q_LOADS = ((0, 1), (1, 2), (2, 4), (4, 8), (8, 16), (16, 24), (24, 32))
 
 
@@ -50,7 +54,7 @@ def tile_llamaadaptergatedpromptattention_t_kernel(tc, q_bytes, q_scale, k, v, g
 
         q_view = q_bytes.rearrange("h (j p i) e -> p (h j) (i e)", p=P, i=TILES)
         out_view = out.rearrange("h (j p i) d -> (h j) p i d", p=P, i=TILES)
-        q_raw = {}
+        q_raw, k_raw, v_raw = {}, {}, {}
 
         def load_q(a, b):
             raw = keep.tile([P, (b - a) * ROW], U8, align_bytes=64, name="q_raw%d" % a)
@@ -58,45 +62,45 @@ def tile_llamaadaptergatedpromptattention_t_kernel(tc, q_bytes, q_scale, k, v, g
             for j in range(a, b):
                 q_raw[j] = raw[:, (j - a) * ROW : (j - a + 1) * ROW]
 
-        def load_rows(src, width, name):
-            raw = keep.tile([P, 4 * width], BF16, align_bytes=64, name=name)
-            nc.sync.dma_start(out=raw[:], in_=src.rearrange("(p t) x -> p (t x)", t=4))
-            return raw
-
-        scale_cols = keep.tile([P, 4], F32)
-        c_cols = keep.tile([P, H, 4], BF16)
-        g_raw = keep.tile([P, H], BF16)
-        k_raw = {}
-
         def load_keys(half):
-            h, w = divmod(half, 2)
+            h, u = divmod(half, 2)
             raw = keep.tile([P, 2 * E], BF16, align_bytes=64, name="k_raw%d" % half)
-            nc.sync.dma_start(out=raw[:], in_=k[h].rearrange("(p w e) x -> w p (e x)", w=2, e=2)[w])
+            nc.sync.dma_start(out=raw[:], in_=k[h].rearrange("(r u e) x -> u r (e x)", u=2, e=2)[u])
             k_raw[half] = raw
 
-        nc.sync.dma_start(out=scale_cols[:], in_=q_scale.rearrange("a b (p t) -> p (a b t)", t=4))
+        def load_values(h):
+            raw = keep.tile([P, PACK * DV], BF16, align_bytes=64, name="v_raw%d" % h)
+            nc.sync.dma_start(out=raw[:], in_=v[h].rearrange("(p t) x -> p (t x)", t=PACK))
+            v_raw[h] = raw
+
+        scale_cols = keep.tile([P, PACK], F32)
+        c_cols = keep.tile([P, H, PACK], BF16)
+        gates = keep.tile([PROMPT_ROWS, H], BF16)
+        nc.sync.dma_start(out=scale_cols[:], in_=q_scale.rearrange("a b (p t) -> p (a b t)", t=PACK))
         load_keys(0)
         load_q(*Q_LOADS[0])
         load_keys(1)
         load_q(*Q_LOADS[1])
-        nc.sync.dma_start(out=g_raw[:], in_=gate.partition_broadcast(P))
-        nc.sync.dma_start(out=c_cols[:], in_=c.rearrange("h (p t) -> p h t", t=4))
+        nc.sync.dma_start(out=gates[:], in_=gate.partition_broadcast(PROMPT_ROWS))
+        nc.sync.dma_start(out=c_cols[:], in_=c.rearrange("h (p t) -> p h t", t=PACK))
         load_q(*Q_LOADS[2])
         load_q(*Q_LOADS[3])
         load_keys(2)
         load_keys(3)
-        v_raw = [load_rows(v[h], DV, "v_raw%d" % h) for h in range(H)]
+        for h in range(H):
+            load_values(h)
         for a, b in Q_LOADS[4:]:
             load_q(a, b)
 
-        scales2 = keep.tile([P, ROW], F32, align_bytes=64)
-        gain_cols = keep.tile([P, H, 4], F32)
-        tanh_gate = keep.tile([P, H], F32)
+        scale_rows = keep.tile([P, ROW], F32, align_bytes=64)
+        gain_cols = keep.tile([P, H, PACK], F32)
+        tanh_gates = keep.tile([PROMPT_ROWS, H], F32)
         k_codes = keep.tile([P, H, N], U32, align_bytes=64)
         k_scales = keep.tile([P, H, N], U8, align_bytes=64)
         v_codes = keep.tile([P, H, DV], U32, align_bytes=64)
         v_scales = keep.tile([P, H, DV], U8, align_bytes=64)
         stage = [keep.tile([P, ROW], BF16, align_bytes=64, name="stage%d" % n) for n in range(3)]
+        live = {}
 
         def q_stage(j):
             if 0 < j < B_TO_Q:
@@ -106,112 +110,104 @@ def tile_llamaadaptergatedpromptattention_t_kernel(tc, q_bytes, q_scale, k, v, g
         def b_stage(j):
             return q_stage(j + B_TO_Q)
 
-        live = {}
-
         def spread_scales():
-            ps = psum.tile([P, 4, P], F32, name="z", bufs=4)
-            for t in range(4):
+            ps = psum.tile([P, PACK, P], F32, name="z", bufs=4)
+            for t in range(PACK):
                 nc.tensor.transpose(ps[:, t, :], scale_cols[:, t : t + 1].to_broadcast([P, P]), ident[:])
-            for a, b in ((0, 64), (64, P)):
+            for a, b in ((0, P // 2), (P // 2, P)):
                 nc.scalar.copy(
-                    out=scales2[:, 4 * a : 4 * b].rearrange("m (p t) -> m p t", t=4),
+                    out=scale_rows[:, PACK * a : PACK * b].rearrange("m (p t) -> m p t", t=PACK),
                     in_=ps[:, :, a:b].rearrange("m t p -> m p t"),
                 )
 
-        def repeat_scales(unused):
-            nc.scalar.copy(out=scales2[:, E:ROW], in_=scales2[:, 0:E])
+        def repeat_scales():
+            nc.scalar.copy(out=scale_rows[:, E:ROW], in_=scale_rows[:, 0:E])
 
-        def make_gains(unused):
-            nc.scalar.activation(out=tanh_gate[:], in_=g_raw[:], func=ACTF.Tanh)
+        def make_gains():
+            nc.scalar.activation(out=tanh_gates[:], in_=gates[:], func=ACTF.Tanh)
             nc.scalar.copy(out=gain_cols[:], in_=c_cols[:])
             for h in range(H):
-                nc.scalar.activation(
-                    out=gain_cols[0:32, h, :], in_=c_cols[0:32, h, :], func=ACTF.Copy,
-                    scale=tanh_gate[0:32, h : h + 1],
-                )
+                prompts = gain_cols[0:PROMPT_ROWS, h, :]
+                nc.scalar.activation(out=prompts, in_=prompts, func=ACTF.Copy, scale=tanh_gates[:, h : h + 1])
 
         def spread_gains(h):
             ps = psum.tile([P, 2, P, 2], F32, name="gain", bufs=1)
-            for t in range(4):
+            for t in range(PACK):
                 nc.tensor.transpose(
                     ps[:, t // 2, :, t % 2], gain_cols[:, h, t : t + 1].to_broadcast([P, P]), ident[:]
                 )
             live["gain", h] = ps[:].rearrange("m u p e -> m u (p e)")
 
-        def turn_keys(half):
-            h, w = divmod(half, 2)
-            if w == 0:
-                live["kg", h] = keep.tile([P, 2, 4 * 2 * P], BF16, align_bytes=64, name="k_grouped%d" % h)
-            ps = psum.tile([P, 2, 2, P], F32, name="turn_b" if half in (0, 3) else "o", bufs=1)
+        def turn_keys(half, bank):
+            ps = psum.tile([P, 2, 2, P], F32, name=bank, bufs=1)
             for e in range(2):
                 words = k_raw[half][:, e * E : (e + 1) * E].bitcast(F32)
                 for u in range(2):
-                    nc.tensor.transpose(ps[:, e, u, :], words[:, u : 256 : 2], ident[:])
-            live["tk", half] = ps
+                    nc.tensor.transpose(ps[:, e, u, :], words[:, u:WORDS:2], ident[:])
+            live["k_turned", half] = ps
 
-        def copy_keys(half):
-            h, w = divmod(half, 2)
-            copy = nc.vector.tensor_copy if half >= 2 else nc.scalar.copy
+        def copy_keys(half, copy):
+            grouped = keep.tile([P, PACK * N // 2], BF16, align_bytes=64, name="k_grouped%d" % half)
             copy(
-                out=live["kg", h][:, w].bitcast(F32).rearrange("p (r e u) -> p r e u", e=2, u=2),
-                in_=live["tk", half][:].rearrange("p e u r -> p r e u"),
+                out=grouped[:].bitcast(F32).rearrange("p (r e u) -> p r e u", e=2, u=2),
+                in_=live["k_turned", half][:].rearrange("p e u r -> p r e u"),
             )
+            live["k_grouped", half] = grouped
 
         def quant_keys(half):
-            h, w = divmod(half, 2)
-            cols = slice(256 * w, 256 * (w + 1))
+            h, u = divmod(half, 2)
+            cols = slice(u * N // 2, (u + 1) * N // 2)
             nc.vector.quantize_mx(
-                out=k_codes[:, h, cols].bitcast(FP8X4), scales=k_scales[:, h, cols], in_=live["kg", h][:, w, :]
+                out=k_codes[:, h, cols].bitcast(FP8X4), scales=k_scales[:, h, cols], in_=live["k_grouped", half][:]
             )
 
         def group_values(half):
             h, w = divmod(half, 2)
             if w == 0:
-                live["vg", h] = keep.tile([P, DV, 4], BF16, align_bytes=64, name="v_grouped%d" % h)
-            cols = slice(w * P, (w + 1) * P)
+                live["v_grouped", h] = keep.tile([P, DV, PACK], BF16, align_bytes=64, name="v_grouped%d" % h)
+            cols = slice(w * DV // 2, (w + 1) * DV // 2)
+            rows = v_raw[h][:].rearrange("p (t d) -> p t d", t=PACK)
             nc.scalar.copy(
-                out=live["vg", h][:, cols, :].rearrange("p (c i) t -> p c t i", i=4),
-                in_=v_raw[h][:].rearrange("p (t d) -> p t d", t=4)[:, :, cols].rearrange("p t (c i) -> p c t i", i=4),
+                out=live["v_grouped", h][:, cols, :].rearrange("p (g i) t -> p g t i", i=4),
+                in_=rows[:, :, cols].rearrange("p t (g i) -> p g t i", i=4),
             )
 
         def quant_values(h):
             nc.vector.quantize_mx(
                 out=v_codes[:, h, :].bitcast(FP8X4), scales=v_scales[:, h, :],
-                in_=live["vg", h][:].rearrange("p d t -> p (d t)"),
+                in_=live["v_grouped", h][:].rearrange("p d t -> p (d t)"),
             )
 
-        def wide(j):
-            if ("wide", j) not in live:
-                live["wide", j] = work.tile([P, ROW], BF16, align_bytes=64, name="q_wide")
-            return live["wide", j]
-
-        def direct(j):
-            return DIRECT_FIRST if j < LEAD else DIRECT_EARLY if j < B_TO_Q else DIRECT
+        def vector_columns(j):
+            return VECTOR_COLUMNS_FIRST if j < LEAD else VECTOR_COLUMNS_EARLY if j < B_TO_Q else 0
 
         def widen(j):
-            a = direct(j)
-            nc.scalar.copy(out=wide(j)[:, a:ROW], in_=q_raw[j][:, a:ROW].bitcast(FP8))
+            a = vector_columns(j)
+            wide = work.tile([P, ROW], BF16, align_bytes=64, name="q_wide")
+            nc.scalar.copy(out=wide[:, a:ROW], in_=q_raw[j][:, a:ROW].bitcast(FP8))
+            live["wide", j] = wide
 
-        def scale_vector(j, span=None):
-            a, b = span or (0, direct(j))
-            if a == b:
-                return
+        def scale_vector(j, a, b):
             nc.vector.tensor_tensor(
-                out=q_stage(j)[:, a:b], in0=q_raw[j][:, a:b].bitcast(FP8), in1=scales2[:, a % E : a % E + b - a],
+                out=q_stage(j)[:, a:b], in0=q_raw[j][:, a:b].bitcast(FP8), in1=scale_rows[:, a % E : a % E + b - a],
                 op=ALU.mult,
             )
 
+        def scale_early(j):
+            if j < B_TO_Q:
+                scale_vector(j, 0, VECTOR_COLUMNS_EARLY)
+
         def scale_gpsimd(j):
-            a = direct(j)
+            a = vector_columns(j)
             nc.gpsimd.tensor_tensor(
-                out=q_stage(j)[:, a:ROW], in0=wide(j)[:, a:ROW], in1=scales2[:, a:ROW], op=ALU.mult
+                out=q_stage(j)[:, a:ROW], in0=live["wide", j][:, a:ROW], in1=scale_rows[:, a:ROW], op=ALU.mult
             )
 
-        def turn(src, bank, tiles=BOTH):
+        def turn(words, bank, tiles):
             ps = psum.tile([P, len(tiles), 2, P], F32, name=bank, bufs=1)
             for n, i in enumerate(tiles):
                 for u in range(2):
-                    nc.tensor.transpose(ps[:, n, u, :], src(i, u), ident[:])
+                    nc.tensor.transpose(ps[:, n, u, :], words(i, u), ident[:])
             return ps
 
         def copy_turned(dst, ps):
@@ -220,24 +216,24 @@ def tile_llamaadaptergatedpromptattention_t_kernel(tc, q_bytes, q_scale, k, v, g
                 in_=ps[:].rearrange("p i u r -> p i r u"),
             )
 
+        def turn_q(j, bank="turn_q"):
+            words = q_stage(j)[:].bitcast(F32)
+            live["q_turned", j] = turn(lambda i, u: words[:, WORDS * i + u : WORDS * (i + 1) : 2], bank, BOTH)
+
+        def copy_q(j):
+            copy_turned(q_stage(j)[:], live["q_turned", j])
+
         def quant_q(j):
             codes = work.tile([P, PAIR], U32, align_bytes=64, name="q_codes")
             scales = work.tile([P, PAIR], U8, align_bytes=64, name="q_scales")
             nc.vector.quantize_mx(out=codes[:].bitcast(FP8X4), scales=scales[:], in_=q_stage(j)[:])
-            live["qc", j] = (codes, scales)
-
-        def turn_q(j):
-            words = q_stage(j)[:].bitcast(F32)
-            live["tq", j] = turn(lambda i, u: words[:, 256 * i + u : 256 * (i + 1) : 2], {1: "gain", 2: "turn_b"}.get(j, "turn_q"))
-
-        def copy_q(j):
-            copy_turned(q_stage(j)[:], live["tq", j])
+            live["q_codes", j] = (codes, scales)
 
         def scores(j):
             h = j // PAIRS_PER_HEAD
-            codes, scales = live["qc", j]
-            for i in range(TILES):
-                z = psum.tile([P, 2, 256], F32, name="z", bufs=4)
+            codes, scales = live["q_codes", j]
+            for i in BOTH:
+                z = psum.tile([P, 2, N // 2], F32, name="z", bufs=4)
                 nc.tensor.matmul_mx(
                     out=z[:].rearrange("p u x -> p (u x)"),
                     lhsT=codes[:, i * P : (i + 1) * P].bitcast(FP8X4),
@@ -250,57 +246,55 @@ def tile_llamaadaptergatedpromptattention_t_kernel(tc, q_bytes, q_scale, k, v, g
                 live["z", j, i] = z
 
         def maxima(j):
-            m = work.tile([P, 2 * TILES], F32, name="row_max")
-            for i in range(TILES):
-                for s, (a, b) in enumerate(SEG):
+            row_max = work.tile([P, 2 * TILES], F32, name="row_max")
+            for i in BOTH:
+                for s, (a, b) in enumerate(SEGMENTS):
                     nc.vector.tensor_reduce(
-                        out=m[:, 2 * i + s : 2 * i + s + 1], in_=live["z", j, i][:, :, a:b], axis=AX.XY, op=ALU.max
+                        out=row_max[:, 2 * i + s : 2 * i + s + 1], in_=live["z", j, i][:, :, a:b], axis=AX.XY, op=ALU.max
                     )
-            live["m", j] = m
+            live["max", j] = row_max
 
         def biases(j):
-            nb = work.tile([P, 2 * TILES], F32, name="neg_max")
-            nc.scalar.activation(out=nb[:], in_=live["m", j][:], func=ACTF.Copy, scale=-ROOT)
-            live["nb", j] = nb
+            bias = work.tile([P, 2 * TILES], F32, name="bias")
+            nc.scalar.activation(out=bias[:], in_=live["max", j][:], func=ACTF.Copy, scale=-ROOT)
+            live["bias", j] = bias
 
         def exps(j):
             sums = work.tile([P, 2 * TILES], F32, name="row_sum")
-            for i in range(TILES):
-                ex = work.tile([P, 2, 256], F32, align_bytes=64, name="ex%d" % i)
-                for s, (a, b) in enumerate(SEG):
+            for i in BOTH:
+                ex = work.tile([P, 2, N // 2], F32, align_bytes=64, name="ex%d" % i)
+                for s, (a, b) in enumerate(SEGMENTS):
                     col = slice(2 * i + s, 2 * i + s + 1)
                     nc.scalar.activation(
                         out=ex[:, :, a:b], in_=live["z", j, i][:, :, a:b], func=ACTF.Exp,
-                        bias=live["nb", j][:, col], scale=ROOT, accum_out=sums[:, col],
+                        bias=live["bias", j][:, col], scale=ROOT, accum_out=sums[:, col],
                     )
                 live["ex", j, i] = ex
             live["sums", j] = sums
 
-        def recips(j, tiles=BOTH):
-            cols = slice(2 * tiles[0], 2 * tiles[-1] + 2)
-            r = work.tile([P, 2 * TILES], F32, name="recip")
-            nc.vector.reciprocal(out=r[:, cols], in_=live["sums", j][:, cols])
-            for i in tiles:
-                live["r", j, i] = r
+        def recips(j):
+            recip = work.tile([P, 2 * TILES], F32, name="recip")
+            nc.vector.reciprocal(out=recip[:], in_=live["sums", j][:])
+            live["recip", j] = recip
 
         def weights(j, tiles=BOTH):
             h = j // PAIRS_PER_HEAD
             for i in tiles:
-                bb = work.tile([P, 2, 256], BF16, align_bytes=64, name="b_plain%d" % i)
-                for s, (a, b) in enumerate(SEG):
+                b_rows = work.tile([P, 2, N // 2], BF16, align_bytes=64, name="b_rows%d" % i)
+                for s, (a, b) in enumerate(SEGMENTS):
                     nc.vector.scalar_tensor_tensor(
-                        out=bb[:, :, a:b], in0=live["ex", j, i][:, :, a:b],
-                        scalar=live["r", j, i][:, 2 * i + s : 2 * i + s + 1],
+                        out=b_rows[:, :, a:b], in0=live["ex", j, i][:, :, a:b],
+                        scalar=live["recip", j][:, 2 * i + s : 2 * i + s + 1],
                         in1=live["gain", h][:, :, a:b], op0=ALU.mult, op1=ALU.mult,
                     )
-                live["bb", j, i] = bb[:].rearrange("p u x -> p (u x)").bitcast(F32)
+                live["b_words", j, i] = b_rows[:].rearrange("p u x -> p (u x)").bitcast(F32)
 
         def turn_b(j, tiles=BOTH):
             bank = "turn_q" if j >= TAIL - 1 and (j + tiles[0]) % 2 == 0 else "turn_b"
-            live["tb", j, tiles] = turn(lambda i, u: live["bb", j, i][:, P * u : P * (u + 1)], bank, tiles)
+            live["b_turned", j, tiles] = turn(lambda i, u: live["b_words", j, i][:, P * u : P * (u + 1)], bank, tiles)
 
         def copy_b(j, tiles=BOTH):
-            copy_turned(b_stage(j)[:, tiles[0] * E : (tiles[-1] + 1) * E], live["tb", j, tiles])
+            copy_turned(b_stage(j)[:, tiles[0] * N : (tiles[-1] + 1) * N], live["b_turned", j, tiles])
 
         def quant_b(j, tiles=BOTH):
             cols = slice(tiles[0] * P, (tiles[-1] + 1) * P)
@@ -308,17 +302,15 @@ def tile_llamaadaptergatedpromptattention_t_kernel(tc, q_bytes, q_scale, k, v, g
             scales = work.tile([P, PAIR], U8, align_bytes=64, name="b_scales")
             nc.vector.quantize_mx(
                 out=codes[:, cols].bitcast(FP8X4), scales=scales[:, cols],
-                in_=b_stage(j)[:, tiles[0] * E : (tiles[-1] + 1) * E],
+                in_=b_stage(j)[:, tiles[0] * N : (tiles[-1] + 1) * N],
             )
-            live["bc", j] = (codes, scales)
+            live["b_codes", j] = (codes, scales)
 
         def outputs(j, tiles=BOTH):
             h = j // PAIRS_PER_HEAD
-            codes, scales = live["bc", j]
-            if j >= TAIL - 1:
-                o = psum.tile([P, len(tiles) * DV], F32, name="z", bufs=4)
-            else:
-                o = psum.tile([P, len(tiles) * DV], F32, name="o", bufs=1)
+            codes, scales = live["b_codes", j]
+            bank, bufs = ("z", 4) if j >= TAIL - 1 else ("o", 1)
+            o = psum.tile([P, len(tiles) * DV], F32, name=bank, bufs=bufs)
             for n, i in enumerate(tiles):
                 nc.tensor.matmul_mx(
                     out=o[:, n * DV : (n + 1) * DV],
@@ -337,71 +329,128 @@ def tile_llamaadaptergatedpromptattention_t_kernel(tc, q_bytes, q_scale, k, v, g
             return live["y", j, tiles]
 
         def copy_o_share(j):
-            if j < SHARED_O:
-                nc.vector.tensor_copy(out=result(j, BOTH)[:, O_SCALAR:], in_=live["o", j, BOTH][:, O_SCALAR:])
+            if j < SHARED_OUT_PAIRS:
+                cols = slice(OUT_COLUMNS_SCALAR, TILES * DV)
+                nc.vector.tensor_copy(out=result(j, BOTH)[:, cols], in_=live["o", j, BOTH][:, cols])
 
         def copy_o(j, tiles=BOTH, copy=nc.scalar.copy):
-            b = O_SCALAR if j < SHARED_O else len(tiles) * DV
+            cols = slice(0, OUT_COLUMNS_SCALAR if j < SHARED_OUT_PAIRS else len(tiles) * DV)
             y = result(j, tiles)
-            copy(out=y[:, 0:b], in_=live["o", j, tiles][:, 0:b])
+            copy(out=y[:, cols], in_=live["o", j, tiles][:, cols])
             nc.sync.dma_start(
                 out=out_view[j][:, tiles[0] : tiles[-1] + 1, :], in_=y[:].rearrange("p (i d) -> p i d", d=DV)
             )
 
-        def copy_o_vector(j, tiles=BOTH):
-            copy_o(j, tiles, nc.vector.tensor_copy)
+        spread_scales()
+        for half, bank in ((0, "turn_b"), (1, "o")):
+            turn_keys(half, bank)
+            copy_keys(half, nc.scalar.copy)
+        scale_vector(0, 0, E // 2)
+        scale_vector(0, E // 2, E)
+        scale_vector(0, E, ROW)
+        turn_q(0)
+        scale_vector(1, 0, E)
+        scale_vector(1, E, ROW)
+        turn_q(1, "gain")
+        copy_q(0)
+        quant_keys(0)
+        quant_keys(1)
+        quant_q(0)
+        copy_q(1)
+        repeat_scales()
+        widen(3)
+        scores(0)
+        scale_vector(2, 0, E)
+        scale_vector(2, E, ROW)
+        turn_q(2, "turn_b")
+        quant_q(1)
+        scale_gpsimd(3)
+        make_gains()
+        widen(4)
+        group_values(0)
+        maxima(0)
+        biases(0)
+        copy_q(2)
+        scores(1)
+        turn_keys(2, "o")
+        turn_keys(3, "turn_b")
+        scale_vector(3, 0, E)
+        scale_vector(3, E, VECTOR_COLUMNS_FIRST)
 
         step = (
-            (quant_b, -3), (quant_q, 2), (scale_gpsimd, 4), (turn_q, 3), (outputs, -3), (maxima, 1), (exps, 0), (scores, 2), (weights, -1),
-            (copy_q, 3), (biases, 1), (copy_b, -2), (turn_b, -1), (copy_o_share, -3), (recips, 0),
-            (widen, 5), (copy_o, -3), (scale_vector, 4),
+            (quant_b, -LAG), (quant_q, 2), (scale_gpsimd, LEAD), (turn_q, 3), (outputs, -LAG), (maxima, 1),
+            (exps, 0), (scores, 2), (weights, -1), (copy_q, 3), (biases, 1), (copy_b, -2), (turn_b, -1),
+            (copy_o_share, -LAG), (recips, 0), (widen, LEAD + 1), (copy_o, -LAG), (scale_early, LEAD),
         )
-        tile0, tile1 = (0, E), (E, ROW)
-        head = (
-            (turn_keys, 0), (copy_keys, 0), (turn_keys, 1), (copy_keys, 1),
-            (scale_vector, 0, (0, E // 2)), (scale_vector, 0, (E // 2, E)), (scale_vector, 0, tile1), (turn_q, 0),
-            (scale_vector, 1, tile0), (scale_vector, 1, tile1), (turn_q, 1), (copy_q, 0), (quant_keys, 0), (quant_keys, 1),
-            (quant_q, 0), (copy_q, 1), (repeat_scales, 0), (widen, 3), (scores, 0), (scale_vector, 2, tile0), (scale_vector, 2, tile1),
-            (turn_q, 2), (quant_q, 1), (scale_gpsimd, 3), (make_gains, 0), (widen, 4), (group_values, 0), (maxima, 0),
-            (biases, 0), (copy_q, 2), (scores, 1), (turn_keys, 2), (turn_keys, 3), (scale_vector, 3, tile0),
-            (scale_vector, 3, (E, DIRECT_FIRST)),
-        )
-        in_place_of = {
-            (turn_b, -1): ((spread_gains, 0),),
-            (weights, -1): ((copy_keys, 2), (copy_keys, 3)),
-            (copy_b, -2): ((group_values, 1),),
-            (copy_b, -1): ((group_values, 2),),
-            (copy_o, -2): ((group_values, 3),),
+        behind = {
+            (weights, -1): lambda: [copy_keys(half, nc.vector.tensor_copy) for half in (2, 3)],
+            (turn_b, -1): lambda: spread_gains(0),
+            (copy_b, -2): lambda: group_values(1),
+            (copy_b, -1): lambda: group_values(2),
+            (copy_o, -2): lambda: group_values(3),
+            (turn_b, PAIRS_PER_HEAD - 1): lambda: spread_gains(1),
         }
-        before_step = {
-            1: ((quant_keys, 2),),
-            2: ((quant_values, 0),),
-            3: ((quant_keys, 3),),
-            4: ((quant_values, 1),),
-        }
-        t = TAIL
-        z = t + 2
-        tail = (
-            (quant_b, t - 3), (quant_q, z), (exps, t), (scores, z), (outputs, t - 3), (maxima, t + 1), (biases, t + 1), (copy_b, t - 2),
-            (weights, t - 1), (turn_b, t - 1), (exps, t + 1), (recips, t), (maxima, z), (copy_o, t - 3), (biases, z), (copy_b, t - 1),
-            (weights, t), (turn_b, t), (exps, z), (recips, t + 1), (quant_b, t - 2), (outputs, t - 2),
-            (weights, t + 1), (copy_b, t), (turn_b, t + 1), (recips, z), (quant_b, t - 1), (outputs, t - 1), (copy_o, t - 2),
-            (quant_b, t), (outputs, t), (weights, z, (0,)), (turn_b, z, (0,)), (copy_b, t + 1), (copy_o, t - 1), (weights, z, (1,)), (turn_b, z, (1,)),
-            (quant_b, t + 1), (outputs, t + 1), (copy_b, z, (0,)), (copy_o_vector, t), (copy_b, z, (1,)), (quant_b, z, (0,)), (outputs, z, (0,)),
-            (quant_b, z, (1,)), (outputs, z, (1,)), (copy_o, t + 1), (copy_o_vector, z, (0,)), (copy_o, z, (1,)),
-        )
-        spread_scales()
-        for stage_fn, *args in head:
-            stage_fn(*args)
+        extra_quants = {1: (quant_keys, 2), 2: (quant_values, 0), 3: (quant_keys, 3), 4: (quant_values, 1)}
         for s in range(TAIL):
-            for extra, h in before_step.get(s, ()):
-                extra(h)
-            for stage_fn, lead in step:
-                if 0 <= s + lead < PAIRS:
-                    stage_fn(s + lead)
-                if (stage_fn, s + lead) == (turn_b, PAIRS_PER_HEAD - 1):
-                    spread_gains(1)
-                for extra, h in in_place_of.get((stage_fn, s + lead), ()):
-                    extra(h)
-        for stage_fn, *args in tail:
-            stage_fn(*args)
+            if s in extra_quants:
+                quant, which = extra_quants[s]
+                quant(which)
+            for stage_fn, ahead in step:
+                if 0 <= s + ahead < PAIRS:
+                    stage_fn(s + ahead)
+                if (stage_fn, s + ahead) in behind:
+                    behind[stage_fn, s + ahead]()
+
+        third, next_to_last, last = TAIL, TAIL + 1, TAIL + 2
+        first, second = (0,), (1,)
+        quant_b(third - 3)
+        quant_q(last)
+        exps(third)
+        scores(last)
+        outputs(third - 3)
+        maxima(next_to_last)
+        biases(next_to_last)
+        copy_b(third - 2)
+        weights(third - 1)
+        turn_b(third - 1)
+
+        exps(next_to_last)
+        recips(third)
+        maxima(last)
+        copy_o(third - 3)
+        biases(last)
+        copy_b(third - 1)
+        weights(third)
+        turn_b(third)
+
+        exps(last)
+        recips(next_to_last)
+        quant_b(third - 2)
+        outputs(third - 2)
+        weights(next_to_last)
+        copy_b(third)
+        turn_b(next_to_last)
+        recips(last)
+        quant_b(third - 1)
+        outputs(third - 1)
+        copy_o(third - 2)
+        quant_b(third)
+        outputs(third)
+
+        weights(last, first)
+        turn_b(last, first)
+        copy_b(next_to_last)
+        copy_o(third - 1)
+        weights(last, second)
+        turn_b(last, second)
+        quant_b(next_to_last)
+        outputs(next_to_last)
+        copy_b(last, first)
+        copy_o(third, BOTH, nc.vector.tensor_copy)
+        copy_b(last, second)
+        for tile in (first, second):
+            quant_b(last, tile)
+            outputs(last, tile)
+        copy_o(next_to_last)
+        copy_o(last, first, nc.vector.tensor_copy)
+        copy_o(last, second)

@@ -32,13 +32,11 @@ SEGMENTS = ((0, 2 * PROMPT_ROWS), (2 * PROMPT_ROWS, N // 2))
 
 LEAD = 4
 LAG = 3
-B_TO_Q = LEAD + LAG
 TAIL = PAIRS - 3
-VECTOR_COLUMNS_FIRST = 736
-VECTOR_COLUMNS_EARLY = 224
-OUT_COLUMNS_SCALAR = 208
-SHARED_OUT_PAIRS = PAIRS - LEAD - LAG - 1
-Q_LOADS = ((0, 1), (1, 2), (2, 4), (4, 8), (8, 16), (16, 24), (24, 32))
+WIDEN_LONG = 320
+WIDEN_SHORT = 832
+HEAD_TILES = (0, 0, 2, 0)
+Q_LOADS = ((0, 1), (1, 2), (2, 3), (3, 4), (4, 6), (6, 8), (8, 16), (16, 24), (24, 32))
 
 
 def tile_llamaadaptergatedpromptattention_t_kernel(tc, q_bytes, q_scale, k, v, gate, c, out):
@@ -77,51 +75,59 @@ def tile_llamaadaptergatedpromptattention_t_kernel(tc, q_bytes, q_scale, k, v, g
         c_cols = keep.tile([P, H, PACK], BF16)
         gates = keep.tile([PROMPT_ROWS, H], BF16)
         nc.sync.dma_start(out=scale_cols[:], in_=q_scale.rearrange("a b (p t) -> p (a b t)", t=PACK))
-        load_keys(0)
         load_q(*Q_LOADS[0])
+        load_keys(0)
         load_keys(1)
-        load_q(*Q_LOADS[1])
+        for a, b in Q_LOADS[1:5]:
+            load_q(a, b)
         nc.sync.dma_start(out=gates[:], in_=gate.partition_broadcast(PROMPT_ROWS))
         nc.sync.dma_start(out=c_cols[:], in_=c.rearrange("h (p t) -> p h t", t=PACK))
-        load_q(*Q_LOADS[2])
-        load_q(*Q_LOADS[3])
         load_keys(2)
         load_keys(3)
-        for h in range(H):
-            load_values(h)
-        for a, b in Q_LOADS[4:]:
+        load_values(0)
+        load_values(1)
+        for a, b in Q_LOADS[5:]:
             load_q(a, b)
 
-        scale_rows = keep.tile([P, ROW], F32, align_bytes=64)
+        scale_rows = keep.tile([P, E], F32, align_bytes=64)
         gain_cols = keep.tile([P, H, PACK], F32)
         tanh_gates = keep.tile([PROMPT_ROWS, H], F32)
         k_codes = keep.tile([P, H, N], U32, align_bytes=64)
         k_scales = keep.tile([P, H, N], U8, align_bytes=64)
         v_codes = keep.tile([P, H, DV], U32, align_bytes=64)
         v_scales = keep.tile([P, H, DV], U8, align_bytes=64)
-        stage = [keep.tile([P, ROW], BF16, align_bytes=64, name="stage%d" % n) for n in range(3)]
+        stage = [keep.tile([P, 2 * ROW], BF16, align_bytes=64, name="stage%d" % n) for n in range(2)]
+        ring = [keep.tile([P, N], F32, align_bytes=64, name="ring%d" % n) for n in range(4)]
         live = {}
 
+        early = [keep.tile([P, ROW], BF16, align_bytes=64, name="early%d" % n) for n in range(LEAD)]
+
         def q_stage(j):
-            if 0 < j < B_TO_Q:
-                return stage[j % 2]
-            return stage[(B_TO_Q + 2 - j) % 3] if j else stage[2]
+            return early[j][:] if j < LEAD else stage[j % 2][:, ROW : 2 * ROW]
 
         def b_stage(j):
-            return q_stage(j + B_TO_Q)
+            return stage[(j + LAG) % 2][:, 0:ROW]
+
+        def q_scaled(j):
+            if j == 2:
+                return live["k_grouped", 0][:]
+            if j < LEAD + 2:
+                return q_stage(j - 3)
+            return ring[(j - LEAD - 2) % 4][:].bitcast(BF16)
+
+        def gpsimd_tiles(j):
+            return HEAD_TILES[j] if j < LEAD else 1 + j % 2
 
         def spread_scales():
             ps = psum.tile([P, PACK, P], F32, name="z", bufs=4)
             for t in range(PACK):
                 nc.tensor.transpose(ps[:, t, :], scale_cols[:, t : t + 1].to_broadcast([P, P]), ident[:])
-            for a, b in ((0, P // 2), (P // 2, P)):
-                nc.scalar.copy(
-                    out=scale_rows[:, PACK * a : PACK * b].rearrange("m (p t) -> m p t", t=PACK),
-                    in_=ps[:, :, a:b].rearrange("m t p -> m p t"),
-                )
+            live["scales"] = ps
 
-        def repeat_scales():
-            nc.scalar.copy(out=scale_rows[:, E:ROW], in_=scale_rows[:, 0:E])
+        def copy_scales():
+            nc.scalar.copy(
+                out=scale_rows[:].rearrange("m (p t) -> m p t", t=PACK), in_=live["scales"][:].rearrange("m t p -> m p t")
+            )
 
         def make_gains():
             nc.scalar.activation(out=tanh_gates[:], in_=gates[:], func=ACTF.Tanh)
@@ -138,12 +144,20 @@ def tile_llamaadaptergatedpromptattention_t_kernel(tc, q_bytes, q_scale, k, v, g
                 )
             live["gain", h] = ps[:].rearrange("m u p e -> m u (p e)")
 
+        def sort_keys(half):
+            words = keep.tile([P, 2, 2, P], F32, align_bytes=64, name="k_sorted%d" % half)
+            nc.vector.tensor_copy(
+                out=words[:], in_=k_raw[half][:].bitcast(F32).rearrange("r (e p u) -> r e u p", e=2, u=2)
+            )
+            live["k_sorted", half] = words
+
         def turn_keys(half, bank):
             ps = psum.tile([P, 2, 2, P], F32, name=bank, bufs=1)
             for e in range(2):
                 words = k_raw[half][:, e * E : (e + 1) * E].bitcast(F32)
                 for u in range(2):
-                    nc.tensor.transpose(ps[:, e, u, :], words[:, u:WORDS:2], ident[:])
+                    rows = live["k_sorted", half][:, e, u, :] if ("k_sorted", half) in live else words[:, u:WORDS:2]
+                    nc.tensor.transpose(ps[:, e, u, :], rows, ident[:])
             live["k_turned", half] = ps
 
         def copy_keys(half, copy):
@@ -178,29 +192,27 @@ def tile_llamaadaptergatedpromptattention_t_kernel(tc, q_bytes, q_scale, k, v, g
                 in_=live["v_grouped", h][:].rearrange("p d t -> p (d t)"),
             )
 
-        def vector_columns(j):
-            return VECTOR_COLUMNS_FIRST if j < LEAD else VECTOR_COLUMNS_EARLY if j < B_TO_Q else 0
+        def widen(j, a, b, copy):
+            if ("wide", j) not in live:
+                live["wide", j] = work.tile([P, ROW], BF16, align_bytes=64, name="q_wide", bufs=6)
+            if a < b:
+                copy(out=live["wide", j][:, a:b], in_=q_raw[j][:, a:b].bitcast(FP8))
 
-        def widen(j):
-            a = vector_columns(j)
-            wide = work.tile([P, ROW], BF16, align_bytes=64, name="q_wide")
-            nc.scalar.copy(out=wide[:, a:ROW], in_=q_raw[j][:, a:ROW].bitcast(FP8))
-            live["wide", j] = wide
+        def gpsimd_columns(j):
+            return WIDEN_SHORT if j % 2 else WIDEN_LONG
 
-        def scale_vector(j, a, b):
-            nc.vector.tensor_tensor(
-                out=q_stage(j)[:, a:b], in0=q_raw[j][:, a:b].bitcast(FP8), in1=scale_rows[:, a % E : a % E + b - a],
-                op=ALU.mult,
-            )
+        def widen_gpsimd(j):
+            widen(j, 0, gpsimd_columns(j), nc.gpsimd.tensor_copy)
 
-        def scale_early(j):
-            if j < B_TO_Q:
-                scale_vector(j, 0, VECTOR_COLUMNS_EARLY)
+        def widen_scalar(j):
+            widen(j, gpsimd_columns(j), ROW, nc.scalar.copy)
 
         def scale_gpsimd(j):
-            a = vector_columns(j)
+            n = gpsimd_tiles(j)
             nc.gpsimd.tensor_tensor(
-                out=q_stage(j)[:, a:ROW], in0=live["wide", j][:, a:ROW], in1=scale_rows[:, a:ROW], op=ALU.mult
+                out=q_scaled(j)[:, 0 : n * E].rearrange("p (i x) -> p i x", x=E),
+                in0=live["wide", j][:, 0 : n * E].rearrange("p (i x) -> p i x", x=E),
+                in1=scale_rows[:].unsqueeze(1).to_broadcast([P, n, E]), op=ALU.mult,
             )
 
         def turn(words, bank, tiles):
@@ -213,21 +225,47 @@ def tile_llamaadaptergatedpromptattention_t_kernel(tc, q_bytes, q_scale, k, v, g
         def copy_turned(dst, ps):
             nc.scalar.copy(
                 out=dst.bitcast(F32).rearrange("p (i r u) -> p i r u", r=P, u=2),
-                in_=ps[:].rearrange("p i u r -> p i r u"),
+                in_=ps.rearrange("p i u r -> p i r u"),
             )
 
         def turn_q(j, bank="turn_q"):
-            words = q_stage(j)[:].bitcast(F32)
-            live["q_turned", j] = turn(lambda i, u: words[:, WORDS * i + u : WORDS * (i + 1) : 2], bank, BOTH)
+            rows = [q_scaled(j) if i < gpsimd_tiles(j) else live["wide", j][:] for i in BOTH]
+            live["q_turned", j] = turn(
+                lambda i, u: rows[i].bitcast(F32)[:, WORDS * i + u : WORDS * (i + 1) : 2], bank, BOTH
+            )
 
         def copy_q(j):
-            copy_turned(q_stage(j)[:], live["q_turned", j])
+            n = gpsimd_tiles(j)
+            if n:
+                copy_turned(q_stage(j)[:, 0 : n * E], live["q_turned", j][:, 0:n])
+
+        def scale_turned(j, tiles=BOTH):
+            for i in tiles:
+                if i >= gpsimd_tiles(j):
+                    turned = live["q_turned", j][:, i].rearrange("p u r -> p (u r)").bitcast(BF16)
+                    nc.vector.tensor_tensor(
+                        out=q_stage(j)[:, i * E : (i + 1) * E].rearrange("p (r u e) -> p r u e", u=2, e=2),
+                        in0=turned.rearrange("p (u r e) -> p r u e", u=2, e=2),
+                        in1=scale_cols[:].rearrange("p (u e) -> p u e", e=2).unsqueeze(1).to_broadcast([P, P, 2, 2]),
+                        op=ALU.mult,
+                    )
 
         def quant_q(j):
-            codes = work.tile([P, PAIR], U32, align_bytes=64, name="q_codes")
-            scales = work.tile([P, PAIR], U8, align_bytes=64, name="q_scales")
-            nc.vector.quantize_mx(out=codes[:].bitcast(FP8X4), scales=scales[:], in_=q_stage(j)[:])
+            codes = work.tile([P, PAIR], U32, align_bytes=64, name="q_codes", bufs=LEAD)
+            scales = work.tile([P, PAIR], U8, align_bytes=64, name="q_scales", bufs=LEAD)
+            nc.vector.quantize_mx(out=codes[:].bitcast(FP8X4), scales=scales[:], in_=q_stage(j))
             live["q_codes", j] = (codes, scales)
+
+        def quant(s):
+            a = 0 if s >= LAG else PAIR
+            b = 2 * PAIR if s + 2 < PAIRS else PAIR
+            codes = work.tile([P, 2 * PAIR], U32, align_bytes=64, name="codes")
+            scales = work.tile([P, 2 * PAIR], U8, align_bytes=64, name="scales")
+            nc.vector.quantize_mx(
+                out=codes[:, a:b].bitcast(FP8X4), scales=scales[:, a:b], in_=stage[s % 2][:, PACK * a : PACK * b]
+            )
+            live["b_codes", s - LAG] = (codes[:, 0:PAIR], scales[:, 0:PAIR])
+            live["q_codes", s + 2] = (codes[:, PAIR:], scales[:, PAIR:])
 
         def scores(j):
             h = j // PAIRS_PER_HEAD
@@ -245,29 +283,34 @@ def tile_llamaadaptergatedpromptattention_t_kernel(tc, q_bytes, q_scale, k, v, g
                 )
                 live["z", j, i] = z
 
-        def maxima(j):
+        def maxima(j, tiles=BOTH):
             row_max = work.tile([P, 2 * TILES], F32, name="row_max")
-            for i in BOTH:
+            for i in tiles:
                 for s, (a, b) in enumerate(SEGMENTS):
                     nc.vector.tensor_reduce(
                         out=row_max[:, 2 * i + s : 2 * i + s + 1], in_=live["z", j, i][:, :, a:b], axis=AX.XY, op=ALU.max
                     )
-            live["max", j] = row_max
+                live["max", j, i] = row_max
 
-        def biases(j):
+        def biases(j, tiles=BOTH):
+            cols = slice(2 * tiles[0], 2 * tiles[-1] + 2)
             bias = work.tile([P, 2 * TILES], F32, name="bias")
-            nc.scalar.activation(out=bias[:], in_=live["max", j][:], func=ACTF.Copy, scale=-ROOT)
-            live["bias", j] = bias
+            nc.scalar.activation(out=bias[:, cols], in_=live["max", j, tiles[0]][:, cols], func=ACTF.Copy, scale=-ROOT)
+            for i in tiles:
+                live["bias", j, i] = bias
 
         def exps(j):
             sums = work.tile([P, 2 * TILES], F32, name="row_sum")
             for i in BOTH:
-                ex = work.tile([P, 2, N // 2], F32, align_bytes=64, name="ex%d" % i)
+                if i == 0:
+                    ex = work.tile([P, 2, N // 2], F32, align_bytes=64, name="ex")
+                else:
+                    ex = ring[j % 4][:].rearrange("p (u x) -> p u x", u=2)
                 for s, (a, b) in enumerate(SEGMENTS):
                     col = slice(2 * i + s, 2 * i + s + 1)
                     nc.scalar.activation(
                         out=ex[:, :, a:b], in_=live["z", j, i][:, :, a:b], func=ACTF.Exp,
-                        bias=live["bias", j][:, col], scale=ROOT, accum_out=sums[:, col],
+                        bias=live["bias", j, i][:, col], scale=ROOT, accum_out=sums[:, col],
                     )
                 live["ex", j, i] = ex
             live["sums", j] = sums
@@ -294,7 +337,7 @@ def tile_llamaadaptergatedpromptattention_t_kernel(tc, q_bytes, q_scale, k, v, g
             live["b_turned", j, tiles] = turn(lambda i, u: live["b_words", j, i][:, P * u : P * (u + 1)], bank, tiles)
 
         def copy_b(j, tiles=BOTH):
-            copy_turned(b_stage(j)[:, tiles[0] * N : (tiles[-1] + 1) * N], live["b_turned", j, tiles])
+            copy_turned(b_stage(j)[:, tiles[0] * N : (tiles[-1] + 1) * N], live["b_turned", j, tiles][:])
 
         def quant_b(j, tiles=BOTH):
             cols = slice(tiles[0] * P, (tiles[-1] + 1) * P)
@@ -323,78 +366,92 @@ def tile_llamaadaptergatedpromptattention_t_kernel(tc, q_bytes, q_scale, k, v, g
                 )
             live["o", j, tiles] = o
 
-        def result(j, tiles):
-            if ("y", j, tiles) not in live:
-                live["y", j, tiles] = work.tile([P, len(tiles) * DV], F32, align_bytes=64, name="y", bufs=5)
-            return live["y", j, tiles]
-
-        def copy_o_share(j):
-            if j < SHARED_OUT_PAIRS:
-                cols = slice(OUT_COLUMNS_SCALAR, TILES * DV)
-                nc.vector.tensor_copy(out=result(j, BOTH)[:, cols], in_=live["o", j, BOTH][:, cols])
-
         def copy_o(j, tiles=BOTH, copy=nc.scalar.copy):
-            cols = slice(0, OUT_COLUMNS_SCALAR if j < SHARED_OUT_PAIRS else len(tiles) * DV)
-            y = result(j, tiles)
-            copy(out=y[:, cols], in_=live["o", j, tiles][:, cols])
+            y = work.tile([P, len(tiles) * DV], F32, align_bytes=64, name="y", bufs=5)
+            copy(out=y[:], in_=live["o", j, tiles][:])
             nc.sync.dma_start(
                 out=out_view[j][:, tiles[0] : tiles[-1] + 1, :], in_=y[:].rearrange("p (i d) -> p i d", d=DV)
             )
 
         spread_scales()
-        for half, bank in ((0, "turn_b"), (1, "o")):
-            turn_keys(half, bank)
-            copy_keys(half, nc.scalar.copy)
-        scale_vector(0, 0, E // 2)
-        scale_vector(0, E // 2, E)
-        scale_vector(0, E, ROW)
+        widen(0, 0, E, nc.vector.tensor_copy)
+        widen(0, E, ROW, nc.scalar.copy)
         turn_q(0)
-        scale_vector(1, 0, E)
-        scale_vector(1, E, ROW)
+        sort_keys(0)
+        turn_keys(0, "turn_b")
+        sort_keys(1)
+        turn_keys(1, "o")
+        copy_scales()
+        widen(1, 0, ROW, nc.scalar.copy)
         turn_q(1, "gain")
-        copy_q(0)
+        widen(2, 0, ROW, nc.scalar.copy)
+        scale_turned(0)
+        copy_keys(0, nc.scalar.copy)
+        copy_keys(1, nc.scalar.copy)
         quant_keys(0)
-        quant_keys(1)
         quant_q(0)
-        copy_q(1)
-        repeat_scales()
-        widen(3)
+        quant_keys(1)
+        scale_gpsimd(2)
+        widen(3, 0, ROW, nc.scalar.copy)
         scores(0)
-        scale_vector(2, 0, E)
-        scale_vector(2, E, ROW)
-        turn_q(2, "turn_b")
-        quant_q(1)
-        scale_gpsimd(3)
+        turn_q(3, "turn_b")
+        scale_turned(1)
+        widen(4, 0, ROW, nc.scalar.copy)
         make_gains()
-        widen(4)
-        group_values(0)
-        maxima(0)
-        biases(0)
-        copy_q(2)
+        widen(5, 0, ROW, nc.scalar.copy)
+        maxima(0, (0,))
+        biases(0, (0,))
+        widen(6, 0, ROW, nc.scalar.copy)
+        maxima(0, (1,))
+        biases(0, (1,))
+        quant_q(1)
+        scale_gpsimd(4)
+        turn_q(2)
         scores(1)
+        spread_gains(0)
         turn_keys(2, "o")
-        turn_keys(3, "turn_b")
-        scale_vector(3, 0, E)
-        scale_vector(3, E, VECTOR_COLUMNS_FIRST)
+        exps(0)
+        scale_turned(3)
+        copy_q(2)
+        maxima(1)
+        recips(0)
+        group_values(0)
+        biases(1)
+        copy_keys(2, nc.scalar.copy)
+        turn_q(4)
+        quant_q(2)
+        quant_q(3)
+        scale_gpsimd(5)
+        scores(2)
+        exps(1)
+        scores(3)
+        turn_keys(3, "o")
+        scale_turned(4)
+        weights(0, (0,))
+        copy_q(4)
+        group_values(1)
+        maxima(2)
+        weights(0, (1,))
+        biases(2)
+        copy_keys(3, nc.scalar.copy)
+        turn_b(0)
+        recips(1)
 
         step = (
-            (quant_b, -LAG), (quant_q, 2), (scale_gpsimd, LEAD), (turn_q, 3), (outputs, -LAG), (maxima, 1),
-            (exps, 0), (scores, 2), (weights, -1), (copy_q, 3), (biases, 1), (copy_b, -2), (turn_b, -1),
-            (copy_o_share, -LAG), (recips, 0), (widen, LEAD + 1), (copy_o, -LAG), (scale_early, LEAD),
+            (quant, 0), (scale_gpsimd, LEAD), (widen_gpsimd, LEAD + 1), (turn_q, 3), (outputs, -LAG), (maxima, 1),
+            (exps, 0), (scores, 2), (scale_turned, 3), (weights, -1), (copy_b, -2), (copy_q, 3), (biases, 1), (turn_b, -1),
+            (recips, 0), (widen_scalar, LEAD + 1), (copy_o, -LAG),
         )
         behind = {
-            (weights, -1): lambda: [copy_keys(half, nc.vector.tensor_copy) for half in (2, 3)],
-            (turn_b, -1): lambda: spread_gains(0),
-            (copy_b, -2): lambda: group_values(1),
-            (copy_b, -1): lambda: group_values(2),
-            (copy_o, -2): lambda: group_values(3),
+            (copy_b, 2): lambda: group_values(2),
+            (copy_b, 4): lambda: group_values(3),
             (turn_b, PAIRS_PER_HEAD - 1): lambda: spread_gains(1),
         }
-        extra_quants = {1: (quant_keys, 2), 2: (quant_values, 0), 3: (quant_keys, 3), 4: (quant_values, 1)}
-        for s in range(TAIL):
+        extra_quants = {2: (quant_values, 0), 4: (quant_keys, 2), 6: (quant_keys, 3), 8: (quant_values, 1)}
+        for s in range(2, TAIL):
             if s in extra_quants:
-                quant, which = extra_quants[s]
-                quant(which)
+                quant_fn, which = extra_quants[s]
+                quant_fn(which)
             for stage_fn, ahead in step:
                 if 0 <= s + ahead < PAIRS:
                     stage_fn(s + ahead)
@@ -403,8 +460,7 @@ def tile_llamaadaptergatedpromptattention_t_kernel(tc, q_bytes, q_scale, k, v, g
 
         third, next_to_last, last = TAIL, TAIL + 1, TAIL + 2
         first, second = (0,), (1,)
-        quant_b(third - 3)
-        quant_q(last)
+        quant(third)
         exps(third)
         scores(last)
         outputs(third - 3)

@@ -35,8 +35,8 @@ LAG = 3
 TAIL = PAIRS - 3
 WIDEN_LONG = 320
 WIDEN_SHORT = 832
-HEAD_TILES = (0, 0, 2, 0)
-Q_LOADS = ((0, 1), (1, 2), (2, 3), (3, 4), (4, 6), (6, 8), (8, 16), (16, 24), (24, 32))
+HEAD_TILES = (0, 0, 2, 0, 1, 2, 2)
+Q_LOADS = ((0, 1), (1, 2), (2, 3), (3, 4), (4, 6), (6, 8), (8, 10), (10, 16), (16, 24), (24, 32))
 
 
 def tile_llamaadaptergatedpromptattention_t_kernel(tc, q_bytes, q_scale, k, v, gate, c, out):
@@ -78,7 +78,7 @@ def tile_llamaadaptergatedpromptattention_t_kernel(tc, q_bytes, q_scale, k, v, g
         load_q(*Q_LOADS[0])
         load_keys(0)
         load_keys(1)
-        for a, b in Q_LOADS[1:5]:
+        for a, b in Q_LOADS[1:6]:
             load_q(a, b)
         nc.sync.dma_start(out=gates[:], in_=gate.partition_broadcast(PROMPT_ROWS))
         nc.sync.dma_start(out=c_cols[:], in_=c.rearrange("h (p t) -> p h t", t=PACK))
@@ -86,7 +86,7 @@ def tile_llamaadaptergatedpromptattention_t_kernel(tc, q_bytes, q_scale, k, v, g
         load_keys(3)
         load_values(0)
         load_values(1)
-        for a, b in Q_LOADS[5:]:
+        for a, b in Q_LOADS[6:]:
             load_q(a, b)
 
         scale_rows = keep.tile([P, E], F32, align_bytes=64)
@@ -116,7 +116,7 @@ def tile_llamaadaptergatedpromptattention_t_kernel(tc, q_bytes, q_scale, k, v, g
             return ring[(j - LEAD - 2) % 4][:].bitcast(BF16)
 
         def gpsimd_tiles(j):
-            return HEAD_TILES[j] if j < LEAD else 1 + j % 2
+            return HEAD_TILES[j] if j < len(HEAD_TILES) else 1 + j % 2
 
         def spread_scales():
             ps = psum.tile([P, PACK, P], F32, name="z", bufs=4)
@@ -194,7 +194,7 @@ def tile_llamaadaptergatedpromptattention_t_kernel(tc, q_bytes, q_scale, k, v, g
 
         def widen(j, a, b, copy):
             if ("wide", j) not in live:
-                live["wide", j] = work.tile([P, ROW], BF16, align_bytes=64, name="q_wide", bufs=6)
+                live["wide", j] = work.tile([P, ROW], BF16, align_bytes=64, name="q_wide", bufs=7)
             if a < b:
                 copy(out=live["wide", j][:, a:b], in_=q_raw[j][:, a:b].bitcast(FP8))
 
@@ -202,10 +202,12 @@ def tile_llamaadaptergatedpromptattention_t_kernel(tc, q_bytes, q_scale, k, v, g
             return WIDEN_SHORT if j % 2 else WIDEN_LONG
 
         def widen_gpsimd(j):
-            widen(j, 0, gpsimd_columns(j), nc.gpsimd.tensor_copy)
+            if j > len(HEAD_TILES) + 1:
+                widen(j, 0, gpsimd_columns(j), nc.gpsimd.tensor_copy)
 
         def widen_scalar(j):
-            widen(j, gpsimd_columns(j), ROW, nc.scalar.copy)
+            if j > len(HEAD_TILES) + 1:
+                widen(j, gpsimd_columns(j), ROW, nc.scalar.copy)
 
         def scale_gpsimd(j):
             n = gpsimd_tiles(j)
@@ -373,6 +375,12 @@ def tile_llamaadaptergatedpromptattention_t_kernel(tc, q_bytes, q_scale, k, v, g
                 out=out_view[j][:, tiles[0] : tiles[-1] + 1, :], in_=y[:].rearrange("p (i d) -> p i d", d=DV)
             )
 
+        def odd(fn):
+            return lambda j: fn(j) if j % 2 else None
+
+        def even(fn):
+            return lambda j: None if j % 2 else fn(j)
+
         spread_scales()
         widen(0, 0, E, nc.vector.tensor_copy)
         widen(0, E, ROW, nc.scalar.copy)
@@ -384,7 +392,7 @@ def tile_llamaadaptergatedpromptattention_t_kernel(tc, q_bytes, q_scale, k, v, g
         copy_scales()
         widen(1, 0, ROW, nc.scalar.copy)
         turn_q(1, "gain")
-        widen(2, 0, ROW, nc.scalar.copy)
+        widen(2, 0, ROW, nc.gpsimd.tensor_copy)
         scale_turned(0)
         copy_keys(0, nc.scalar.copy)
         copy_keys(1, nc.scalar.copy)
@@ -399,9 +407,10 @@ def tile_llamaadaptergatedpromptattention_t_kernel(tc, q_bytes, q_scale, k, v, g
         widen(4, 0, ROW, nc.scalar.copy)
         make_gains()
         widen(5, 0, ROW, nc.scalar.copy)
+        widen(6, 0, ROW, nc.scalar.copy)
         maxima(0, (0,))
         biases(0, (0,))
-        widen(6, 0, ROW, nc.scalar.copy)
+        widen(7, 0, ROW, nc.scalar.copy)
         maxima(0, (1,))
         biases(0, (1,))
         quant_q(1)
@@ -423,26 +432,28 @@ def tile_llamaadaptergatedpromptattention_t_kernel(tc, q_bytes, q_scale, k, v, g
         quant_q(3)
         scale_gpsimd(5)
         scores(2)
+        turn_keys(3, "o")
         exps(1)
         scores(3)
-        turn_keys(3, "o")
         scale_turned(4)
         weights(0, (0,))
         copy_q(4)
         group_values(1)
         maxima(2)
         weights(0, (1,))
-        biases(2)
         copy_keys(3, nc.scalar.copy)
+        biases(2)
+        widen(8, 0, E, nc.scalar.copy)
         turn_b(0)
         recips(1)
 
         step = (
             (quant, 0), (scale_gpsimd, LEAD), (widen_gpsimd, LEAD + 1), (turn_q, 3), (outputs, -LAG), (maxima, 1),
-            (exps, 0), (scores, 2), (scale_turned, 3), (weights, -1), (copy_b, -2), (copy_q, 3), (biases, 1), (turn_b, -1),
-            (recips, 0), (widen_scalar, LEAD + 1), (copy_o, -LAG),
+            (exps, 0), (scores, 2), (scale_turned, 3), (weights, -1), (copy_b, -2), (odd(copy_q), 3), (even(widen_scalar), LEAD + 1), (biases, 1), (even(copy_q), 3), (turn_b, -1),
+            (recips, 0), (odd(widen_scalar), LEAD + 1), (copy_o, -LAG),
         )
         behind = {
+            (biases, 3): lambda: widen(8, E, ROW, nc.scalar.copy),
             (copy_b, 2): lambda: group_values(2),
             (copy_b, 4): lambda: group_values(3),
             (turn_b, PAIRS_PER_HEAD - 1): lambda: spread_gains(1),

@@ -35,6 +35,9 @@ LAG = 3
 TAIL = PAIRS - 3
 WIDEN_LONG = 320
 WIDEN_SHORT = 832
+PERIOD = 2
+SHARED = (0,)
+OUT_SHARE = 0
 HEAD_TILES = (0, 0, 2, 0, 1, 2, 2)
 Q_LOADS = ((0, 1), (1, 2), (2, 3), (3, 4), (4, 6), (6, 8), (8, 10), (10, 16), (16, 24), (24, 32))
 
@@ -90,6 +93,7 @@ def tile_llamaadaptergatedpromptattention_t_kernel(tc, q_bytes, q_scale, k, v, g
             load_q(a, b)
 
         scale_rows = keep.tile([P, E], F32, align_bytes=64)
+        scale_words = keep.tile([P, P, PACK], F32, align_bytes=64)
         gain_cols = keep.tile([P, H, PACK], F32)
         tanh_gates = keep.tile([PROMPT_ROWS, H], F32)
         k_codes = keep.tile([P, H, N], U32, align_bytes=64)
@@ -116,13 +120,18 @@ def tile_llamaadaptergatedpromptattention_t_kernel(tc, q_bytes, q_scale, k, v, g
             return ring[(j - LEAD - 2) % 4][:].bitcast(BF16)
 
         def gpsimd_tiles(j):
-            return HEAD_TILES[j] if j < len(HEAD_TILES) else 1 + j % 2
+            if j < len(HEAD_TILES):
+                return HEAD_TILES[j]
+            return 1 if j % PERIOD in SHARED else TILES
 
         def spread_scales():
             ps = psum.tile([P, PACK, P], F32, name="z", bufs=4)
             for t in range(PACK):
                 nc.tensor.transpose(ps[:, t, :], scale_cols[:, t : t + 1].to_broadcast([P, P]), ident[:])
             live["scales"] = ps
+
+        def repeat_scales():
+            nc.vector.tensor_copy(out=scale_words[:], in_=scale_cols[:].unsqueeze(1).to_broadcast([P, P, PACK]))
 
         def copy_scales():
             nc.scalar.copy(
@@ -199,7 +208,9 @@ def tile_llamaadaptergatedpromptattention_t_kernel(tc, q_bytes, q_scale, k, v, g
                 copy(out=live["wide", j][:, a:b], in_=q_raw[j][:, a:b].bitcast(FP8))
 
         def gpsimd_columns(j):
-            return WIDEN_SHORT if j % 2 else WIDEN_LONG
+            if gpsimd_tiles(j - 1) < TILES:
+                return WIDEN_SHORT
+            return WIDEN_LONG if gpsimd_tiles(j - 2) < TILES else 0
 
         def widen_gpsimd(j):
             if j > len(HEAD_TILES) + 1:
@@ -230,11 +241,19 @@ def tile_llamaadaptergatedpromptattention_t_kernel(tc, q_bytes, q_scale, k, v, g
                 in_=ps.rearrange("p i u r -> p i r u"),
             )
 
+        def side_by_side(j, i):
+            return j >= len(HEAD_TILES) and i >= gpsimd_tiles(j)
+
         def turn_q(j, bank="turn_q"):
-            rows = [q_scaled(j) if i < gpsimd_tiles(j) else live["wide", j][:] for i in BOTH]
-            live["q_turned", j] = turn(
-                lambda i, u: rows[i].bitcast(F32)[:, WORDS * i + u : WORDS * (i + 1) : 2], bank, BOTH
-            )
+            ps = psum.tile([P, TILES, 2, P], F32, name=bank, bufs=1)
+            for i in BOTH:
+                words = (q_scaled(j) if i < gpsimd_tiles(j) else live["wide", j][:]).bitcast(F32)
+                planes = ps[:, i]
+                if side_by_side(j, i):
+                    planes = planes.rearrange("p u r -> p (u r)").rearrange("p (r u) -> p u r", u=2)
+                for u in range(2):
+                    nc.tensor.transpose(planes[:, u, :], words[:, WORDS * i + u : WORDS * (i + 1) : 2], ident[:])
+            live["q_turned", j] = ps
 
         def copy_q(j):
             n = gpsimd_tiles(j)
@@ -245,10 +264,11 @@ def tile_llamaadaptergatedpromptattention_t_kernel(tc, q_bytes, q_scale, k, v, g
             for i in tiles:
                 if i >= gpsimd_tiles(j):
                     turned = live["q_turned", j][:, i].rearrange("p u r -> p (u r)").bitcast(BF16)
+                    order = "p (r u e) -> p r u e" if side_by_side(j, i) else "p (u r e) -> p r u e"
                     nc.vector.tensor_tensor(
                         out=q_stage(j)[:, i * E : (i + 1) * E].rearrange("p (r u e) -> p r u e", u=2, e=2),
-                        in0=turned.rearrange("p (u r e) -> p r u e", u=2, e=2),
-                        in1=scale_cols[:].rearrange("p (u e) -> p u e", e=2).unsqueeze(1).to_broadcast([P, P, 2, 2]),
+                        in0=turned.rearrange(order, u=2, e=2),
+                        in1=scale_words[:].rearrange("p r (u e) -> p r u e", e=2),
                         op=ALU.mult,
                     )
 
@@ -368,20 +388,37 @@ def tile_llamaadaptergatedpromptattention_t_kernel(tc, q_bytes, q_scale, k, v, g
                 )
             live["o", j, tiles] = o
 
+        def vector_share(j):
+            s = j + LAG
+            tight = gpsimd_tiles(s + 3) == TILES and gpsimd_tiles(s + LEAD) == TILES
+            return OUT_SHARE if tight and len(HEAD_TILES) < s + 3 < PAIRS - 1 else 0
+
+        def result(j, tiles):
+            if ("y", j, tiles) not in live:
+                live["y", j, tiles] = work.tile([P, len(tiles) * DV], F32, align_bytes=64, name="y", bufs=5)
+            return live["y", j, tiles]
+
+        def copy_o_share(j):
+            if vector_share(j):
+                cols = slice(0, vector_share(j))
+                nc.vector.tensor_copy(out=result(j, BOTH)[:, cols], in_=live["o", j, BOTH][:, cols])
+
         def copy_o(j, tiles=BOTH, copy=nc.scalar.copy):
-            y = work.tile([P, len(tiles) * DV], F32, align_bytes=64, name="y", bufs=5)
-            copy(out=y[:], in_=live["o", j, tiles][:])
+            cols = slice(vector_share(j), len(tiles) * DV)
+            y = result(j, tiles)
+            copy(out=y[:, cols], in_=live["o", j, tiles][:, cols])
             nc.sync.dma_start(
                 out=out_view[j][:, tiles[0] : tiles[-1] + 1, :], in_=y[:].rearrange("p (i d) -> p i d", d=DV)
             )
 
-        def odd(fn):
-            return lambda j: fn(j) if j % 2 else None
+        def whole(fn, back):
+            return lambda j: fn(j) if gpsimd_tiles(j - back) == TILES else None
 
-        def even(fn):
-            return lambda j: None if j % 2 else fn(j)
+        def shared(fn, back):
+            return lambda j: fn(j) if gpsimd_tiles(j - back) < TILES else None
 
         spread_scales()
+        repeat_scales()
         widen(0, 0, E, nc.vector.tensor_copy)
         widen(0, E, ROW, nc.scalar.copy)
         turn_q(0)
@@ -449,8 +486,8 @@ def tile_llamaadaptergatedpromptattention_t_kernel(tc, q_bytes, q_scale, k, v, g
 
         step = (
             (quant, 0), (scale_gpsimd, LEAD), (widen_gpsimd, LEAD + 1), (turn_q, 3), (outputs, -LAG), (maxima, 1),
-            (exps, 0), (scores, 2), (scale_turned, 3), (weights, -1), (copy_b, -2), (odd(copy_q), 3), (even(widen_scalar), LEAD + 1), (biases, 1), (even(copy_q), 3), (turn_b, -1),
-            (recips, 0), (odd(widen_scalar), LEAD + 1), (copy_o, -LAG),
+            (exps, 0), (scores, 2), (scale_turned, 3), (weights, -1), (copy_b, -2), (whole(copy_q, 0), 3), (shared(widen_scalar, 2), LEAD + 1), (biases, 1), (shared(copy_q, 0), 3), (turn_b, -1),
+            (copy_o_share, -LAG), (recips, 0), (whole(widen_scalar, 2), LEAD + 1), (copy_o, -LAG),
         )
         behind = {
             (biases, 3): lambda: widen(8, E, ROW, nc.scalar.copy),

@@ -31,12 +31,16 @@ PROMPT_ROWS = L // PACK
 SEGMENTS = ((0, 2 * PROMPT_ROWS), (2 * PROMPT_ROWS, N // 2))
 
 LEAD = 4
-LAG = 3
+LAG = 4
 TAIL = PAIRS - 3
-WIDEN_LONG = 320
-WIDEN_SHORT = 832
-PERIOD = 2
-SHARED = (0,)
+WIDEN_LONG = 448
+WIDEN_SHORT = 896
+SIDE = False
+OUT_BANKS = {(30, 0): ("o", 1)}
+GPSIMD_WEIGHTS = (27, 28, 29)
+LAST_SHARED = 29
+PERIOD = 5
+SHARED = (3, 0)
 OUT_SHARE = 0
 HEAD_TILES = (0, 0, 2, 0, 1, 2, 2)
 Q_LOADS = ((0, 1), (1, 2), (2, 3), (3, 4), (4, 6), (6, 8), (8, 10), (10, 16), (16, 24), (24, 32))
@@ -92,6 +96,9 @@ def tile_llamaadaptergatedpromptattention_t_kernel(tc, q_bytes, q_scale, k, v, g
         for a, b in Q_LOADS[6:]:
             load_q(a, b)
 
+        c_rows = keep.tile([P, N], BF16, align_bytes=64)
+        nc.sync.dma_start(out=c_rows[:], in_=c[H - 1].partition_broadcast(P))
+
         scale_rows = keep.tile([P, E], F32, align_bytes=64)
         scale_words = keep.tile([P, P, PACK], F32, align_bytes=64)
         gain_cols = keep.tile([P, H, PACK], F32)
@@ -100,17 +107,17 @@ def tile_llamaadaptergatedpromptattention_t_kernel(tc, q_bytes, q_scale, k, v, g
         k_scales = keep.tile([P, H, N], U8, align_bytes=64)
         v_codes = keep.tile([P, H, DV], U32, align_bytes=64)
         v_scales = keep.tile([P, H, DV], U8, align_bytes=64)
-        stage = [keep.tile([P, 2 * ROW], BF16, align_bytes=64, name="stage%d" % n) for n in range(2)]
+        stage = [keep.tile([P, 2 * ROW], BF16, align_bytes=64, name="stage%d" % n) for n in range(3)]
         ring = [keep.tile([P, N], F32, align_bytes=64, name="ring%d" % n) for n in range(4)]
         live = {}
 
         early = [keep.tile([P, ROW], BF16, align_bytes=64, name="early%d" % n) for n in range(LEAD)]
 
         def q_stage(j):
-            return early[j][:] if j < LEAD else stage[j % 2][:, ROW : 2 * ROW]
+            return early[j][:] if j < LEAD else stage[(j - 2) % 3][:, ROW : 2 * ROW]
 
         def b_stage(j):
-            return stage[(j + LAG) % 2][:, 0:ROW]
+            return stage[(j + LAG) % 3][:, 0:ROW]
 
         def q_scaled(j):
             if j == 2:
@@ -122,7 +129,7 @@ def tile_llamaadaptergatedpromptattention_t_kernel(tc, q_bytes, q_scale, k, v, g
         def gpsimd_tiles(j):
             if j < len(HEAD_TILES):
                 return HEAD_TILES[j]
-            return 1 if j % PERIOD in SHARED else TILES
+            return 1 if j % PERIOD in SHARED and j < LAST_SHARED else TILES
 
         def spread_scales():
             ps = psum.tile([P, PACK, P], F32, name="z", bufs=4)
@@ -242,7 +249,7 @@ def tile_llamaadaptergatedpromptattention_t_kernel(tc, q_bytes, q_scale, k, v, g
             )
 
         def side_by_side(j, i):
-            return j >= len(HEAD_TILES) and i >= gpsimd_tiles(j)
+            return SIDE and j >= len(HEAD_TILES) and i >= gpsimd_tiles(j)
 
         def turn_q(j, bank="turn_q"):
             ps = psum.tile([P, TILES, 2, P], F32, name=bank, bufs=1)
@@ -284,9 +291,10 @@ def tile_llamaadaptergatedpromptattention_t_kernel(tc, q_bytes, q_scale, k, v, g
             codes = work.tile([P, 2 * PAIR], U32, align_bytes=64, name="codes")
             scales = work.tile([P, 2 * PAIR], U8, align_bytes=64, name="scales")
             nc.vector.quantize_mx(
-                out=codes[:, a:b].bitcast(FP8X4), scales=scales[:, a:b], in_=stage[s % 2][:, PACK * a : PACK * b]
+                out=codes[:, a:b].bitcast(FP8X4), scales=scales[:, a:b], in_=stage[s % 3][:, PACK * a : PACK * b]
             )
-            live["b_codes", s - LAG] = (codes[:, 0:PAIR], scales[:, 0:PAIR])
+            for i in BOTH:
+                live["b_codes", s - LAG, i] = (codes[:, 0:PAIR], scales[:, 0:PAIR])
             live["q_codes", s + 2] = (codes[:, PAIR:], scales[:, PAIR:])
 
         def scores(j):
@@ -337,22 +345,43 @@ def tile_llamaadaptergatedpromptattention_t_kernel(tc, q_bytes, q_scale, k, v, g
                 live["ex", j, i] = ex
             live["sums", j] = sums
 
-        def recips(j):
+        def recips(j, tiles=BOTH):
+            cols = slice(2 * tiles[0], 2 * tiles[-1] + 2)
             recip = work.tile([P, 2 * TILES], F32, name="recip")
-            nc.vector.reciprocal(out=recip[:], in_=live["sums", j][:])
-            live["recip", j] = recip
+            nc.vector.reciprocal(out=recip[:, cols], in_=live["sums", j][:, cols])
+            for i in tiles:
+                live["recip", j, i] = recip
+
+        def b_tile(j, i):
+            if ("b_rows", j, i) not in live:
+                live["b_rows", j, i] = work.tile([P, 2, N // 2], BF16, align_bytes=64, name="b_rows%d" % i)
+                live["b_words", j, i] = live["b_rows", j, i][:].rearrange("p u x -> p (u x)").bitcast(F32)
+            return live["b_rows", j, i]
 
         def weights(j, tiles=BOTH):
             h = j // PAIRS_PER_HEAD
             for i in tiles:
-                b_rows = work.tile([P, 2, N // 2], BF16, align_bytes=64, name="b_rows%d" % i)
                 for s, (a, b) in enumerate(SEGMENTS):
-                    nc.vector.scalar_tensor_tensor(
-                        out=b_rows[:, :, a:b], in0=live["ex", j, i][:, :, a:b],
-                        scalar=live["recip", j][:, 2 * i + s : 2 * i + s + 1],
-                        in1=live["gain", h][:, :, a:b], op0=ALU.mult, op1=ALU.mult,
-                    )
-                live["b_words", j, i] = b_rows[:].rearrange("p u x -> p (u x)").bitcast(F32)
+                    if (i, s) != (0, 1) or j not in GPSIMD_WEIGHTS:
+                        nc.vector.scalar_tensor_tensor(
+                            out=b_tile(j, i)[:, :, a:b], in0=live["ex", j, i][:, :, a:b],
+                            scalar=live["recip", j, i][:, 2 * i + s : 2 * i + s + 1],
+                            in1=live["gain", h][:, :, a:b], op0=ALU.mult, op1=ALU.mult,
+                        )
+
+        def weights_gpsimd(j):
+            if j in GPSIMD_WEIGHTS:
+                a, b = SEGMENTS[1]
+                gained = ring[(j - 1) % 4][:].rearrange("p (u x) -> p u x", u=2)[:, :, a:b]
+                nc.gpsimd.tensor_tensor(
+                    out=gained.rearrange("m u (p e) -> m u p e", e=2),
+                    in0=live["ex", j, 0][:, :, a:b].rearrange("m u (p e) -> m u p e", e=2),
+                    in1=c_rows[:].rearrange("m (p u e) -> m u p e", u=2, e=2)[:, :, PROMPT_ROWS:, :], op=ALU.mult,
+                )
+                nc.gpsimd.tensor_scalar(
+                    out=b_tile(j, 0)[:, :, a:b], in0=gained, scalar1=live["recip", j, 0][:, 1:2], scalar2=0.0,
+                    op0=ALU.mult, op1=ALU.add,
+                )
 
         def turn_b(j, tiles=BOTH):
             bank = "turn_q" if j >= TAIL - 1 and (j + tiles[0]) % 2 == 0 else "turn_b"
@@ -363,18 +392,19 @@ def tile_llamaadaptergatedpromptattention_t_kernel(tc, q_bytes, q_scale, k, v, g
 
         def quant_b(j, tiles=BOTH):
             cols = slice(tiles[0] * P, (tiles[-1] + 1) * P)
-            codes = work.tile([P, PAIR], U32, align_bytes=64, name="b_codes")
-            scales = work.tile([P, PAIR], U8, align_bytes=64, name="b_scales")
+            codes = work.tile([P, PAIR], U32, align_bytes=64, name="b_codes", bufs=4)
+            scales = work.tile([P, PAIR], U8, align_bytes=64, name="b_scales", bufs=4)
             nc.vector.quantize_mx(
                 out=codes[:, cols].bitcast(FP8X4), scales=scales[:, cols],
                 in_=b_stage(j)[:, tiles[0] * N : (tiles[-1] + 1) * N],
             )
-            live["b_codes", j] = (codes, scales)
+            for i in tiles:
+                live["b_codes", j, i] = (codes, scales)
 
         def outputs(j, tiles=BOTH):
             h = j // PAIRS_PER_HEAD
-            codes, scales = live["b_codes", j]
-            bank, bufs = ("z", 4) if j >= TAIL - 1 else ("o", 1)
+            codes, scales = live["b_codes", j, tiles[0]]
+            bank, bufs = OUT_BANKS.get((j, tiles[0]), ("z", 4)) if j >= TAIL - 3 else ("o", 1)
             o = psum.tile([P, len(tiles) * DV], F32, name=bank, bufs=bufs)
             for n, i in enumerate(tiles):
                 nc.tensor.matmul_mx(
@@ -395,7 +425,7 @@ def tile_llamaadaptergatedpromptattention_t_kernel(tc, q_bytes, q_scale, k, v, g
 
         def result(j, tiles):
             if ("y", j, tiles) not in live:
-                live["y", j, tiles] = work.tile([P, len(tiles) * DV], F32, align_bytes=64, name="y", bufs=5)
+                live["y", j, tiles] = work.tile([P, len(tiles) * DV], F32, align_bytes=64, name="y", bufs=7)
             return live["y", j, tiles]
 
         def copy_o_share(j):
@@ -410,6 +440,22 @@ def tile_llamaadaptergatedpromptattention_t_kernel(tc, q_bytes, q_scale, k, v, g
             nc.sync.dma_start(
                 out=out_view[j][:, tiles[0] : tiles[-1] + 1, :], in_=y[:].rearrange("p (i d) -> p i d", d=DV)
             )
+
+        def loop_copy_o(j):
+            if j + LAG + 1 < TAIL:
+                copy_o(j)
+
+        def vector_copy_o(j):
+            if j + LAG + 1 == TAIL:
+                copy_o(j, BOTH, nc.vector.tensor_copy)
+
+        def early_bias(j):
+            if j == TAIL:
+                biases(j)
+
+        def late_bias(j):
+            if j != TAIL:
+                biases(j)
 
         def whole(fn, back):
             return lambda j: fn(j) if gpsimd_tiles(j - back) == TILES else None
@@ -481,21 +527,21 @@ def tile_llamaadaptergatedpromptattention_t_kernel(tc, q_bytes, q_scale, k, v, g
         copy_keys(3, nc.scalar.copy)
         biases(2)
         widen(8, 0, E, nc.scalar.copy)
-        turn_b(0)
         recips(1)
 
         step = (
-            (quant, 0), (scale_gpsimd, LEAD), (widen_gpsimd, LEAD + 1), (turn_q, 3), (outputs, -LAG), (maxima, 1),
-            (exps, 0), (scores, 2), (scale_turned, 3), (weights, -1), (copy_b, -2), (whole(copy_q, 0), 3), (shared(widen_scalar, 2), LEAD + 1), (biases, 1), (shared(copy_q, 0), 3), (turn_b, -1),
-            (copy_o_share, -LAG), (recips, 0), (whole(widen_scalar, 2), LEAD + 1), (copy_o, -LAG),
+            (quant, 0), (scale_gpsimd, LEAD), (widen_gpsimd, LEAD + 1), (weights_gpsimd, -1), (turn_q, 3), (turn_b, -2), (outputs, -LAG), (maxima, 1),
+            (exps, 0), (scores, 2), (scale_turned, 3), (vector_copy_o, -LAG), (weights, -1), (whole(copy_q, 0), 3), (early_bias, 1), (copy_b, -2),
+            (shared(widen_scalar, 2), LEAD + 1), (late_bias, 1), (shared(copy_q, 0), 3),
+            (recips, 0), (whole(widen_scalar, 2), LEAD + 1), (loop_copy_o, -LAG),
         )
         behind = {
-            (biases, 3): lambda: widen(8, E, ROW, nc.scalar.copy),
+            (late_bias, 3): lambda: widen(8, E, ROW, nc.scalar.copy),
             (copy_b, 2): lambda: group_values(2),
             (copy_b, 4): lambda: group_values(3),
             (turn_b, PAIRS_PER_HEAD - 1): lambda: spread_gains(1),
         }
-        extra_quants = {2: (quant_values, 0), 4: (quant_keys, 2), 6: (quant_keys, 3), 8: (quant_values, 1)}
+        extra_quants = {3: (quant_values, 0), 4: (quant_keys, 2), 6: (quant_keys, 3), 8: (quant_values, 1)}
         for s in range(2, TAIL):
             if s in extra_quants:
                 quant_fn, which = extra_quants[s]
@@ -509,21 +555,28 @@ def tile_llamaadaptergatedpromptattention_t_kernel(tc, q_bytes, q_scale, k, v, g
         third, next_to_last, last = TAIL, TAIL + 1, TAIL + 2
         first, second = (0,), (1,)
         quant(third)
+        weights_gpsimd(third - 1)
+        turn_b(third - 2)
+        outputs(third - 4)
         exps(third)
         scores(last)
-        outputs(third - 3)
         maxima(next_to_last)
-        biases(next_to_last)
         copy_b(third - 2)
+        biases(next_to_last)
+        copy_o(third - 4)
         weights(third - 1)
         turn_b(third - 1)
 
         exps(next_to_last)
         recips(third)
-        maxima(last)
-        copy_o(third - 3)
-        biases(last)
+        quant_b(third - 3)
+        weights_gpsimd(third)
+        maxima(last, first)
+        biases(last, first)
         copy_b(third - 1)
+        maxima(last, second)
+        biases(last, second)
+        outputs(third - 3)
         weights(third)
         turn_b(third)
 
@@ -533,28 +586,29 @@ def tile_llamaadaptergatedpromptattention_t_kernel(tc, q_bytes, q_scale, k, v, g
         outputs(third - 2)
         weights(next_to_last)
         copy_b(third)
+        copy_o(third - 3)
         turn_b(next_to_last)
         recips(last)
         quant_b(third - 1)
-        outputs(third - 1)
-        copy_o(third - 2)
         quant_b(third)
-        outputs(third)
-
         weights(last, first)
-        turn_b(last, first)
+        outputs(third - 1)
+        outputs(third)
         copy_b(next_to_last)
-        copy_o(third - 1)
+        turn_b(last, first)
         weights(last, second)
         turn_b(last, second)
+        copy_o(third - 2)
         quant_b(next_to_last)
-        outputs(next_to_last)
+        copy_o(third - 1, BOTH, nc.vector.tensor_copy)
         copy_b(last, first)
-        copy_o(third, BOTH, nc.vector.tensor_copy)
         copy_b(last, second)
-        for tile in (first, second):
-            quant_b(last, tile)
-            outputs(last, tile)
-        copy_o(next_to_last)
-        copy_o(last, first, nc.vector.tensor_copy)
-        copy_o(last, second)
+        outputs(next_to_last)
+        quant_b(last, first)
+        quant_b(last, second)
+        outputs(last, first)
+        outputs(last, second)
+        copy_o(third)
+        copy_o(last, first)
+        copy_o(next_to_last, BOTH, nc.vector.tensor_copy)
+        copy_o(last, second, nc.vector.tensor_copy)

@@ -89,10 +89,10 @@ def tile_llamaadaptergatedpromptattention_t_kernel(tc, q_bytes, q_scale, k, v, g
             load_q(a, b)
         nc.sync.dma_start(out=gates[:], in_=gate.partition_broadcast(PROMPT_ROWS))
         nc.sync.dma_start(out=c_cols[:], in_=c.rearrange("h (p t) -> p h t", t=PACK))
-        load_keys(2)
-        load_keys(3)
         load_values(0)
         load_values(1)
+        load_keys(2)
+        load_keys(3)
         for a, b in Q_LOADS[6:]:
             load_q(a, b)
 
@@ -145,9 +145,11 @@ def tile_llamaadaptergatedpromptattention_t_kernel(tc, q_bytes, q_scale, k, v, g
                 out=scale_rows[:].rearrange("m (p t) -> m p t", t=PACK), in_=live["scales"][:].rearrange("m t p -> m p t")
             )
 
-        def make_gains():
+        def start_gains():
             nc.scalar.activation(out=tanh_gates[:], in_=gates[:], func=ACTF.Tanh)
             nc.scalar.copy(out=gain_cols[:], in_=c_cols[:])
+
+        def gate_prompts():
             for h in range(H):
                 prompts = gain_cols[0:PROMPT_ROWS, h, :]
                 nc.scalar.activation(out=prompts, in_=prompts, func=ACTF.Copy, scale=tanh_gates[:, h : h + 1])
@@ -475,7 +477,8 @@ def tile_llamaadaptergatedpromptattention_t_kernel(tc, q_bytes, q_scale, k, v, g
         copy_scales()
         widen(1, 0, ROW, nc.scalar.copy)
         turn_q(1, "gain")
-        widen(2, 0, ROW, nc.gpsimd.tensor_copy)
+        widen(2, 0, E, nc.gpsimd.tensor_copy)
+        widen(2, E, ROW, nc.scalar.copy)
         scale_turned(0)
         copy_keys(0, nc.scalar.copy)
         copy_keys(1, nc.scalar.copy)
@@ -488,8 +491,9 @@ def tile_llamaadaptergatedpromptattention_t_kernel(tc, q_bytes, q_scale, k, v, g
         turn_q(3, "turn_b")
         scale_turned(1)
         widen(4, 0, ROW, nc.scalar.copy)
-        make_gains()
+        start_gains()
         widen(5, 0, ROW, nc.scalar.copy)
+        gate_prompts()
         widen(6, 0, ROW, nc.scalar.copy)
         maxima(0, (0,))
         biases(0, (0,))
@@ -501,7 +505,6 @@ def tile_llamaadaptergatedpromptattention_t_kernel(tc, q_bytes, q_scale, k, v, g
         turn_q(2)
         scores(1)
         spread_gains(0)
-        turn_keys(2, "o")
         exps(0)
         scale_turned(3)
         copy_q(2)
@@ -509,22 +512,20 @@ def tile_llamaadaptergatedpromptattention_t_kernel(tc, q_bytes, q_scale, k, v, g
         recips(0)
         group_values(0)
         biases(1)
-        copy_keys(2, nc.scalar.copy)
+        group_values(1)
         turn_q(4)
         quant_q(2)
         quant_q(3)
         scale_gpsimd(5)
         scores(2)
-        turn_keys(3, "o")
         exps(1)
         scores(3)
         scale_turned(4)
         weights(0, (0,))
         copy_q(4)
-        group_values(1)
+        group_values(2)
         maxima(2)
         weights(0, (1,))
-        copy_keys(3, nc.scalar.copy)
         biases(2)
         widen(8, 0, E, nc.scalar.copy)
         recips(1)
@@ -537,7 +538,10 @@ def tile_llamaadaptergatedpromptattention_t_kernel(tc, q_bytes, q_scale, k, v, g
         )
         behind = {
             (late_bias, 3): lambda: widen(8, E, ROW, nc.scalar.copy),
-            (copy_b, 2): lambda: group_values(2),
+            (turn_b, 0): lambda: turn_keys(2, "o"),
+            (copy_b, 0): lambda: copy_keys(2, nc.scalar.copy),
+            (turn_b, 1): lambda: turn_keys(3, "o"),
+            (late_bias, 4): lambda: copy_keys(3, nc.scalar.copy),
             (copy_b, 4): lambda: group_values(3),
             (turn_b, PAIRS_PER_HEAD - 1): lambda: spread_gains(1),
         }

@@ -35,14 +35,16 @@ LAG = 4
 TAIL = PAIRS - 3
 WIDEN_LONG = 448
 WIDEN_SHORT = 896
-SIDE = False
-OUT_BANKS = {(30, 0): ("o", 1)}
-GPSIMD_WEIGHTS = (27, 28, 29)
 LAST_SHARED = 29
+FIRST_SHARED = 8
 PERIOD = 5
 SHARED = (3, 0)
-OUT_SHARE = 0
-HEAD_TILES = (0, 0, 2, 0, 1, 2, 2)
+RING = 4
+PAIRED = 32
+RELEASED = 29
+WARM = False
+GPSIMD_WEIGHTS = ((27, 0), (28, 0), (29, 0))
+HEAD_TILES = (0, 0, 1, 0, 2, 2, 2)
 Q_LOADS = ((0, 1), (1, 2), (2, 3), (3, 4), (4, 6), (6, 8), (8, 10), (10, 16), (16, 24), (24, 32))
 
 
@@ -65,7 +67,7 @@ def tile_llamaadaptergatedpromptattention_t_kernel(tc, q_bytes, q_scale, k, v, g
             raw = keep.tile([P, (b - a) * ROW], U8, align_bytes=64, name="q_raw%d" % a)
             nc.sync.dma_start(out=raw[:].rearrange("p (j x) -> p j x", x=ROW), in_=q_view[:, a:b, :])
             for j in range(a, b):
-                q_raw[j] = raw[:, (j - a) * ROW : (j - a + 1) * ROW]
+                q_raw[j] = raw[:, (j - a) * ROW :]
 
         def load_keys(half):
             h, u = divmod(half, 2)
@@ -83,17 +85,20 @@ def tile_llamaadaptergatedpromptattention_t_kernel(tc, q_bytes, q_scale, k, v, g
         gates = keep.tile([PROMPT_ROWS, H], BF16)
         nc.sync.dma_start(out=scale_cols[:], in_=q_scale.rearrange("a b (p t) -> p (a b t)", t=PACK))
         load_q(*Q_LOADS[0])
+        load_q(*Q_LOADS[1])
         load_keys(0)
         load_keys(1)
-        for a, b in Q_LOADS[1:6]:
+        for a, b in Q_LOADS[2:6]:
             load_q(a, b)
         nc.sync.dma_start(out=gates[:], in_=gate.partition_broadcast(PROMPT_ROWS))
         nc.sync.dma_start(out=c_cols[:], in_=c.rearrange("h (p t) -> p h t", t=PACK))
+        load_q(*Q_LOADS[6])
         load_values(0)
         load_values(1)
         load_keys(2)
+        load_q(*Q_LOADS[7])
         load_keys(3)
-        for a, b in Q_LOADS[6:]:
+        for a, b in Q_LOADS[8:]:
             load_q(a, b)
 
         c_rows = keep.tile([P, N], BF16, align_bytes=64)
@@ -108,28 +113,44 @@ def tile_llamaadaptergatedpromptattention_t_kernel(tc, q_bytes, q_scale, k, v, g
         v_codes = keep.tile([P, H, DV], U32, align_bytes=64)
         v_scales = keep.tile([P, H, DV], U8, align_bytes=64)
         stage = [keep.tile([P, 2 * ROW], BF16, align_bytes=64, name="stage%d" % n) for n in range(3)]
-        ring = [keep.tile([P, N], F32, align_bytes=64, name="ring%d" % n) for n in range(4)]
+        ring = [keep.tile([P, N + 2 * TILES], F32, align_bytes=64, name="ring%d" % n) for n in range(RING)]
         live = {}
 
-        early = [keep.tile([P, ROW], BF16, align_bytes=64, name="early%d" % n) for n in range(LEAD)]
+        early = [keep.tile([P, 2 * ROW], BF16, align_bytes=64, name="early%d" % n) for n in range(LEAD // 2)]
 
         def q_stage(j):
-            return early[j][:] if j < LEAD else stage[(j - 2) % 3][:, ROW : 2 * ROW]
+            return early[j // 2][:, (j % 2) * ROW : (j % 2 + 1) * ROW] if j < LEAD else stage[(j - 2) % 3][:, ROW : 2 * ROW]
 
         def b_stage(j):
-            return stage[(j + LAG) % 3][:, 0:ROW]
+            if j < PAIRED:
+                return stage[(j + LAG) % 3][:, 0:ROW]
+            n, half = divmod(j - PAIRED, 2)
+            return stage[(PAIRED + LAG + n) % 3][:, half * ROW : (half + 1) * ROW]
 
-        def q_scaled(j):
+        def second_exps(j):
+            return ring[j % RING][:, 0:N]
+
+        def row_sums(j):
+            return ring[(j - 1) % RING][:, N:]
+
+        def released(j):
+            return ring[j % RING][:, 2 * TILES :]
+
+        def q_scaled(j, i):
             if j == 2:
-                return live["k_grouped", 0][:]
-            if j < LEAD + 2:
-                return q_stage(j - 3)
-            return ring[(j - LEAD - 2) % 4][:].bitcast(BF16)
+                rows = k_raw[1][:]
+            elif j == 4:
+                rows = live["k_grouped", 1][:]
+            elif j == 5:
+                rows = q_stage(3)
+            else:
+                rows = released(j - LEAD - 2).bitcast(BF16)
+            return rows
 
         def gpsimd_tiles(j):
             if j < len(HEAD_TILES):
                 return HEAD_TILES[j]
-            return 1 if j % PERIOD in SHARED and j < LAST_SHARED else TILES
+            return 1 if j % PERIOD in SHARED and FIRST_SHARED <= j < LAST_SHARED else TILES
 
         def spread_scales():
             ps = psum.tile([P, PACK, P], F32, name="z", bufs=4)
@@ -193,13 +214,13 @@ def tile_llamaadaptergatedpromptattention_t_kernel(tc, q_bytes, q_scale, k, v, g
                 out=k_codes[:, h, cols].bitcast(FP8X4), scales=k_scales[:, h, cols], in_=live["k_grouped", half][:]
             )
 
-        def group_values(half):
+        def group_values(half, copy=nc.scalar.copy):
             h, w = divmod(half, 2)
-            if w == 0:
+            if ("v_grouped", h) not in live:
                 live["v_grouped", h] = keep.tile([P, DV, PACK], BF16, align_bytes=64, name="v_grouped%d" % h)
             cols = slice(w * DV // 2, (w + 1) * DV // 2)
             rows = v_raw[h][:].rearrange("p (t d) -> p t d", t=PACK)
-            nc.scalar.copy(
+            copy(
                 out=live["v_grouped", h][:, cols, :].rearrange("p (g i) t -> p g t i", i=4),
                 in_=rows[:, :, cols].rearrange("p t (g i) -> p g t i", i=4),
             )
@@ -229,16 +250,20 @@ def tile_llamaadaptergatedpromptattention_t_kernel(tc, q_bytes, q_scale, k, v, g
             if j > len(HEAD_TILES) + 1:
                 widen(j, gpsimd_columns(j), ROW, nc.scalar.copy)
 
-        def scale_gpsimd(j):
-            n = gpsimd_tiles(j)
+        def scale_gpsimd(j, tiles=BOTH):
+            n = len(tiles)
+            cols = slice(tiles[0] * E, (tiles[-1] + 1) * E)
             nc.gpsimd.tensor_tensor(
-                out=q_scaled(j)[:, 0 : n * E].rearrange("p (i x) -> p i x", x=E),
-                in0=live["wide", j][:, 0 : n * E].rearrange("p (i x) -> p i x", x=E),
+                out=q_scaled(j, tiles[0])[:, cols].rearrange("p (i x) -> p i x", x=E),
+                in0=live["wide", j][:, cols].rearrange("p (i x) -> p i x", x=E),
                 in1=scale_rows[:].unsqueeze(1).to_broadcast([P, n, E]), op=ALU.mult,
             )
 
+        def product(j):
+            scale_gpsimd(j, BOTH[: gpsimd_tiles(j)])
+
         def turn(words, bank, tiles):
-            ps = psum.tile([P, len(tiles), 2, P], F32, name=bank, bufs=1)
+            ps = psum.tile([P, len(tiles), 2, P], F32, name=bank, bufs=4 if bank == "z" else 1)
             for n, i in enumerate(tiles):
                 for u in range(2):
                     nc.tensor.transpose(ps[:, n, u, :], words(i, u), ident[:])
@@ -250,42 +275,36 @@ def tile_llamaadaptergatedpromptattention_t_kernel(tc, q_bytes, q_scale, k, v, g
                 in_=ps.rearrange("p i u r -> p i r u"),
             )
 
-        def side_by_side(j, i):
-            return SIDE and j >= len(HEAD_TILES) and i >= gpsimd_tiles(j)
-
-        def turn_q(j, bank="turn_q"):
-            ps = psum.tile([P, TILES, 2, P], F32, name=bank, bufs=1)
-            for i in BOTH:
-                words = (q_scaled(j) if i < gpsimd_tiles(j) else live["wide", j][:]).bitcast(F32)
-                planes = ps[:, i]
-                if side_by_side(j, i):
-                    planes = planes.rearrange("p u r -> p (u r)").rearrange("p (r u) -> p u r", u=2)
+        def turn_q(j, bank="turn_q", tiles=BOTH):
+            ps = psum.tile([P, TILES, 2, P], F32, name=bank, bufs=4 if bank == "z" else 1)
+            for i in tiles:
+                words = (q_scaled(j, i) if i < gpsimd_tiles(j) else live["wide", j][:]).bitcast(F32)
                 for u in range(2):
-                    nc.tensor.transpose(planes[:, u, :], words[:, WORDS * i + u : WORDS * (i + 1) : 2], ident[:])
-            live["q_turned", j] = ps
+                    nc.tensor.transpose(ps[:, i, u, :], words[:, WORDS * i + u : WORDS * (i + 1) : 2], ident[:])
+                live["q_turned", j, i] = ps
 
         def copy_q(j):
             n = gpsimd_tiles(j)
             if n:
-                copy_turned(q_stage(j)[:, 0 : n * E], live["q_turned", j][:, 0:n])
+                copy_turned(q_stage(j)[:, 0 : n * E], live["q_turned", j, 0][:, 0:n])
 
         def scale_turned(j, tiles=BOTH):
             for i in tiles:
                 if i >= gpsimd_tiles(j):
-                    turned = live["q_turned", j][:, i].rearrange("p u r -> p (u r)").bitcast(BF16)
-                    order = "p (r u e) -> p r u e" if side_by_side(j, i) else "p (u r e) -> p r u e"
+                    turned = live["q_turned", j, i][:, i].rearrange("p u r -> p (u r)").bitcast(BF16)
                     nc.vector.tensor_tensor(
                         out=q_stage(j)[:, i * E : (i + 1) * E].rearrange("p (r u e) -> p r u e", u=2, e=2),
-                        in0=turned.rearrange(order, u=2, e=2),
+                        in0=turned.rearrange("p (u r e) -> p r u e", u=2, e=2),
                         in1=scale_words[:].rearrange("p r (u e) -> p r u e", e=2),
                         op=ALU.mult,
                     )
 
-        def quant_q(j):
-            codes = work.tile([P, PAIR], U32, align_bytes=64, name="q_codes", bufs=LEAD)
-            scales = work.tile([P, PAIR], U8, align_bytes=64, name="q_scales", bufs=LEAD)
-            nc.vector.quantize_mx(out=codes[:].bitcast(FP8X4), scales=scales[:], in_=q_stage(j))
-            live["q_codes", j] = (codes, scales)
+        def quant_early(n):
+            codes = work.tile([P, 2 * PAIR], U32, align_bytes=64, name="q_codes", bufs=2)
+            scales = work.tile([P, 2 * PAIR], U8, align_bytes=64, name="q_scales", bufs=2)
+            nc.vector.quantize_mx(out=codes[:].bitcast(FP8X4), scales=scales[:], in_=early[n][:])
+            for m in range(2):
+                live["q_codes", 2 * n + m] = (codes[:, m * PAIR : (m + 1) * PAIR], scales[:, m * PAIR : (m + 1) * PAIR])
 
         def quant(s):
             a = 0 if s >= LAG else PAIR
@@ -316,7 +335,10 @@ def tile_llamaadaptergatedpromptattention_t_kernel(tc, q_bytes, q_scale, k, v, g
                 live["z", j, i] = z
 
         def maxima(j, tiles=BOTH):
-            row_max = work.tile([P, 2 * TILES], F32, name="row_max")
+            if ("max", j, 0) in live:
+                row_max = live["max", j, 0]
+            else:
+                row_max = work.tile([P, 2 * TILES], F32, name="row_max", bufs=8)
             for i in tiles:
                 for s, (a, b) in enumerate(SEGMENTS):
                     nc.vector.tensor_reduce(
@@ -326,67 +348,81 @@ def tile_llamaadaptergatedpromptattention_t_kernel(tc, q_bytes, q_scale, k, v, g
 
         def biases(j, tiles=BOTH):
             cols = slice(2 * tiles[0], 2 * tiles[-1] + 2)
-            bias = work.tile([P, 2 * TILES], F32, name="bias")
+            bias = work.tile([P, 2 * TILES], F32, name="bias", bufs=8)
             nc.scalar.activation(out=bias[:, cols], in_=live["max", j, tiles[0]][:, cols], func=ACTF.Copy, scale=-ROOT)
             for i in tiles:
                 live["bias", j, i] = bias
 
-        def exps(j):
-            sums = work.tile([P, 2 * TILES], F32, name="row_sum")
-            for i in BOTH:
-                if i == 0:
-                    ex = work.tile([P, 2, N // 2], F32, align_bytes=64, name="ex")
+        def exps(j, tiles=BOTH, segments=BOTH):
+            sums = row_sums(j)
+            for i in tiles:
+                if ("ex", j, i) in live:
+                    ex = live["ex", j, i]
+                elif i == 0:
+                    ex = work.tile([P, 2, N // 2], F32, align_bytes=64, name="ex", bufs=4)
                 else:
-                    ex = ring[j % 4][:].rearrange("p (u x) -> p u x", u=2)
-                for s, (a, b) in enumerate(SEGMENTS):
+                    ex = second_exps(j).rearrange("p (u x) -> p u x", u=2)
+                for s in segments:
+                    a, b = SEGMENTS[s]
                     col = slice(2 * i + s, 2 * i + s + 1)
                     nc.scalar.activation(
                         out=ex[:, :, a:b], in_=live["z", j, i][:, :, a:b], func=ACTF.Exp,
                         bias=live["bias", j, i][:, col], scale=ROOT, accum_out=sums[:, col],
                     )
                 live["ex", j, i] = ex
-            live["sums", j] = sums
 
         def recips(j, tiles=BOTH):
             cols = slice(2 * tiles[0], 2 * tiles[-1] + 2)
-            recip = work.tile([P, 2 * TILES], F32, name="recip")
-            nc.vector.reciprocal(out=recip[:, cols], in_=live["sums", j][:, cols])
+            recip = work.tile([P, 2 * TILES], F32, name="recip", bufs=8)
+            nc.vector.reciprocal(out=recip[:, cols], in_=row_sums(j)[:, cols])
             for i in tiles:
                 live["recip", j, i] = recip
 
         def b_tile(j, i):
             if ("b_rows", j, i) not in live:
-                live["b_rows", j, i] = work.tile([P, 2, N // 2], BF16, align_bytes=64, name="b_rows%d" % i)
+                live["b_rows", j, i] = work.tile([P, 2, N // 2], BF16, align_bytes=64, name="b_rows%d" % i, bufs=4)
                 live["b_words", j, i] = live["b_rows", j, i][:].rearrange("p u x -> p (u x)").bitcast(F32)
             return live["b_rows", j, i]
 
-        def weights(j, tiles=BOTH):
+        def weights(j, tiles=BOTH, segments=BOTH):
             h = j // PAIRS_PER_HEAD
             for i in tiles:
                 for s, (a, b) in enumerate(SEGMENTS):
-                    if (i, s) != (0, 1) or j not in GPSIMD_WEIGHTS:
+                    if s in segments and (s == 0 or (j, i) not in GPSIMD_WEIGHTS):
                         nc.vector.scalar_tensor_tensor(
                             out=b_tile(j, i)[:, :, a:b], in0=live["ex", j, i][:, :, a:b],
                             scalar=live["recip", j, i][:, 2 * i + s : 2 * i + s + 1],
                             in1=live["gain", h][:, :, a:b], op0=ALU.mult, op1=ALU.mult,
                         )
 
-        def weights_gpsimd(j):
-            if j in GPSIMD_WEIGHTS:
-                a, b = SEGMENTS[1]
-                gained = ring[(j - 1) % 4][:].rearrange("p (u x) -> p u x", u=2)[:, :, a:b]
-                nc.gpsimd.tensor_tensor(
-                    out=gained.rearrange("m u (p e) -> m u p e", e=2),
-                    in0=live["ex", j, 0][:, :, a:b].rearrange("m u (p e) -> m u p e", e=2),
-                    in1=c_rows[:].rearrange("m (p u e) -> m u p e", u=2, e=2)[:, :, PROMPT_ROWS:, :], op=ALU.mult,
-                )
-                nc.gpsimd.tensor_scalar(
-                    out=b_tile(j, 0)[:, :, a:b], in0=gained, scalar1=live["recip", j, 0][:, 1:2], scalar2=0.0,
-                    op0=ALU.mult, op1=ALU.add,
-                )
+        def gain_gpsimd(j, i):
+            a, b = SEGMENTS[1]
+            if i == 0 and j <= RELEASED:
+                gained = released(j - 1)
+            else:
+                gained = keep.tile([P, N], F32, align_bytes=64, name="gained%d_%d" % (j, i))[:]
+            gained = gained.rearrange("p (u x) -> p u x", u=2)[:, :, a:b]
+            nc.gpsimd.tensor_tensor(
+                out=gained.rearrange("m u (p e) -> m u p e", e=2),
+                in0=live["ex", j, i][:, :, a:b].rearrange("m u (p e) -> m u p e", e=2),
+                in1=c_rows[:].rearrange("m (p u e) -> m u p e", u=2, e=2)[:, :, PROMPT_ROWS:, :], op=ALU.mult,
+            )
+            live["gained", j, i] = gained
 
-        def turn_b(j, tiles=BOTH):
-            bank = "turn_q" if j >= TAIL - 1 and (j + tiles[0]) % 2 == 0 else "turn_b"
+        def divide_gpsimd(j, i):
+            a, b = SEGMENTS[1]
+            nc.gpsimd.tensor_scalar(
+                out=b_tile(j, i)[:, :, a:b], in0=live["gained", j, i], scalar1=live["recip", j, i][:, 2 * i + 1 : 2 * i + 2],
+                scalar2=0.0, op0=ALU.mult, op1=ALU.add,
+            )
+
+        def weights_gpsimd(j):
+            for fn in (gain_gpsimd, divide_gpsimd):
+                for i in BOTH:
+                    if (j, i) in GPSIMD_WEIGHTS:
+                        fn(j, i)
+
+        def turn_b(j, tiles=BOTH, bank="turn_b"):
             live["b_turned", j, tiles] = turn(lambda i, u: live["b_words", j, i][:, P * u : P * (u + 1)], bank, tiles)
 
         def copy_b(j, tiles=BOTH):
@@ -403,11 +439,20 @@ def tile_llamaadaptergatedpromptattention_t_kernel(tc, q_bytes, q_scale, k, v, g
             for i in tiles:
                 live["b_codes", j, i] = (codes, scales)
 
-        def outputs(j, tiles=BOTH):
+        def quant_two(j):
+            codes = work.tile([P, 2 * PAIR], U32, align_bytes=64, name="codes")
+            scales = work.tile([P, 2 * PAIR], U8, align_bytes=64, name="scales")
+            nc.vector.quantize_mx(
+                out=codes[:].bitcast(FP8X4), scales=scales[:], in_=stage[(PAIRED + LAG + (j - PAIRED) // 2) % 3][:]
+            )
+            for n in range(2):
+                for i in BOTH:
+                    live["b_codes", j + n, i] = (codes[:, n * PAIR : (n + 1) * PAIR], scales[:, n * PAIR : (n + 1) * PAIR])
+
+        def outputs(j, tiles=BOTH, bank="o"):
             h = j // PAIRS_PER_HEAD
             codes, scales = live["b_codes", j, tiles[0]]
-            bank, bufs = OUT_BANKS.get((j, tiles[0]), ("z", 4)) if j >= TAIL - 3 else ("o", 1)
-            o = psum.tile([P, len(tiles) * DV], F32, name=bank, bufs=bufs)
+            o = psum.tile([P, len(tiles) * DV], F32, name=bank, bufs=4 if bank == "z" else 1)
             for n, i in enumerate(tiles):
                 nc.tensor.matmul_mx(
                     out=o[:, n * DV : (n + 1) * DV],
@@ -420,25 +465,14 @@ def tile_llamaadaptergatedpromptattention_t_kernel(tc, q_bytes, q_scale, k, v, g
                 )
             live["o", j, tiles] = o
 
-        def vector_share(j):
-            s = j + LAG
-            tight = gpsimd_tiles(s + 3) == TILES and gpsimd_tiles(s + LEAD) == TILES
-            return OUT_SHARE if tight and len(HEAD_TILES) < s + 3 < PAIRS - 1 else 0
-
         def result(j, tiles):
             if ("y", j, tiles) not in live:
                 live["y", j, tiles] = work.tile([P, len(tiles) * DV], F32, align_bytes=64, name="y", bufs=7)
             return live["y", j, tiles]
 
-        def copy_o_share(j):
-            if vector_share(j):
-                cols = slice(0, vector_share(j))
-                nc.vector.tensor_copy(out=result(j, BOTH)[:, cols], in_=live["o", j, BOTH][:, cols])
-
         def copy_o(j, tiles=BOTH, copy=nc.scalar.copy):
-            cols = slice(vector_share(j), len(tiles) * DV)
             y = result(j, tiles)
-            copy(out=y[:, cols], in_=live["o", j, tiles][:, cols])
+            copy(out=y[:], in_=live["o", j, tiles][:])
             nc.sync.dma_start(
                 out=out_view[j][:, tiles[0] : tiles[-1] + 1, :], in_=y[:].rearrange("p (i d) -> p i d", d=DV)
             )
@@ -450,6 +484,24 @@ def tile_llamaadaptergatedpromptattention_t_kernel(tc, q_bytes, q_scale, k, v, g
         def vector_copy_o(j):
             if j + LAG + 1 == TAIL:
                 copy_o(j, BOTH, nc.vector.tensor_copy)
+
+        def prompt_weights(j):
+            if j == TAIL - 2:
+                weights(j, BOTH, (0,))
+
+        def rest_weights(j):
+            weights(j, BOTH, (1,) if j == TAIL - 2 else BOTH)
+
+        def warm(j, i, bank="o", n=256):
+            if WARM:
+                ps = psum.tile([P, n], F32, name=bank, bufs=4 if bank == "z" else 1)
+                nc.tensor.matmul(out=ps[:], lhsT=ident[:], rhs=live["ex", j, i][:, 0, 0:n], start=True, stop=True)
+
+        def first_exps(j):
+            exps(j, (0,))
+
+        def second_exps_step(j):
+            exps(j, (1,))
 
         def early_bias(j):
             if j == TAIL:
@@ -465,83 +517,91 @@ def tile_llamaadaptergatedpromptattention_t_kernel(tc, q_bytes, q_scale, k, v, g
         def shared(fn, back):
             return lambda j: fn(j) if gpsimd_tiles(j - back) < TILES else None
 
+        S = nc.scalar.copy
+        A = (0,)
+        B = (1,)
         spread_scales()
         repeat_scales()
         widen(0, 0, E, nc.vector.tensor_copy)
-        widen(0, E, ROW, nc.scalar.copy)
-        turn_q(0)
+        widen(0, E, ROW, S)
+        turn_q(0, "z", A)
+        turn_q(0, "z", B)
+        widen(1, 0, ROW, S)
+        turn_q(1, "z", A)
+        copy_scales()
         sort_keys(0)
         turn_keys(0, "turn_b")
+        scale_turned(0, A)
         sort_keys(1)
+        turn_q(1, "gain", B)
         turn_keys(1, "o")
-        copy_scales()
-        widen(1, 0, ROW, nc.scalar.copy)
-        turn_q(1, "gain")
-        widen(2, 0, E, nc.gpsimd.tensor_copy)
-        widen(2, E, ROW, nc.scalar.copy)
-        scale_turned(0)
-        copy_keys(0, nc.scalar.copy)
-        copy_keys(1, nc.scalar.copy)
-        quant_keys(0)
-        quant_q(0)
-        quant_keys(1)
-        scale_gpsimd(2)
-        widen(3, 0, ROW, nc.scalar.copy)
-        scores(0)
-        turn_q(3, "turn_b")
+        widen(2, 0, E, S)
+        scale_gpsimd(2, A)
+        widen(3, 0, ROW, S)
+        scale_turned(0, B)
+        turn_q(3)
+        copy_keys(0, S)
+        widen(2, E, ROW, S)
         scale_turned(1)
-        widen(4, 0, ROW, nc.scalar.copy)
-        start_gains()
-        widen(5, 0, ROW, nc.scalar.copy)
-        gate_prompts()
-        widen(6, 0, ROW, nc.scalar.copy)
-        maxima(0, (0,))
-        biases(0, (0,))
-        widen(7, 0, ROW, nc.scalar.copy)
-        maxima(0, (1,))
-        biases(0, (1,))
-        quant_q(1)
+        copy_keys(1, S)
+        widen(4, 0, ROW, S)
+        turn_q(2, "turn_b")
+        quant_keys(0)
+        quant_early(0)
+        quant_keys(1)
         scale_gpsimd(4)
-        turn_q(2)
+        scores(0)
         scores(1)
-        spread_gains(0)
-        exps(0)
+        widen(5, 0, ROW, S)
+        start_gains()
+        widen(6, 0, ROW, S)
+        gate_prompts()
         scale_turned(3)
+        scale_turned(2)
+        spread_gains(0)
+        maxima(0, A)
+        widen(7, 0, ROW, S)
         copy_q(2)
-        maxima(1)
-        recips(0)
+        widen(8, 0, E, S)
+        biases(0, A)
+        widen(8, E, ROW, S)
+        maxima(0, B)
+        quant_early(1)
+        scale_gpsimd(5)
+        group_values(1, nc.gpsimd.tensor_copy)
+        turn_q(4)
+        exps(0, A, A)
+        biases(0, B)
+        exps(0, A, B)
+        maxima(1, A)
+        exps(0, B)
+        recips(0, A)
+        maxima(1, B)
+        scores(2)
+        turn_keys(3, "turn_b")
+        turn_keys(2, "o")
         group_values(0)
         biases(1)
-        group_values(1)
-        turn_q(4)
-        quant_q(2)
-        quant_q(3)
-        scale_gpsimd(5)
-        scores(2)
+        copy_q(4)
+        weights(0, A)
+        recips(0, B)
         exps(1)
         scores(3)
-        scale_turned(4)
-        weights(0, (0,))
-        copy_q(4)
-        group_values(2)
         maxima(2)
-        weights(0, (1,))
+        weights(0, B)
         biases(2)
-        widen(8, 0, E, nc.scalar.copy)
+        copy_keys(3, S)
         recips(1)
 
         step = (
-            (quant, 0), (scale_gpsimd, LEAD), (widen_gpsimd, LEAD + 1), (weights_gpsimd, -1), (turn_q, 3), (turn_b, -2), (outputs, -LAG), (maxima, 1),
-            (exps, 0), (scores, 2), (scale_turned, 3), (vector_copy_o, -LAG), (weights, -1), (whole(copy_q, 0), 3), (early_bias, 1), (copy_b, -2),
+            (quant, 0), (product, LEAD), (widen_gpsimd, LEAD + 1), (weights_gpsimd, -1), (turn_q, 3), (turn_b, -2), (outputs, -LAG), (maxima, 1),
+            (exps, 0), (scores, 2), (scale_turned, 3), (prompt_weights, -1), (vector_copy_o, -LAG), (rest_weights, -1), (whole(copy_q, 0), 3), (early_bias, 1), (copy_b, -2),
             (shared(widen_scalar, 2), LEAD + 1), (late_bias, 1), (shared(copy_q, 0), 3),
             (recips, 0), (whole(widen_scalar, 2), LEAD + 1), (loop_copy_o, -LAG),
         )
         behind = {
-            (late_bias, 3): lambda: widen(8, E, ROW, nc.scalar.copy),
-            (turn_b, 0): lambda: turn_keys(2, "o"),
-            (copy_b, 0): lambda: copy_keys(2, nc.scalar.copy),
-            (turn_b, 1): lambda: turn_keys(3, "o"),
-            (late_bias, 4): lambda: copy_keys(3, nc.scalar.copy),
+            (late_bias, 3): lambda: copy_keys(2, nc.scalar.copy),
+            (late_bias, 4): lambda: group_values(2),
             (copy_b, 4): lambda: group_values(3),
             (turn_b, PAIRS_PER_HEAD - 1): lambda: spread_gains(1),
         }
@@ -556,63 +616,61 @@ def tile_llamaadaptergatedpromptattention_t_kernel(tc, q_bytes, q_scale, k, v, g
                 if (stage_fn, s + ahead) in behind:
                     behind[stage_fn, s + ahead]()
 
-        third, next_to_last, last = TAIL, TAIL + 1, TAIL + 2
-        first, second = (0,), (1,)
-        quant(third)
-        weights_gpsimd(third - 1)
-        turn_b(third - 2)
-        outputs(third - 4)
-        exps(third)
-        scores(last)
-        maxima(next_to_last)
-        copy_b(third - 2)
-        biases(next_to_last)
-        copy_o(third - 4)
-        weights(third - 1)
-        turn_b(third - 1)
-
-        exps(next_to_last)
-        recips(third)
-        quant_b(third - 3)
-        weights_gpsimd(third)
-        maxima(last, first)
-        biases(last, first)
-        copy_b(third - 1)
-        maxima(last, second)
-        biases(last, second)
-        outputs(third - 3)
-        weights(third)
-        turn_b(third)
-
-        exps(last)
-        recips(next_to_last)
-        quant_b(third - 2)
-        outputs(third - 2)
-        weights(next_to_last)
-        copy_b(third)
-        copy_o(third - 3)
-        turn_b(next_to_last)
-        recips(last)
-        quant_b(third - 1)
-        quant_b(third)
-        weights(last, first)
-        outputs(third - 1)
-        outputs(third)
-        copy_b(next_to_last)
-        turn_b(last, first)
-        weights(last, second)
-        turn_b(last, second)
-        copy_o(third - 2)
-        quant_b(next_to_last)
-        copy_o(third - 1, BOTH, nc.vector.tensor_copy)
-        copy_b(last, first)
-        copy_b(last, second)
-        outputs(next_to_last)
-        quant_b(last, first)
-        quant_b(last, second)
-        outputs(last, first)
-        outputs(last, second)
-        copy_o(third)
-        copy_o(last, first)
-        copy_o(next_to_last, BOTH, nc.vector.tensor_copy)
-        copy_o(last, second, nc.vector.tensor_copy)
+        V = nc.vector.tensor_copy
+        TQ = "turn_q"
+        quant(29)
+        weights_gpsimd(28)
+        turn_b(27)
+        outputs(25)
+        exps(29)
+        scores(31)
+        maxima(30)
+        copy_b(27)
+        biases(30)
+        copy_o(25)
+        weights(28)
+        turn_b(28, BOTH, TQ)
+        exps(30)
+        recips(29)
+        quant_b(26)
+        weights_gpsimd(29)
+        maxima(31, A)
+        biases(31, A)
+        copy_b(28)
+        maxima(31, B)
+        biases(31, B)
+        outputs(26, BOTH, "z")
+        weights(29)
+        turn_b(29)
+        exps(31)
+        recips(30)
+        quant_b(27)
+        outputs(27, BOTH, "z")
+        weights(30)
+        copy_b(29)
+        copy_o(26)
+        turn_b(30, BOTH, TQ)
+        recips(31)
+        quant_b(28)
+        quant_b(29)
+        weights(31, A)
+        outputs(28, BOTH, "z")
+        outputs(29, BOTH, "z")
+        copy_b(30)
+        turn_b(31, A)
+        weights(31, B)
+        turn_b(31, B, TQ)
+        copy_o(27)
+        quant_b(30)
+        copy_o(28, BOTH, V)
+        copy_b(31, A)
+        copy_b(31, B)
+        outputs(30)
+        quant_b(31, A)
+        quant_b(31, B)
+        outputs(31, A, "z")
+        outputs(31, B, "z")
+        copy_o(29)
+        copy_o(31, A)
+        copy_o(30, BOTH, V)
+        copy_o(31, B, V)

@@ -43,6 +43,9 @@ RING = 4
 PAIRED = 32
 RELEASED = 29
 WARM = False
+NW = 128
+V24 = True
+SPLIT5 = False
 GPSIMD_WEIGHTS = ((27, 0), (28, 0), (29, 0))
 HEAD_TILES = (0, 0, 1, 0, 2, 2, 2)
 Q_LOADS = ((0, 1), (1, 2), (2, 3), (3, 4), (4, 6), (6, 8), (8, 10), (10, 16), (16, 24), (24, 32))
@@ -87,8 +90,9 @@ def tile_llamaadaptergatedpromptattention_t_kernel(tc, q_bytes, q_scale, k, v, g
         load_q(*Q_LOADS[0])
         load_q(*Q_LOADS[1])
         load_keys(0)
+        load_q(*Q_LOADS[2])
         load_keys(1)
-        for a, b in Q_LOADS[2:6]:
+        for a, b in Q_LOADS[3:6]:
             load_q(a, b)
         nc.sync.dma_start(out=gates[:], in_=gate.partition_broadcast(PROMPT_ROWS))
         nc.sync.dma_start(out=c_cols[:], in_=c.rearrange("h (p t) -> p h t", t=PACK))
@@ -118,6 +122,8 @@ def tile_llamaadaptergatedpromptattention_t_kernel(tc, q_bytes, q_scale, k, v, g
 
         early = [keep.tile([P, 2 * ROW], BF16, align_bytes=64, name="early%d" % n) for n in range(LEAD // 2)]
 
+        first_product = keep.tile([P, E], BF16, align_bytes=64)
+
         def q_stage(j):
             return early[j // 2][:, (j % 2) * ROW : (j % 2 + 1) * ROW] if j < LEAD else stage[(j - 2) % 3][:, ROW : 2 * ROW]
 
@@ -138,13 +144,13 @@ def tile_llamaadaptergatedpromptattention_t_kernel(tc, q_bytes, q_scale, k, v, g
 
         def q_scaled(j, i):
             if j == 2:
-                rows = k_raw[1][:]
+                rows = first_product[:]
             elif j == 4:
-                rows = live["k_grouped", 1][:]
+                rows = q_stage(1)
             elif j == 5:
-                rows = q_stage(3)
+                rows = q_stage(0) if i == 0 and SPLIT5 else q_stage(3)
             else:
-                rows = released(j - LEAD - 2).bitcast(BF16)
+                rows = released(j - LEAD - 2).bitcast(BF16)[:, (TILES - gpsimd_tiles(j)) * E :]
             return rows
 
         def gpsimd_tiles(j):
@@ -467,7 +473,7 @@ def tile_llamaadaptergatedpromptattention_t_kernel(tc, q_bytes, q_scale, k, v, g
 
         def result(j, tiles):
             if ("y", j, tiles) not in live:
-                live["y", j, tiles] = work.tile([P, len(tiles) * DV], F32, align_bytes=64, name="y", bufs=7)
+                live["y", j, tiles] = work.tile([P, len(tiles) * DV], F32, align_bytes=64, name="y", bufs=9)
             return live["y", j, tiles]
 
         def copy_o(j, tiles=BOTH, copy=nc.scalar.copy):
@@ -477,12 +483,17 @@ def tile_llamaadaptergatedpromptattention_t_kernel(tc, q_bytes, q_scale, k, v, g
                 out=out_view[j][:, tiles[0] : tiles[-1] + 1, :], in_=y[:].rearrange("p (i d) -> p i d", d=DV)
             )
 
+        def copy_half(j, i, copy=nc.scalar.copy):
+            y = result(j, (i,))
+            copy(out=y[:], in_=live["o", j, BOTH][:, i * DV : (i + 1) * DV])
+            nc.sync.dma_start(out=out_view[j][:, i : i + 1, :], in_=y[:].rearrange("p (i d) -> p i d", d=DV))
+
         def loop_copy_o(j):
-            if j + LAG + 1 < TAIL:
+            if j + LAG + 1 < TAIL or not V24:
                 copy_o(j)
 
         def vector_copy_o(j):
-            if j + LAG + 1 == TAIL:
+            if j + LAG + 1 == TAIL and V24:
                 copy_o(j, BOTH, nc.vector.tensor_copy)
 
         def prompt_weights(j):
@@ -532,20 +543,20 @@ def tile_llamaadaptergatedpromptattention_t_kernel(tc, q_bytes, q_scale, k, v, g
         sort_keys(0)
         turn_keys(0, "turn_b")
         scale_turned(0, A)
-        sort_keys(1)
         turn_q(1, "gain", B)
         turn_keys(1, "o")
         widen(2, 0, E, S)
         scale_gpsimd(2, A)
-        widen(3, 0, ROW, S)
-        scale_turned(0, B)
-        turn_q(3)
-        copy_keys(0, S)
         widen(2, E, ROW, S)
+        turn_q(2, "turn_q", B)
+        copy_keys(0, S)
+        scale_turned(0, B)
+        widen(3, 0, ROW, S)
         scale_turned(1)
+        turn_q(2, "turn_b", A)
+        turn_q(3, "gain")
         copy_keys(1, S)
         widen(4, 0, ROW, S)
-        turn_q(2, "turn_b")
         quant_keys(0)
         quant_early(0)
         quant_keys(1)
@@ -554,14 +565,14 @@ def tile_llamaadaptergatedpromptattention_t_kernel(tc, q_bytes, q_scale, k, v, g
         scores(1)
         widen(5, 0, ROW, S)
         start_gains()
-        widen(6, 0, ROW, S)
+        copy_q(2)
         gate_prompts()
-        scale_turned(3)
+        widen(6, 0, ROW, S)
         scale_turned(2)
+        scale_turned(3)
         spread_gains(0)
         maxima(0, A)
         widen(7, 0, ROW, S)
-        copy_q(2)
         widen(8, 0, E, S)
         biases(0, A)
         widen(8, E, ROW, S)

@@ -62,13 +62,17 @@ def tile_llamaadaptergatedpromptattention_t_kernel(tc, q_bytes, q_scale, k, v, g
         ident = keep.tile([P, P], F32)
         make_identity(nc, ident[:])
 
-        q_view = q_bytes.rearrange("h (j p i) e -> p (h j) (i e)", p=P, i=TILES)
-        out_view = out.rearrange("h (j p i) d -> (h j) p i d", p=P, i=TILES)
+        q_view = q_bytes.rearrange("h (n p m i) e -> p (h n) (m i e)", p=P, m=2, i=TILES)
+        out_quads = out.rearrange("h (n p m i) d -> (h n) m p i d", p=P, m=2, i=TILES)
+        out_view = [out_quads[j // 2][j % 2] for j in range(PAIRS)]
         q_raw, k_raw, v_raw = {}, {}, {}
 
         def load_q(a, b):
             raw = keep.tile([P, (b - a) * ROW], U8, align_bytes=64, name="q_raw%d" % a)
-            nc.sync.dma_start(out=raw[:].rearrange("p (j x) -> p j x", x=ROW), in_=q_view[:, a:b, :])
+            if b - a == 1:
+                nc.sync.dma_start(out=raw[:], in_=q_view[:, a // 2, (a % 2) * ROW : (a % 2 + 1) * ROW])
+            else:
+                nc.sync.dma_start(out=raw[:].rearrange("p (n x) -> p n x", x=2 * ROW), in_=q_view[:, a // 2 : b // 2, :])
             for j in range(a, b):
                 q_raw[j] = raw[:, (j - a) * ROW :]
 
@@ -99,10 +103,9 @@ def tile_llamaadaptergatedpromptattention_t_kernel(tc, q_bytes, q_scale, k, v, g
         load_q(*Q_LOADS[6])
         load_values(0)
         load_values(1)
-        load_keys(2)
-        load_q(*Q_LOADS[7])
         load_keys(3)
-        for a, b in Q_LOADS[8:]:
+        load_keys(2)
+        for a, b in Q_LOADS[7:]:
             load_q(a, b)
 
         c_rows = keep.tile([P, N], BF16, align_bytes=64)
@@ -616,7 +619,7 @@ def tile_llamaadaptergatedpromptattention_t_kernel(tc, q_bytes, q_scale, k, v, g
             (copy_b, 4): lambda: group_values(3),
             (turn_b, PAIRS_PER_HEAD - 1): lambda: spread_gains(1),
         }
-        extra_quants = {3: (quant_values, 0), 4: (quant_keys, 2), 6: (quant_keys, 3), 8: (quant_values, 1)}
+        extra_quants = {2: (quant_values, 0), 3: (quant_keys, 3), 4: (quant_keys, 2), 8: (quant_values, 1)}
         for s in range(2, TAIL):
             if s in extra_quants:
                 quant_fn, which = extra_quants[s]

@@ -65,6 +65,8 @@ def tile_llamaadaptergatedpromptattention_t_kernel(tc, q_bytes, q_scale, k, v, g
         q_view = q_bytes.rearrange("h (n p m i) e -> p (h n) (m i e)", p=P, m=2, i=TILES)
         out_quads = out.rearrange("h (n p m i) d -> (h n) m p i d", p=P, m=2, i=TILES)
         out_view = [out_quads[j // 2][j % 2] for j in range(PAIRS)]
+        out_rows = out.rearrange("h (n p q) d -> (h n) p (q d)", p=P, q=2 * TILES)[PAIRS // 2 - 1]
+        last_rows = keep.tile([P, 2 * TILES * DV], F32, align_bytes=64)
         q_raw, k_raw, v_raw = {}, {}, {}
 
         def load_q(a, b):
@@ -491,6 +493,21 @@ def tile_llamaadaptergatedpromptattention_t_kernel(tc, q_bytes, q_scale, k, v, g
             copy(out=y[:], in_=live["o", j, BOTH][:, i * DV : (i + 1) * DV])
             nc.sync.dma_start(out=out_view[j][:, i : i + 1, :], in_=y[:].rearrange("p (i d) -> p i d", d=DV))
 
+        def copy_last(j, tiles, copy):
+            first = TILES * (j % 2) + tiles[0]
+            cols = slice(first * DV, (first + len(tiles)) * DV)
+            copy(out=last_rows[:, cols], in_=live["o", j, tiles][:])
+
+        def store_last(a, b):
+            nc.sync.dma_start(out=out_rows[:, a * DV : b * DV], in_=last_rows[:, a * DV : b * DV])
+
+        def copy_tile(j, i):
+            cols = slice(i * DV, (i + 1) * DV)
+            y = result(j, BOTH)
+            nc.scalar.copy(out=y[:, cols], in_=live["o", j, BOTH][:, cols])
+            if i == TILES - 1:
+                nc.sync.dma_start(out=out_view[j], in_=y[:].rearrange("p (i d) -> p i d", d=DV))
+
         def loop_copy_o(j):
             if j + LAG + 1 < TAIL or not V24:
                 copy_o(j)
@@ -670,21 +687,25 @@ def tile_llamaadaptergatedpromptattention_t_kernel(tc, q_bytes, q_scale, k, v, g
         weights(31, A)
         outputs(28, BOTH, "z")
         outputs(29, BOTH, "z")
+        copy_o(27)
         copy_b(30)
         turn_b(31, A)
         weights(31, B)
         turn_b(31, B, TQ)
-        copy_o(27)
+        copy_o(28)
         quant_b(30)
-        copy_o(28, BOTH, V)
+        copy_o(29, BOTH, V)
         copy_b(31, A)
         copy_b(31, B)
-        outputs(30)
+        outputs(30, A)
+        outputs(30, B, "gain")
         quant_b(31, A)
         quant_b(31, B)
         outputs(31, A, "z")
         outputs(31, B, "z")
-        copy_o(29)
-        copy_o(31, A)
-        copy_o(30, BOTH, V)
-        copy_o(31, B, V)
+        copy_last(30, A, S)
+        copy_last(30, B, V)
+        store_last(0, 2)
+        copy_last(31, A, S)
+        copy_last(31, B, V)
+        store_last(2, 4)

@@ -33,21 +33,20 @@ SEGMENTS = ((0, 2 * PROMPT_ROWS), (2 * PROMPT_ROWS, N // 2))
 LEAD = 4
 LAG = 4
 TAIL = PAIRS - 3
-WIDEN_LONG = 448
-WIDEN_SHORT = 896
-LAST_SHARED = 29
+SHARE = 192
+WIDEN = 528
 FIRST_SHARED = 8
-PERIOD = 5
-SHARED = (3, 0)
+FIRST_WIDEN = 9
+HEAD_TILES = (0, 0, 1, 0, 2, 2, 2, 2)
+VECTOR_COPIES = (12, 24)
 RING = 4
+RELEASE = {4: 1, 5: 3}
 PAIRED = 32
 RELEASED = 29
-WARM = False
-NW = 128
-V24 = True
-SPLIT5 = False
 GPSIMD_WEIGHTS = ((27, 0), (28, 0), (29, 0))
-HEAD_TILES = (0, 0, 1, 0, 2, 2, 2)
+PROMPT_AT = SHARE
+TEXT_AT = PROMPT_AT + L
+TEXT_WORDS = P - PROMPT_ROWS
 Q_LOADS = ((0, 1), (1, 2), (2, 3), (3, 4), (4, 6), (6, 8), (8, 10), (10, 16), (16, 24), (24, 32))
 
 
@@ -91,7 +90,9 @@ def tile_llamaadaptergatedpromptattention_t_kernel(tc, q_bytes, q_scale, k, v, g
 
         scale_cols = keep.tile([P, PACK], F32)
         c_cols = keep.tile([P, H, PACK], BF16)
-        gates = keep.tile([PROMPT_ROWS, H], BF16)
+        gates = keep.tile([P, H], BF16)
+        c_prompts = keep.tile([P, H, 2], BF16)
+        share_cols = [keep.tile([P, 1], F32, name="share_col%d" % g) for g in range(2)]
         nc.sync.dma_start(out=scale_cols[:], in_=q_scale.rearrange("a b (p t) -> p (a b t)", t=PACK))
         load_q(*Q_LOADS[0])
         load_q(*Q_LOADS[1])
@@ -100,9 +101,13 @@ def tile_llamaadaptergatedpromptattention_t_kernel(tc, q_bytes, q_scale, k, v, g
         load_keys(1)
         for a, b in Q_LOADS[3:6]:
             load_q(a, b)
-        nc.sync.dma_start(out=gates[:], in_=gate.partition_broadcast(PROMPT_ROWS))
+        nc.sync.dma_start(out=gates[:], in_=gate.partition_broadcast(P))
+        with nc.allow_non_contiguous_dma(reason="one value a partition"):
+            nc.sync.dma_start(out=c_prompts[:, :, 0:1], in_=c[:, 0:L].rearrange("h (n o) -> n h o", o=1))
         nc.sync.dma_start(out=c_cols[:], in_=c.rearrange("h (p t) -> p h t", t=PACK))
         load_q(*Q_LOADS[6])
+        for g, first in enumerate((0, SHARE - P)):
+            nc.sync.dma_start(out=share_cols[g][:], in_=q_scale[0, :, first : first + P].rearrange("o n -> n o"))
         load_values(0)
         load_values(1)
         load_keys(3)
@@ -113,21 +118,20 @@ def tile_llamaadaptergatedpromptattention_t_kernel(tc, q_bytes, q_scale, k, v, g
         c_rows = keep.tile([P, N], BF16, align_bytes=64)
         nc.sync.dma_start(out=c_rows[:], in_=c[H - 1].partition_broadcast(P))
 
-        scale_rows = keep.tile([P, E], F32, align_bytes=64)
+        scale_rows = keep.tile([P, ROW], F32, align_bytes=64)
         scale_words = keep.tile([P, P, PACK], F32, align_bytes=64)
-        gain_cols = keep.tile([P, H, PACK], F32)
-        tanh_gates = keep.tile([PROMPT_ROWS, H], F32)
+        prompt_gains = keep.tile([P, H], F32)
+        tanh_gates = keep.tile([P, H], F32)
         k_codes = keep.tile([P, H, N], U32, align_bytes=64)
         k_scales = keep.tile([P, H, N], U8, align_bytes=64)
         v_codes = keep.tile([P, H, DV], U32, align_bytes=64)
         v_scales = keep.tile([P, H, DV], U8, align_bytes=64)
         stage = [keep.tile([P, 2 * ROW], BF16, align_bytes=64, name="stage%d" % n) for n in range(3)]
-        ring = [keep.tile([P, N + 2 * TILES], F32, align_bytes=64, name="ring%d" % n) for n in range(RING)]
+        ring = [keep.tile([P, N + 8], F32, align_bytes=64, name="ring%d" % n) for n in range(RING)]
         live = {}
 
         early = [keep.tile([P, 2 * ROW], BF16, align_bytes=64, name="early%d" % n) for n in range(LEAD // 2)]
-
-        first_product = keep.tile([P, E], BF16, align_bytes=64)
+        first_product = keep.tile([P, ROW], BF16, align_bytes=64)
 
         def q_stage(j):
             return early[j // 2][:, (j % 2) * ROW : (j % 2 + 1) * ROW] if j < LEAD else stage[(j - 2) % 3][:, ROW : 2 * ROW]
@@ -142,26 +146,21 @@ def tile_llamaadaptergatedpromptattention_t_kernel(tc, q_bytes, q_scale, k, v, g
             return ring[j % RING][:, 0:N]
 
         def row_sums(j):
-            return ring[(j - 1) % RING][:, N:]
+            return ring[(j - 1) % RING][:, N : N + 2 * TILES]
 
         def released(j):
-            return ring[j % RING][:, 2 * TILES :]
+            return ring[j % RING][:, 8:]
 
-        def q_scaled(j, i):
-            if j == 2:
-                rows = first_product[:]
-            elif j == 4:
-                rows = q_stage(1)
-            elif j == 5:
-                rows = q_stage(0) if i == 0 and SPLIT5 else q_stage(3)
-            else:
-                rows = released(j - LEAD - 2).bitcast(BF16)[:, (TILES - gpsimd_tiles(j)) * E :]
-            return rows
+        def q_scaled(j):
+            if j in RELEASE:
+                return q_stage(RELEASE[j])
+            return first_product[:] if j < LEAD else released(j - LEAD - 2).bitcast(BF16)
 
-        def gpsimd_tiles(j):
-            if j < len(HEAD_TILES):
-                return HEAD_TILES[j]
-            return 1 if j % PERIOD in SHARED and FIRST_SHARED <= j < LAST_SHARED else TILES
+        def share(j):
+            return 0 if j < FIRST_SHARED else SHARE
+
+        def scaled_tiles(j):
+            return HEAD_TILES[j] if j < len(HEAD_TILES) else TILES
 
         def spread_scales():
             ps = psum.tile([P, PACK, P], F32, name="z", bufs=4)
@@ -174,25 +173,45 @@ def tile_llamaadaptergatedpromptattention_t_kernel(tc, q_bytes, q_scale, k, v, g
 
         def copy_scales():
             nc.scalar.copy(
-                out=scale_rows[:].rearrange("m (p t) -> m p t", t=PACK), in_=live["scales"][:].rearrange("m t p -> m p t")
+                out=scale_rows[:, E:].rearrange("m (p t) -> m p t", t=PACK), in_=live["scales"][:].rearrange("m t p -> m p t")
             )
+
+        def share_scales():
+            for g, first in enumerate((0, SHARE - P)):
+                nc.tensor.transpose(
+                    live["consts"][:, first : first + P], share_cols[g][:].to_broadcast([P, P]), ident[:]
+                )
+
+        def open_consts():
+            live["consts"] = psum.tile([P, E], F32, name="consts", bufs=1)
+
+        def double_scales():
+            nc.gpsimd.tensor_copy(out=scale_rows[:, SHARE:E], in_=scale_rows[:, E + SHARE :])
 
         def start_gains():
             nc.scalar.activation(out=tanh_gates[:], in_=gates[:], func=ACTF.Tanh)
-            nc.scalar.copy(out=gain_cols[:], in_=c_cols[:])
 
         def gate_prompts():
             for h in range(H):
-                prompts = gain_cols[0:PROMPT_ROWS, h, :]
-                nc.scalar.activation(out=prompts, in_=prompts, func=ACTF.Copy, scale=tanh_gates[:, h : h + 1])
+                nc.scalar.activation(
+                    out=prompt_gains[:, h : h + 1], in_=c_prompts[:, h, 0:1], func=ACTF.Copy, scale=tanh_gates[:, h : h + 1]
+                )
 
         def spread_gains(h):
-            ps = psum.tile([P, 2, P, 2], F32, name="gain", bufs=1)
-            for t in range(PACK):
-                nc.tensor.transpose(
-                    ps[:, t // 2, :, t % 2], gain_cols[:, h, t : t + 1].to_broadcast([P, P]), ident[:]
-                )
-            live["gain", h] = ps[:].rearrange("m u p e -> m u (p e)")
+            pairs = c_cols[:, h, :].bitcast(F32)
+            consts = live["consts"]
+            for u in (1, 0):
+                end = TEXT_AT + (u + 1) * TEXT_WORDS
+                nc.tensor.transpose(consts[:, end - P : end], pairs[:, u : u + 1].to_broadcast([P, P]), ident[:])
+            nc.tensor.transpose(
+                consts[:, PROMPT_AT:TEXT_AT], prompt_gains[:, h : h + 1].to_broadcast([P, P]),
+                ident[:].rearrange("k (p u e) -> k u p e", u=2, e=2),
+            )
+
+        def gains(s):
+            if s == 0:
+                return live["consts"][:, PROMPT_AT:TEXT_AT].rearrange("m (u x) -> m u x", u=2)
+            return live["consts"][:, TEXT_AT:].bitcast(BF16).rearrange("m (u x) -> m u x", u=2)
 
         def sort_keys(half):
             words = keep.tile([P, 2, 2, P], F32, align_bytes=64, name="k_sorted%d" % half)
@@ -248,30 +267,36 @@ def tile_llamaadaptergatedpromptattention_t_kernel(tc, q_bytes, q_scale, k, v, g
             if a < b:
                 copy(out=live["wide", j][:, a:b], in_=q_raw[j][:, a:b].bitcast(FP8))
 
-        def gpsimd_columns(j):
-            if gpsimd_tiles(j - 1) < TILES:
-                return WIDEN_SHORT
-            return WIDEN_LONG if gpsimd_tiles(j - 2) < TILES else 0
+        def gpsimd_end(j):
+            return ROW if j - LEAD - 1 - LAG in VECTOR_COPIES else share(j) + WIDEN
 
         def widen_gpsimd(j):
-            if j > len(HEAD_TILES) + 1:
-                widen(j, 0, gpsimd_columns(j), nc.gpsimd.tensor_copy)
+            if j >= FIRST_WIDEN:
+                widen(j, share(j), gpsimd_end(j), nc.gpsimd.tensor_copy)
 
         def widen_scalar(j):
-            if j > len(HEAD_TILES) + 1:
-                widen(j, gpsimd_columns(j), ROW, nc.scalar.copy)
-
-        def scale_gpsimd(j, tiles=BOTH):
-            n = len(tiles)
-            cols = slice(tiles[0] * E, (tiles[-1] + 1) * E)
-            nc.gpsimd.tensor_tensor(
-                out=q_scaled(j, tiles[0])[:, cols].rearrange("p (i x) -> p i x", x=E),
-                in0=live["wide", j][:, cols].rearrange("p (i x) -> p i x", x=E),
-                in1=scale_rows[:].unsqueeze(1).to_broadcast([P, n, E]), op=ALU.mult,
-            )
+            if j >= FIRST_WIDEN:
+                widen(j, gpsimd_end(j), ROW, nc.scalar.copy)
 
         def product(j):
-            scale_gpsimd(j, BOTH[: gpsimd_tiles(j)])
+            if share(j):
+                nc.gpsimd.tensor_tensor(
+                    out=q_scaled(j)[:, SHARE:], in0=live["wide", j][:, SHARE:], in1=scale_rows[:, SHARE:], op=ALU.mult
+                )
+            else:
+                n = scaled_tiles(j)
+                nc.gpsimd.tensor_tensor(
+                    out=q_scaled(j)[:, 0 : n * E].rearrange("p (i x) -> p i x", x=E),
+                    in0=live["wide", j][:, 0 : n * E].rearrange("p (i x) -> p i x", x=E),
+                    in1=scale_rows[:, E:].unsqueeze(1).to_broadcast([P, n, E]), op=ALU.mult,
+                )
+
+        def scale_bytes(j):
+            if share(j):
+                nc.vector.tensor_tensor(
+                    out=q_scaled(j)[:, 0:SHARE], in0=q_raw[j][:, 0:SHARE].bitcast(FP8), in1=live["consts"][:, 0:SHARE],
+                    op=ALU.mult,
+                )
 
         def turn(words, bank, tiles):
             ps = psum.tile([P, len(tiles), 2, P], F32, name=bank, bufs=4 if bank == "z" else 1)
@@ -289,19 +314,19 @@ def tile_llamaadaptergatedpromptattention_t_kernel(tc, q_bytes, q_scale, k, v, g
         def turn_q(j, bank="turn_q", tiles=BOTH):
             ps = psum.tile([P, TILES, 2, P], F32, name=bank, bufs=4 if bank == "z" else 1)
             for i in tiles:
-                words = (q_scaled(j, i) if i < gpsimd_tiles(j) else live["wide", j][:]).bitcast(F32)
+                words = (q_scaled(j) if i < scaled_tiles(j) else live["wide", j][:]).bitcast(F32)
                 for u in range(2):
                     nc.tensor.transpose(ps[:, i, u, :], words[:, WORDS * i + u : WORDS * (i + 1) : 2], ident[:])
                 live["q_turned", j, i] = ps
 
         def copy_q(j):
-            n = gpsimd_tiles(j)
+            n = scaled_tiles(j)
             if n:
                 copy_turned(q_stage(j)[:, 0 : n * E], live["q_turned", j, 0][:, 0:n])
 
         def scale_turned(j, tiles=BOTH):
             for i in tiles:
-                if i >= gpsimd_tiles(j):
+                if i >= scaled_tiles(j):
                     turned = live["q_turned", j, i][:, i].rearrange("p u r -> p (u r)").bitcast(BF16)
                     nc.vector.tensor_tensor(
                         out=q_stage(j)[:, i * E : (i + 1) * E].rearrange("p (r u e) -> p r u e", u=2, e=2),
@@ -396,20 +421,19 @@ def tile_llamaadaptergatedpromptattention_t_kernel(tc, q_bytes, q_scale, k, v, g
             return live["b_rows", j, i]
 
         def weights(j, tiles=BOTH, segments=BOTH):
-            h = j // PAIRS_PER_HEAD
             for i in tiles:
                 for s, (a, b) in enumerate(SEGMENTS):
                     if s in segments and (s == 0 or (j, i) not in GPSIMD_WEIGHTS):
                         nc.vector.scalar_tensor_tensor(
                             out=b_tile(j, i)[:, :, a:b], in0=live["ex", j, i][:, :, a:b],
                             scalar=live["recip", j, i][:, 2 * i + s : 2 * i + s + 1],
-                            in1=live["gain", h][:, :, a:b], op0=ALU.mult, op1=ALU.mult,
+                            in1=gains(s), op0=ALU.mult, op1=ALU.mult,
                         )
 
         def gain_gpsimd(j, i):
             a, b = SEGMENTS[1]
             if i == 0 and j <= RELEASED:
-                gained = released(j - 1)
+                gained = released(j - 1)[:, 0:N]
             else:
                 gained = keep.tile([P, N], F32, align_bytes=64, name="gained%d_%d" % (j, i))[:]
             gained = gained.rearrange("p (u x) -> p u x", u=2)[:, :, a:b]
@@ -509,11 +533,11 @@ def tile_llamaadaptergatedpromptattention_t_kernel(tc, q_bytes, q_scale, k, v, g
                 nc.sync.dma_start(out=out_view[j], in_=y[:].rearrange("p (i d) -> p i d", d=DV))
 
         def loop_copy_o(j):
-            if j + LAG + 1 < TAIL or not V24:
+            if j not in VECTOR_COPIES:
                 copy_o(j)
 
         def vector_copy_o(j):
-            if j + LAG + 1 == TAIL and V24:
+            if j in VECTOR_COPIES:
                 copy_o(j, BOTH, nc.vector.tensor_copy)
 
         def prompt_weights(j):
@@ -523,17 +547,6 @@ def tile_llamaadaptergatedpromptattention_t_kernel(tc, q_bytes, q_scale, k, v, g
         def rest_weights(j):
             weights(j, BOTH, (1,) if j == TAIL - 2 else BOTH)
 
-        def warm(j, i, bank="o", n=256):
-            if WARM:
-                ps = psum.tile([P, n], F32, name=bank, bufs=4 if bank == "z" else 1)
-                nc.tensor.matmul(out=ps[:], lhsT=ident[:], rhs=live["ex", j, i][:, 0, 0:n], start=True, stop=True)
-
-        def first_exps(j):
-            exps(j, (0,))
-
-        def second_exps_step(j):
-            exps(j, (1,))
-
         def early_bias(j):
             if j == TAIL:
                 biases(j)
@@ -541,12 +554,6 @@ def tile_llamaadaptergatedpromptattention_t_kernel(tc, q_bytes, q_scale, k, v, g
         def late_bias(j):
             if j != TAIL:
                 biases(j)
-
-        def whole(fn, back):
-            return lambda j: fn(j) if gpsimd_tiles(j - back) == TILES else None
-
-        def shared(fn, back):
-            return lambda j: fn(j) if gpsimd_tiles(j - back) < TILES else None
 
         S = nc.scalar.copy
         A = (0,)
@@ -563,10 +570,11 @@ def tile_llamaadaptergatedpromptattention_t_kernel(tc, q_bytes, q_scale, k, v, g
         sort_keys(0)
         turn_keys(0, "turn_b")
         scale_turned(0, A)
-        turn_q(1, "gain", B)
+        turn_q(1, "consts", B)
         turn_keys(1, "o")
         widen(2, 0, E, S)
-        scale_gpsimd(2, A)
+        product(2)
+        double_scales()
         widen(2, E, ROW, S)
         turn_q(2, "turn_q", B)
         copy_keys(0, S)
@@ -574,13 +582,13 @@ def tile_llamaadaptergatedpromptattention_t_kernel(tc, q_bytes, q_scale, k, v, g
         widen(3, 0, ROW, S)
         scale_turned(1)
         turn_q(2, "turn_b", A)
-        turn_q(3, "gain")
+        turn_q(3, "consts")
         copy_keys(1, S)
         widen(4, 0, ROW, S)
         quant_keys(0)
         quant_early(0)
         quant_keys(1)
-        scale_gpsimd(4)
+        product(4)
         scores(0)
         scores(1)
         widen(5, 0, ROW, S)
@@ -590,15 +598,17 @@ def tile_llamaadaptergatedpromptattention_t_kernel(tc, q_bytes, q_scale, k, v, g
         widen(6, 0, ROW, S)
         scale_turned(2)
         scale_turned(3)
+        open_consts()
+        share_scales()
         spread_gains(0)
         maxima(0, A)
         widen(7, 0, ROW, S)
-        widen(8, 0, E, S)
+        widen(8, SHARE, E, S)
         biases(0, A)
         widen(8, E, ROW, S)
         maxima(0, B)
         quant_early(1)
-        scale_gpsimd(5)
+        product(5)
         group_values(1, nc.gpsimd.tensor_copy)
         turn_q(4)
         exps(0, A, A)
@@ -625,10 +635,10 @@ def tile_llamaadaptergatedpromptattention_t_kernel(tc, q_bytes, q_scale, k, v, g
         recips(1)
 
         step = (
-            (quant, 0), (product, LEAD), (widen_gpsimd, LEAD + 1), (weights_gpsimd, -1), (turn_q, 3), (turn_b, -2), (outputs, -LAG), (maxima, 1),
-            (exps, 0), (scores, 2), (scale_turned, 3), (prompt_weights, -1), (vector_copy_o, -LAG), (rest_weights, -1), (whole(copy_q, 0), 3), (early_bias, 1), (copy_b, -2),
-            (shared(widen_scalar, 2), LEAD + 1), (late_bias, 1), (shared(copy_q, 0), 3),
-            (recips, 0), (whole(widen_scalar, 2), LEAD + 1), (loop_copy_o, -LAG),
+            (quant, 0), (product, LEAD), (widen_gpsimd, LEAD + 1), (weights_gpsimd, -1), (turn_q, 3), (turn_b, -2),
+            (outputs, -LAG), (maxima, 1), (exps, 0), (scores, 2), (scale_bytes, LEAD), (prompt_weights, -1),
+            (vector_copy_o, -LAG), (rest_weights, -1), (copy_q, 3), (early_bias, 1), (copy_b, -2), (late_bias, 1),
+            (recips, 0), (widen_scalar, LEAD + 2), (loop_copy_o, -LAG),
         )
         behind = {
             (late_bias, 3): lambda: copy_keys(2, nc.scalar.copy),
@@ -698,7 +708,7 @@ def tile_llamaadaptergatedpromptattention_t_kernel(tc, q_bytes, q_scale, k, v, g
         copy_b(31, A)
         copy_b(31, B)
         outputs(30, A)
-        outputs(30, B, "gain")
+        outputs(30, B, "consts")
         quant_b(31, A)
         quant_b(31, B)
         outputs(31, A, "z")

@@ -34,7 +34,7 @@ LEAD = 4
 LAG = 4
 TAIL = PAIRS - 3
 SHARE = 192
-WIDEN = 528
+WIDEN = 448
 FIRST_SHARED = 8
 FIRST_WIDEN = 9
 HEAD_TILES = (0, 0, 1, 0, 2, 2, 2, 2)

@@ -34,9 +34,7 @@ LEAD = 4
 LAG = 4
 TAIL = PAIRS - 3
 SHARE = 192
-WIDEN = 448
 FIRST_SHARED = 8
-FIRST_WIDEN = 9
 HEAD_TILES = (0, 0, 1, 0, 2, 2, 2, 2)
 VECTOR_COPIES = (12, 24)
 RING = 4
@@ -118,7 +116,7 @@ def tile_llamaadaptergatedpromptattention_t_kernel(tc, q_bytes, q_scale, k, v, g
         c_rows = keep.tile([P, N], BF16, align_bytes=64)
         nc.sync.dma_start(out=c_rows[:], in_=c[H - 1].partition_broadcast(P))
 
-        scale_rows = keep.tile([P, ROW], F32, align_bytes=64)
+        scale_rows = keep.tile([P, E], F32, align_bytes=64)
         scale_words = keep.tile([P, P, PACK], F32, align_bytes=64)
         prompt_gains = keep.tile([P, H], F32)
         tanh_gates = keep.tile([P, H], F32)
@@ -157,7 +155,7 @@ def tile_llamaadaptergatedpromptattention_t_kernel(tc, q_bytes, q_scale, k, v, g
             return first_product[:] if j < LEAD else released(j - LEAD - 2).bitcast(BF16)
 
         def share(j):
-            return 0 if j < FIRST_SHARED else SHARE
+            return SHARE if j >= FIRST_SHARED and j % 2 == 0 else 0
 
         def scaled_tiles(j):
             return HEAD_TILES[j] if j < len(HEAD_TILES) else TILES
@@ -173,7 +171,7 @@ def tile_llamaadaptergatedpromptattention_t_kernel(tc, q_bytes, q_scale, k, v, g
 
         def copy_scales():
             nc.scalar.copy(
-                out=scale_rows[:, E:].rearrange("m (p t) -> m p t", t=PACK), in_=live["scales"][:].rearrange("m t p -> m p t")
+                out=scale_rows[:].rearrange("m (p t) -> m p t", t=PACK), in_=live["scales"][:].rearrange("m t p -> m p t")
             )
 
         def share_scales():
@@ -184,9 +182,6 @@ def tile_llamaadaptergatedpromptattention_t_kernel(tc, q_bytes, q_scale, k, v, g
 
         def open_consts():
             live["consts"] = psum.tile([P, E], F32, name="consts", bufs=1)
-
-        def double_scales():
-            nc.gpsimd.tensor_copy(out=scale_rows[:, SHARE:E], in_=scale_rows[:, E + SHARE :])
 
         def start_gains():
             nc.scalar.activation(out=tanh_gates[:], in_=gates[:], func=ACTF.Tanh)
@@ -267,36 +262,36 @@ def tile_llamaadaptergatedpromptattention_t_kernel(tc, q_bytes, q_scale, k, v, g
             if a < b:
                 copy(out=live["wide", j][:, a:b], in_=q_raw[j][:, a:b].bitcast(FP8))
 
-        def gpsimd_end(j):
-            return ROW if j - LEAD - 1 - LAG in VECTOR_COPIES else share(j) + WIDEN
-
         def widen_gpsimd(j):
-            if j >= FIRST_WIDEN:
-                widen(j, share(j), gpsimd_end(j), nc.gpsimd.tensor_copy)
+            if j > FIRST_SHARED and not share(j):
+                widen(j, 0, ROW, nc.gpsimd.tensor_copy)
 
-        def widen_scalar(j):
-            if j >= FIRST_WIDEN:
-                widen(j, gpsimd_end(j), ROW, nc.scalar.copy)
+        def widen_rest(j):
+            if share(j) and ("wide", j) not in live:
+                wide = work.tile([P, ROW], BF16, align_bytes=64, name="q_wide", bufs=7)
+                nc.scalar.copy(
+                    out=wide[:, 0 : TILES * (E - SHARE)],
+                    in_=q_raw[j][:, 0:ROW].bitcast(FP8).rearrange("p (i x) -> p i x", x=E)[:, :, SHARE:],
+                )
+                live["wide", j] = wide
 
         def product(j):
-            if share(j):
-                nc.gpsimd.tensor_tensor(
-                    out=q_scaled(j)[:, SHARE:], in0=live["wide", j][:, SHARE:], in1=scale_rows[:, SHARE:], op=ALU.mult
-                )
-            else:
-                n = scaled_tiles(j)
-                nc.gpsimd.tensor_tensor(
-                    out=q_scaled(j)[:, 0 : n * E].rearrange("p (i x) -> p i x", x=E),
-                    in0=live["wide", j][:, 0 : n * E].rearrange("p (i x) -> p i x", x=E),
-                    in1=scale_rows[:, E:].unsqueeze(1).to_broadcast([P, n, E]), op=ALU.mult,
-                )
+            n = scaled_tiles(j)
+            a = share(j)
+            nc.gpsimd.tensor_tensor(
+                out=q_scaled(j)[:, 0 : n * E].rearrange("p (i x) -> p i x", x=E)[:, :, a:],
+                in0=live["wide", j][:, 0 : n * (E - a)].rearrange("p (i x) -> p i x", i=n),
+                in1=scale_rows[:, a:].unsqueeze(1).to_broadcast([P, n, E - a]), op=ALU.mult,
+            )
 
         def scale_bytes(j):
             if share(j):
-                nc.vector.tensor_tensor(
-                    out=q_scaled(j)[:, 0:SHARE], in0=q_raw[j][:, 0:SHARE].bitcast(FP8), in1=live["consts"][:, 0:SHARE],
-                    op=ALU.mult,
-                )
+                for i in BOTH:
+                    cols = slice(i * E, i * E + SHARE)
+                    nc.vector.tensor_tensor(
+                        out=q_scaled(j)[:, cols], in0=q_raw[j][:, cols].bitcast(FP8), in1=live["consts"][:, 0:SHARE],
+                        op=ALU.mult,
+                    )
 
         def turn(words, bank, tiles):
             ps = psum.tile([P, len(tiles), 2, P], F32, name=bank, bufs=4 if bank == "z" else 1)
@@ -574,7 +569,6 @@ def tile_llamaadaptergatedpromptattention_t_kernel(tc, q_bytes, q_scale, k, v, g
         turn_keys(1, "o")
         widen(2, 0, E, S)
         product(2)
-        double_scales()
         widen(2, E, ROW, S)
         turn_q(2, "turn_q", B)
         copy_keys(0, S)
@@ -603,9 +597,8 @@ def tile_llamaadaptergatedpromptattention_t_kernel(tc, q_bytes, q_scale, k, v, g
         spread_gains(0)
         maxima(0, A)
         widen(7, 0, ROW, S)
-        widen(8, SHARE, E, S)
+        widen_rest(8)
         biases(0, A)
-        widen(8, E, ROW, S)
         maxima(0, B)
         quant_early(1)
         product(5)
@@ -638,7 +631,7 @@ def tile_llamaadaptergatedpromptattention_t_kernel(tc, q_bytes, q_scale, k, v, g
             (quant, 0), (product, LEAD), (widen_gpsimd, LEAD + 1), (weights_gpsimd, -1), (turn_q, 3), (turn_b, -2),
             (outputs, -LAG), (maxima, 1), (exps, 0), (scores, 2), (scale_bytes, LEAD), (prompt_weights, -1),
             (vector_copy_o, -LAG), (rest_weights, -1), (copy_q, 3), (early_bias, 1), (copy_b, -2), (late_bias, 1),
-            (recips, 0), (widen_scalar, LEAD + 2), (loop_copy_o, -LAG),
+            (recips, 0), (widen_rest, LEAD + 2), (loop_copy_o, -LAG),
         )
         behind = {
             (late_bias, 3): lambda: copy_keys(2, nc.scalar.copy),
@@ -646,7 +639,7 @@ def tile_llamaadaptergatedpromptattention_t_kernel(tc, q_bytes, q_scale, k, v, g
             (copy_b, 4): lambda: group_values(3),
             (turn_b, PAIRS_PER_HEAD - 1): lambda: spread_gains(1),
         }
-        extra_quants = {2: (quant_values, 0), 3: (quant_keys, 3), 4: (quant_keys, 2), 8: (quant_values, 1)}
+        extra_quants = {3: (quant_values, 0), 4: (quant_keys, 3), 5: (quant_keys, 2), 8: (quant_values, 1)}
         for s in range(2, TAIL):
             if s in extra_quants:
                 quant_fn, which = extra_quants[s]

@@ -36,7 +36,7 @@ TAIL = PAIRS - 3
 SHARE = 192
 FIRST_SHARED = 8
 HEAD_TILES = (0, 0, 1, 0, 2, 2, 2, 2)
-VECTOR_COPIES = (12, 24)
+VECTOR_COPIES = ()
 RING = 4
 RELEASE = {4: 1, 5: 3}
 PAIRED = 32
@@ -571,14 +571,14 @@ def tile_llamaadaptergatedpromptattention_t_kernel(tc, q_bytes, q_scale, k, v, g
         product(2)
         widen(2, E, ROW, S)
         turn_q(2, "turn_q", B)
+        widen(3, 0, ROW, S)
         copy_keys(0, S)
         scale_turned(0, B)
-        widen(3, 0, ROW, S)
         scale_turned(1)
         turn_q(2, "turn_b", A)
         turn_q(3, "consts")
-        copy_keys(1, S)
         widen(4, 0, ROW, S)
+        copy_keys(1, S)
         quant_keys(0)
         quant_early(0)
         quant_keys(1)

@@ -35,6 +35,7 @@ LAG = 4
 TAIL = PAIRS - 3
 SHARE = 192
 FIRST_SHARED = 8
+SHARED = tuple(range(10, 32, 2))
 HEAD_TILES = (0, 0, 1, 0, 2, 2, 2, 2)
 VECTOR_COPIES = ()
 RING = 4
@@ -155,7 +156,7 @@ def tile_llamaadaptergatedpromptattention_t_kernel(tc, q_bytes, q_scale, k, v, g
             return first_product[:] if j < LEAD else released(j - LEAD - 2).bitcast(BF16)
 
         def share(j):
-            return SHARE if j >= FIRST_SHARED and j % 2 == 0 else 0
+            return SHARE if j in SHARED else 0
 
         def scaled_tiles(j):
             return HEAD_TILES[j] if j < len(HEAD_TILES) else TILES
@@ -262,8 +263,17 @@ def tile_llamaadaptergatedpromptattention_t_kernel(tc, q_bytes, q_scale, k, v, g
             if a < b:
                 copy(out=live["wide", j][:, a:b], in_=q_raw[j][:, a:b].bitcast(FP8))
 
+        def widen_sorted(j, i):
+            widen(j, 0, 0, None)
+            cols = slice(i * E, (i + 1) * E)
+            nc.vector.tensor_copy(
+                out=live["wide", j][:, cols].rearrange("m (u p e) -> m p u e", u=2, e=2),
+                in_=q_raw[j][:, cols].bitcast(FP8).rearrange("m (p u e) -> m p u e", u=2, e=2),
+            )
+            live["sorted", j, i] = True
+
         def widen_gpsimd(j):
-            if j > FIRST_SHARED and not share(j):
+            if share(j - 1):
                 widen(j, 0, ROW, nc.gpsimd.tensor_copy)
 
         def widen_rest(j):
@@ -274,6 +284,10 @@ def tile_llamaadaptergatedpromptattention_t_kernel(tc, q_bytes, q_scale, k, v, g
                     in_=q_raw[j][:, 0:ROW].bitcast(FP8).rearrange("p (i x) -> p i x", x=E)[:, :, SHARE:],
                 )
                 live["wide", j] = wide
+
+        def widen_whole(j):
+            if j > FIRST_SHARED and not share(j) and not share(j - 1):
+                widen(j, 0, ROW, nc.scalar.copy)
 
         def product(j):
             n = scaled_tiles(j)
@@ -311,7 +325,11 @@ def tile_llamaadaptergatedpromptattention_t_kernel(tc, q_bytes, q_scale, k, v, g
             for i in tiles:
                 words = (q_scaled(j) if i < scaled_tiles(j) else live["wide", j][:]).bitcast(F32)
                 for u in range(2):
-                    nc.tensor.transpose(ps[:, i, u, :], words[:, WORDS * i + u : WORDS * (i + 1) : 2], ident[:])
+                    if ("sorted", j, i) in live:
+                        rows = words[:, WORDS * i + P * u : WORDS * i + P * (u + 1)]
+                    else:
+                        rows = words[:, WORDS * i + u : WORDS * (i + 1) : 2]
+                    nc.tensor.transpose(ps[:, i, u, :], rows, ident[:])
                 live["q_turned", j, i] = ps
 
         def copy_q(j):
@@ -555,11 +573,12 @@ def tile_llamaadaptergatedpromptattention_t_kernel(tc, q_bytes, q_scale, k, v, g
         B = (1,)
         spread_scales()
         repeat_scales()
-        widen(0, 0, E, nc.vector.tensor_copy)
+        widen_sorted(0, 0)
         widen(0, E, ROW, S)
         turn_q(0, "z", A)
         turn_q(0, "z", B)
-        widen(1, 0, ROW, S)
+        widen_sorted(1, 0)
+        widen_sorted(1, 1)
         turn_q(1, "z", A)
         copy_scales()
         sort_keys(0)
@@ -597,12 +616,13 @@ def tile_llamaadaptergatedpromptattention_t_kernel(tc, q_bytes, q_scale, k, v, g
         spread_gains(0)
         maxima(0, A)
         widen(7, 0, ROW, S)
-        widen_rest(8)
+        widen(8, 0, ROW, S)
+        group_values(0)
         biases(0, A)
         maxima(0, B)
         quant_early(1)
         product(5)
-        group_values(1, nc.gpsimd.tensor_copy)
+        group_values(2, nc.gpsimd.tensor_copy)
         turn_q(4)
         exps(0, A, A)
         biases(0, B)
@@ -613,8 +633,7 @@ def tile_llamaadaptergatedpromptattention_t_kernel(tc, q_bytes, q_scale, k, v, g
         maxima(1, B)
         scores(2)
         turn_keys(3, "turn_b")
-        turn_keys(2, "o")
-        group_values(0)
+        group_values(1)
         biases(1)
         copy_q(4)
         weights(0, A)
@@ -631,15 +650,15 @@ def tile_llamaadaptergatedpromptattention_t_kernel(tc, q_bytes, q_scale, k, v, g
             (quant, 0), (product, LEAD), (widen_gpsimd, LEAD + 1), (weights_gpsimd, -1), (turn_q, 3), (turn_b, -2),
             (outputs, -LAG), (maxima, 1), (exps, 0), (scores, 2), (scale_bytes, LEAD), (prompt_weights, -1),
             (vector_copy_o, -LAG), (rest_weights, -1), (copy_q, 3), (early_bias, 1), (copy_b, -2), (late_bias, 1),
-            (recips, 0), (widen_rest, LEAD + 2), (loop_copy_o, -LAG),
+            (recips, 0), (widen_rest, LEAD + 2), (widen_whole, LEAD + 2), (loop_copy_o, -LAG),
         )
         behind = {
             (late_bias, 3): lambda: copy_keys(2, nc.scalar.copy),
-            (late_bias, 4): lambda: group_values(2),
-            (copy_b, 4): lambda: group_values(3),
+            (turn_b, 0): lambda: turn_keys(2, "o"),
+            (late_bias, 4): lambda: group_values(3),
             (turn_b, PAIRS_PER_HEAD - 1): lambda: spread_gains(1),
         }
-        extra_quants = {3: (quant_values, 0), 4: (quant_keys, 3), 5: (quant_keys, 2), 8: (quant_values, 1)}
+        extra_quants = {2: (quant_values, 0), 3: (quant_keys, 3), 4: (quant_keys, 2), 8: (quant_values, 1)}
         for s in range(2, TAIL):
             if s in extra_quants:
                 quant_fn, which = extra_quants[s]

from contextlib import ExitStack

import concourse.mybir as mybir
from concourse.masks import make_identity

H, T, E, L, S, DV = 2, 4096, 512, 128, 384, 256
N = L + S
P = 128
FLOPS = 2 * H * T * N * (E + DV)

F32 = mybir.dt.float32
BF16 = mybir.dt.bfloat16
U32 = mybir.dt.uint32
U8 = mybir.dt.uint8
FP8 = mybir.dt.float8_e4m3fn
FP8X4 = mybir.dt.float8_e4m3fn_x4
ALU = mybir.AluOpType
ACTF = mybir.ActivationFunctionType
AX = mybir.AxisListType

PACK = 4
TILES = 2
BOTH = (0, 1)
PAIR = TILES * P
ROW = TILES * E
WORDS = E // 2
PAIRS_PER_HEAD = T // PAIR
PAIRS = H * PAIRS_PER_HEAD
ROOT = 512.0 ** -0.5
PROMPT_ROWS = L // PACK
SEGMENTS = ((0, 2 * PROMPT_ROWS), (2 * PROMPT_ROWS, N // 2))

LEAD = 4
LAG = 4
TAIL = PAIRS - 3
SHARE = 192
FIRST_SHARED = 8
SHARED = tuple(range(10, 32, 2))
HEAD_TILES = (0, 0, 1, 0, 2, 2, 2, 2)
VECTOR_COPIES = ()
RING = 4
RELEASE = {4: 1, 5: 3}
PAIRED = 32
RELEASED = 29
GPSIMD_WEIGHTS = ((27, 0), (28, 0), (29, 0))
PROMPT_AT = SHARE
TEXT_AT = PROMPT_AT + L
TEXT_WORDS = P - PROMPT_ROWS
Q_LOADS = ((0, 1), (1, 2), (2, 3), (3, 4), (4, 6), (6, 8), (8, 10), (10, 16), (16, 24), (24, 32))


def tile_llamaadaptergatedpromptattention_t_kernel(tc, q_bytes, q_scale, k, v, gate, c, out):
    nc = tc.nc
    with ExitStack() as ctx:
        keep = ctx.enter_context(tc.tile_pool(name="keep", bufs=1))
        work = ctx.enter_context(tc.tile_pool(name="work", bufs=3))
        psum = ctx.enter_context(tc.psum_pool(name="psum", bufs=1))
        ctx.enter_context(tc.manual_schedule())

        ident = keep.tile([P, P], F32)
        make_identity(nc, ident[:])

        q_view = q_bytes.rearrange("h (n p m i) e -> p (h n) (m i e)", p=P, m=2, i=TILES)
        out_quads = out.rearrange("h (n p m i) d -> (h n) m p i d", p=P, m=2, i=TILES)
        out_view = [out_quads[j // 2][j % 2] for j in range(PAIRS)]
        out_rows = out.rearrange("h (n p q) d -> (h n) p (q d)", p=P, q=2 * TILES)[PAIRS // 2 - 1]
        last_rows = keep.tile([P, 2 * TILES * DV], F32, align_bytes=64)
        q_raw, k_raw, v_raw = {}, {}, {}

        def load_q(a, b):
            raw = keep.tile([P, (b - a) * ROW], U8, align_bytes=64, name="q_raw%d" % a)
            if b - a == 1:
                nc.sync.dma_start(out=raw[:], in_=q_view[:, a // 2, (a % 2) * ROW : (a % 2 + 1) * ROW])
            else:
                nc.sync.dma_start(out=raw[:].rearrange("p (n x) -> p n x", x=2 * ROW), in_=q_view[:, a // 2 : b // 2, :])
            for j in range(a, b):
                q_raw[j] = raw[:, (j - a) * ROW :]

        def load_keys(half):
            h, u = divmod(half, 2)
            raw = keep.tile([P, 2 * E], BF16, align_bytes=64, name="k_raw%d" % half)
            nc.sync.dma_start(out=raw[:], in_=k[h].rearrange("(r u e) x -> u r (e x)", u=2, e=2)[u])
            k_raw[half] = raw

        def load_values(h):
            raw = keep.tile([P, PACK * DV], BF16, align_bytes=64, name="v_raw%d" % h)
            nc.sync.dma_start(out=raw[:], in_=v[h].rearrange("(p t) x -> p (t x)", t=PACK))
            v_raw[h] = raw

        scale_cols = keep.tile([P, PACK], F32)
        c_cols = keep.tile([P, H, PACK], BF16)
        gates = keep.tile([P, H], BF16)
        c_prompts = keep.tile([P, H, 2], BF16)
        share_cols = [keep.tile([P, 1], F32, name="share_col%d" % g) for g in range(2)]
        nc.sync.dma_start(out=scale_cols[:], in_=q_scale.rearrange("a b (p t) -> p (a b t)", t=PACK))
        load_q(*Q_LOADS[0])
        load_q(*Q_LOADS[1])
        load_keys(0)
        load_q(*Q_LOADS[2])
        load_keys(1)
        for a, b in Q_LOADS[3:6]:
            load_q(a, b)
        nc.sync.dma_start(out=gates[:], in_=gate.partition_broadcast(P))
        with nc.allow_non_contiguous_dma(reason="one value a partition"):
            nc.sync.dma_start(out=c_prompts[:, :, 0:1], in_=c[:, 0:L].rearrange("h (n o) -> n h o", o=1))
        nc.sync.dma_start(out=c_cols[:], in_=c.rearrange("h (p t) -> p h t", t=PACK))
        load_q(*Q_LOADS[6])
        for g, first in enumerate((0, SHARE - P)):
            nc.sync.dma_start(out=share_cols[g][:], in_=q_scale[0, :, first : first + P].rearrange("o n -> n o"))
        load_values(0)
        load_values(1)
        load_keys(3)
        load_keys(2)
        for a, b in Q_LOADS[7:]:
            load_q(a, b)

        c_rows = keep.tile([P, N], BF16, align_bytes=64)
        nc.sync.dma_start(out=c_rows[:], in_=c[H - 1].partition_broadcast(P))

        scale_rows = keep.tile([P, E], F32, align_bytes=64)
        scale_words = keep.tile([P, P, PACK], F32, align_bytes=64)
        prompt_gains = keep.tile([P, H], F32)
        tanh_gates = keep.tile([P, H], F32)
        k_codes = keep.tile([P, H, N], U32, align_bytes=64)
        k_scales = keep.tile([P, H, N], U8, align_bytes=64)
        v_codes = keep.tile([P, H, DV], U32, align_bytes=64)
        v_scales = keep.tile([P, H, DV], U8, align_bytes=64)
        stage = [keep.tile([P, 2 * ROW], BF16, align_bytes=64, name="stage%d" % n) for n in range(3)]
        ring = [keep.tile([P, N + 8], F32, align_bytes=64, name="ring%d" % n) for n in range(RING)]
        live = {}

        early = [keep.tile([P, 2 * ROW], BF16, align_bytes=64, name="early%d" % n) for n in range(LEAD // 2)]
        first_product = keep.tile([P, ROW], BF16, align_bytes=64)

        def q_stage(j):
            return early[j // 2][:, (j % 2) * ROW : (j % 2 + 1) * ROW] if j < LEAD else stage[(j - 2) % 3][:, ROW : 2 * ROW]

        def b_stage(j):
            if j < PAIRED:
                return stage[(j + LAG) % 3][:, 0:ROW]
            n, half = divmod(j - PAIRED, 2)
            return stage[(PAIRED + LAG + n) % 3][:, half * ROW : (half + 1) * ROW]

        def second_exps(j):
            return ring[j % RING][:, 0:N]

        def row_sums(j):
            return ring[(j - 1) % RING][:, N : N + 2 * TILES]

        def released(j):
            return ring[j % RING][:, 8:]

        def q_scaled(j):
            if j in RELEASE:
                return q_stage(RELEASE[j])
            return first_product[:] if j < LEAD else released(j - LEAD - 2).bitcast(BF16)

        def share(j):
            return SHARE if j in SHARED else 0

        def scaled_tiles(j):
            return HEAD_TILES[j] if j < len(HEAD_TILES) else TILES

        def spread_scales():
            ps = psum.tile([P, PACK, P], F32, name="z", bufs=4)
            for t in range(PACK):
                nc.tensor.transpose(ps[:, t, :], scale_cols[:, t : t + 1].to_broadcast([P, P]), ident[:])
            live["scales"] = ps

        def repeat_scales():
            nc.vector.tensor_copy(out=scale_words[:], in_=scale_cols[:].unsqueeze(1).to_broadcast([P, P, PACK]))

        def copy_scales():
            nc.scalar.copy(
                out=scale_rows[:].rearrange("m (p t) -> m p t", t=PACK), in_=live["scales"][:].rearrange("m t p -> m p t")
            )

        def share_scales():
            for g, first in enumerate((0, SHARE - P)):
                nc.tensor.transpose(
                    live["consts"][:, first : first + P], share_cols[g][:].to_broadcast([P, P]), ident[:]
                )

        def open_consts():
            live["consts"] = psum.tile([P, E], F32, name="consts", bufs=1)

        def start_gains():
            nc.scalar.activation(out=tanh_gates[:], in_=gates[:], func=ACTF.Tanh)

        def gate_prompts():
            for h in range(H):
                nc.scalar.activation(
                    out=prompt_gains[:, h : h + 1], in_=c_prompts[:, h, 0:1], func=ACTF.Copy, scale=tanh_gates[:, h : h + 1]
                )

        def spread_gains(h):
            pairs = c_cols[:, h, :].bitcast(F32)
            consts = live["consts"]
            for u in (1, 0):
                end = TEXT_AT + (u + 1) * TEXT_WORDS
                nc.tensor.transpose(consts[:, end - P : end], pairs[:, u : u + 1].to_broadcast([P, P]), ident[:])
            nc.tensor.transpose(
                consts[:, PROMPT_AT:TEXT_AT], prompt_gains[:, h : h + 1].to_broadcast([P, P]),
                ident[:].rearrange("k (p u e) -> k u p e", u=2, e=2),
            )

        def gains(s):
            if s == 0:
                return live["consts"][:, PROMPT_AT:TEXT_AT].rearrange("m (u x) -> m u x", u=2)
            return live["consts"][:, TEXT_AT:].bitcast(BF16).rearrange("m (u x) -> m u x", u=2)

        def sort_keys(half):
            words = keep.tile([P, 2, 2, P], F32, align_bytes=64, name="k_sorted%d" % half)
            nc.vector.tensor_copy(
                out=words[:], in_=k_raw[half][:].bitcast(F32).rearrange("r (e p u) -> r e u p", e=2, u=2)
            )
            live["k_sorted", half] = words

        def turn_keys(half, bank):
            ps = psum.tile([P, 2, 2, P], F32, name=bank, bufs=1)
            for e in range(2):
                words = k_raw[half][:, e * E : (e + 1) * E].bitcast(F32)
                for u in range(2):
                    rows = live["k_sorted", half][:, e, u, :] if ("k_sorted", half) in live else words[:, u:WORDS:2]
                    nc.tensor.transpose(ps[:, e, u, :], rows, ident[:])
            live["k_turned", half] = ps

        def copy_keys(half, copy):
            grouped = keep.tile([P, PACK * N // 2], BF16, align_bytes=64, name="k_grouped%d" % half)
            copy(
                out=grouped[:].bitcast(F32).rearrange("p (r e u) -> p r e u", e=2, u=2),
                in_=live["k_turned", half][:].rearrange("p e u r -> p r e u"),
            )
            live["k_grouped", half] = grouped

        def quant_keys(half):
            h, u = divmod(half, 2)
            cols = slice(u * N // 2, (u + 1) * N // 2)
            nc.vector.quantize_mx(
                out=k_codes[:, h, cols].bitcast(FP8X4), scales=k_scales[:, h, cols], in_=live["k_grouped", half][:]
            )

        def group_values(half, copy=nc.scalar.copy):
            h, w = divmod(half, 2)
            if ("v_grouped", h) not in live:
                live["v_grouped", h] = keep.tile([P, DV, PACK], BF16, align_bytes=64, name="v_grouped%d" % h)
            cols = slice(w * DV // 2, (w + 1) * DV // 2)
            rows = v_raw[h][:].rearrange("p (t d) -> p t d", t=PACK)
            copy(
                out=live["v_grouped", h][:, cols, :].rearrange("p (g i) t -> p g t i", i=4),
                in_=rows[:, :, cols].rearrange("p t (g i) -> p g t i", i=4),
            )

        def quant_values(h):
            nc.vector.quantize_mx(
                out=v_codes[:, h, :].bitcast(FP8X4), scales=v_scales[:, h, :],
                in_=live["v_grouped", h][:].rearrange("p d t -> p (d t)"),
            )

        def widen(j, a, b, copy):
            if ("wide", j) not in live:
                live["wide", j] = work.tile([P, ROW], BF16, align_bytes=64, name="q_wide", bufs=7)
            if a < b:
                copy(out=live["wide", j][:, a:b], in_=q_raw[j][:, a:b].bitcast(FP8))

        def widen_sorted(j, i):
            widen(j, 0, 0, None)
            cols = slice(i * E, (i + 1) * E)
            nc.vector.tensor_copy(
                out=live["wide", j][:, cols].rearrange("m (u p e) -> m p u e", u=2, e=2),
                in_=q_raw[j][:, cols].bitcast(FP8).rearrange("m (p u e) -> m p u e", u=2, e=2),
            )
            live["sorted", j, i] = True

        def widen_gpsimd(j):
            if share(j - 1):
                widen(j, 0, ROW, nc.gpsimd.tensor_copy)

        def widen_rest(j):
            if share(j) and ("wide", j) not in live:
                wide = work.tile([P, ROW], BF16, align_bytes=64, name="q_wide", bufs=7)
                nc.scalar.copy(
                    out=wide[:, 0 : TILES * (E - SHARE)],
                    in_=q_raw[j][:, 0:ROW].bitcast(FP8).rearrange("p (i x) -> p i x", x=E)[:, :, SHARE:],
                )
                live["wide", j] = wide

        def widen_whole(j):
            if j > FIRST_SHARED and not share(j) and not share(j - 1):
                widen(j, 0, ROW, nc.scalar.copy)

        def product(j):
            n = scaled_tiles(j)
            a = share(j)
            nc.gpsimd.tensor_tensor(
                out=q_scaled(j)[:, 0 : n * E].rearrange("p (i x) -> p i x", x=E)[:, :, a:],
                in0=live["wide", j][:, 0 : n * (E - a)].rearrange("p (i x) -> p i x", i=n),
                in1=scale_rows[:, a:].unsqueeze(1).to_broadcast([P, n, E - a]), op=ALU.mult,
            )

        def scale_bytes(j):
            if share(j):
                for i in BOTH:
                    cols = slice(i * E, i * E + SHARE)
                    nc.vector.tensor_tensor(
                        out=q_scaled(j)[:, cols], in0=q_raw[j][:, cols].bitcast(FP8), in1=live["consts"][:, 0:SHARE],
                        op=ALU.mult,
                    )

        def turn(words, bank, tiles):
            ps = psum.tile([P, len(tiles), 2, P], F32, name=bank, bufs=4 if bank == "z" else 1)
            for n, i in enumerate(tiles):
                for u in range(2):
                    nc.tensor.transpose(ps[:, n, u, :], words(i, u), ident[:])
            return ps

        def copy_turned(dst, ps):
            nc.scalar.copy(
                out=dst.bitcast(F32).rearrange("p (i r u) -> p i r u", r=P, u=2),
                in_=ps.rearrange("p i u r -> p i r u"),
            )

        def turn_q(j, bank="turn_q", tiles=BOTH):
            ps = psum.tile([P, TILES, 2, P], F32, name=bank, bufs=4 if bank == "z" else 1)
            for i in tiles:
                words = (q_scaled(j) if i < scaled_tiles(j) else live["wide", j][:]).bitcast(F32)
                for u in range(2):
                    if ("sorted", j, i) in live:
                        rows = words[:, WORDS * i + P * u : WORDS * i + P * (u + 1)]
                    else:
                        rows = words[:, WORDS * i + u : WORDS * (i + 1) : 2]
                    nc.tensor.transpose(ps[:, i, u, :], rows, ident[:])
                live["q_turned", j, i] = ps

        def copy_q(j):
            n = scaled_tiles(j)
            if n:
                copy_turned(q_stage(j)[:, 0 : n * E], live["q_turned", j, 0][:, 0:n])

        def scale_turned(j, tiles=BOTH):
            for i in tiles:
                if i >= scaled_tiles(j):
                    turned = live["q_turned", j, i][:, i].rearrange("p u r -> p (u r)").bitcast(BF16)
                    nc.vector.tensor_tensor(
                        out=q_stage(j)[:, i * E : (i + 1) * E].rearrange("p (r u e) -> p r u e", u=2, e=2),
                        in0=turned.rearrange("p (u r e) -> p r u e", u=2, e=2),
                        in1=scale_words[:].rearrange("p r (u e) -> p r u e", e=2),
                        op=ALU.mult,
                    )

        def quant_early(n):
            codes = work.tile([P, 2 * PAIR], U32, align_bytes=64, name="q_codes", bufs=2)
            scales = work.tile([P, 2 * PAIR], U8, align_bytes=64, name="q_scales", bufs=2)
            nc.vector.quantize_mx(out=codes[:].bitcast(FP8X4), scales=scales[:], in_=early[n][:])
            for m in range(2):
                live["q_codes", 2 * n + m] = (codes[:, m * PAIR : (m + 1) * PAIR], scales[:, m * PAIR : (m + 1) * PAIR])

        def quant(s):
            a = 0 if s >= LAG else PAIR
            b = 2 * PAIR if s + 2 < PAIRS else PAIR
            codes = work.tile([P, 2 * PAIR], U32, align_bytes=64, name="codes")
            scales = work.tile([P, 2 * PAIR], U8, align_bytes=64, name="scales")
            nc.vector.quantize_mx(
                out=codes[:, a:b].bitcast(FP8X4), scales=scales[:, a:b], in_=stage[s % 3][:, PACK * a : PACK * b]
            )
            for i in BOTH:
                live["b_codes", s - LAG, i] = (codes[:, 0:PAIR], scales[:, 0:PAIR])
            live["q_codes", s + 2] = (codes[:, PAIR:], scales[:, PAIR:])

        def scores(j):
            h = j // PAIRS_PER_HEAD
            codes, scales = live["q_codes", j]
            for i in BOTH:
                z = psum.tile([P, 2, N // 2], F32, name="z", bufs=4)
                nc.tensor.matmul_mx(
                    out=z[:].rearrange("p u x -> p (u x)"),
                    lhsT=codes[:, i * P : (i + 1) * P].bitcast(FP8X4),
                    lhsT_scale=scales[:, i * P : (i + 1) * P],
                    rhs=k_codes[:, h, :].bitcast(FP8X4),
                    rhs_scale=k_scales[:, h, :],
                    start=True,
                    stop=True,
                )
                live["z", j, i] = z

        def maxima(j, tiles=BOTH):
            if ("max", j, 0) in live:
                row_max = live["max", j, 0]
            else:
                row_max = work.tile([P, 2 * TILES], F32, name="row_max", bufs=8)
            for i in tiles:
                for s, (a, b) in enumerate(SEGMENTS):
                    nc.vector.tensor_reduce(
                        out=row_max[:, 2 * i + s : 2 * i + s + 1], in_=live["z", j, i][:, :, a:b], axis=AX.XY, op=ALU.max
                    )
                live["max", j, i] = row_max

        def biases(j, tiles=BOTH):
            cols = slice(2 * tiles[0], 2 * tiles[-1] + 2)
            bias = work.tile([P, 2 * TILES], F32, name="bias", bufs=8)
            nc.scalar.activation(out=bias[:, cols], in_=live["max", j, tiles[0]][:, cols], func=ACTF.Copy, scale=-ROOT)
            for i in tiles:
                live["bias", j, i] = bias

        def exps(j, tiles=BOTH, segments=BOTH):
            sums = row_sums(j)
            for i in tiles:
                if ("ex", j, i) in live:
                    ex = live["ex", j, i]
                elif i == 0:
                    ex = work.tile([P, 2, N // 2], F32, align_bytes=64, name="ex", bufs=4)
                else:
                    ex = second_exps(j).rearrange("p (u x) -> p u x", u=2)
                for s in segments:
                    a, b = SEGMENTS[s]
                    col = slice(2 * i + s, 2 * i + s + 1)
                    nc.scalar.activation(
                        out=ex[:, :, a:b], in_=live["z", j, i][:, :, a:b], func=ACTF.Exp,
                        bias=live["bias", j, i][:, col], scale=ROOT, accum_out=sums[:, col],
                    )
                live["ex", j, i] = ex

        def recips(j, tiles=BOTH):
            cols = slice(2 * tiles[0], 2 * tiles[-1] + 2)
            recip = work.tile([P, 2 * TILES], F32, name="recip", bufs=8)
            nc.vector.reciprocal(out=recip[:, cols], in_=row_sums(j)[:, cols])
            for i in tiles:
                live["recip", j, i] = recip

        def b_tile(j, i):
            if ("b_rows", j, i) not in live:
                live["b_rows", j, i] = work.tile([P, 2, N // 2], BF16, align_bytes=64, name="b_rows%d" % i, bufs=4)
                live["b_words", j, i] = live["b_rows", j, i][:].rearrange("p u x -> p (u x)").bitcast(F32)
            return live["b_rows", j, i]

        def weights(j, tiles=BOTH, segments=BOTH):
            for i in tiles:
                for s, (a, b) in enumerate(SEGMENTS):
                    if s in segments and (s == 0 or (j, i) not in GPSIMD_WEIGHTS):
                        nc.vector.scalar_tensor_tensor(
                            out=b_tile(j, i)[:, :, a:b], in0=live["ex", j, i][:, :, a:b],
                            scalar=live["recip", j, i][:, 2 * i + s : 2 * i + s + 1],
                            in1=gains(s), op0=ALU.mult, op1=ALU.mult,
                        )

        def gain_gpsimd(j, i):
            a, b = SEGMENTS[1]
            if i == 0 and j <= RELEASED:
                gained = released(j - 1)[:, 0:N]
            else:
                gained = keep.tile([P, N], F32, align_bytes=64, name="gained%d_%d" % (j, i))[:]
            gained = gained.rearrange("p (u x) -> p u x", u=2)[:, :, a:b]
            nc.gpsimd.tensor_tensor(
                out=gained.rearrange("m u (p e) -> m u p e", e=2),
                in0=live["ex", j, i][:, :, a:b].rearrange("m u (p e) -> m u p e", e=2),
                in1=c_rows[:].rearrange("m (p u e) -> m u p e", u=2, e=2)[:, :, PROMPT_ROWS:, :], op=ALU.mult,
            )
            live["gained", j, i] = gained

        def divide_gpsimd(j, i):
            a, b = SEGMENTS[1]
            nc.gpsimd.tensor_scalar(
                out=b_tile(j, i)[:, :, a:b], in0=live["gained", j, i], scalar1=live["recip", j, i][:, 2 * i + 1 : 2 * i + 2],
                scalar2=0.0, op0=ALU.mult, op1=ALU.add,
            )

        def weights_gpsimd(j):
            for fn in (gain_gpsimd, divide_gpsimd):
                for i in BOTH:
                    if (j, i) in GPSIMD_WEIGHTS:
                        fn(j, i)

        def turn_b(j, tiles=BOTH, bank="turn_b"):
            live["b_turned", j, tiles] = turn(lambda i, u: live["b_words", j, i][:, P * u : P * (u + 1)], bank, tiles)

        def copy_b(j, tiles=BOTH):
            copy_turned(b_stage(j)[:, tiles[0] * N : (tiles[-1] + 1) * N], live["b_turned", j, tiles][:])

        def quant_b(j, tiles=BOTH):
            cols = slice(tiles[0] * P, (tiles[-1] + 1) * P)
            codes = work.tile([P, PAIR], U32, align_bytes=64, name="b_codes", bufs=4)
            scales = work.tile([P, PAIR], U8, align_bytes=64, name="b_scales", bufs=4)
            nc.vector.quantize_mx(
                out=codes[:, cols].bitcast(FP8X4), scales=scales[:, cols],
                in_=b_stage(j)[:, tiles[0] * N : (tiles[-1] + 1) * N],
            )
            for i in tiles:
                live["b_codes", j, i] = (codes, scales)

        def quant_two(j):
            codes = work.tile([P, 2 * PAIR], U32, align_bytes=64, name="codes")
            scales = work.tile([P, 2 * PAIR], U8, align_bytes=64, name="scales")
            nc.vector.quantize_mx(
                out=codes[:].bitcast(FP8X4), scales=scales[:], in_=stage[(PAIRED + LAG + (j - PAIRED) // 2) % 3][:]
            )
            for n in range(2):
                for i in BOTH:
                    live["b_codes", j + n, i] = (codes[:, n * PAIR : (n + 1) * PAIR], scales[:, n * PAIR : (n + 1) * PAIR])

        def outputs(j, tiles=BOTH, bank="o"):
            h = j // PAIRS_PER_HEAD
            codes, scales = live["b_codes", j, tiles[0]]
            o = psum.tile([P, len(tiles) * DV], F32, name=bank, bufs=4 if bank == "z" else 1)
            for n, i in enumerate(tiles):
                nc.tensor.matmul_mx(
                    out=o[:, n * DV : (n + 1) * DV],
                    lhsT=codes[:, i * P : (i + 1) * P].bitcast(FP8X4),
                    lhsT_scale=scales[:, i * P : (i + 1) * P],
                    rhs=v_codes[:, h, :].bitcast(FP8X4),
                    rhs_scale=v_scales[:, h, :],
                    start=True,
                    stop=True,
                )
            live["o", j, tiles] = o

        def result(j, tiles):
            if ("y", j, tiles) not in live:
                live["y", j, tiles] = work.tile([P, len(tiles) * DV], F32, align_bytes=64, name="y", bufs=9)
            return live["y", j, tiles]

        def copy_o(j, tiles=BOTH, copy=nc.scalar.copy):
            y = result(j, tiles)
            copy(out=y[:], in_=live["o", j, tiles][:])
            nc.sync.dma_start(
                out=out_view[j][:, tiles[0] : tiles[-1] + 1, :], in_=y[:].rearrange("p (i d) -> p i d", d=DV)
            )

        def copy_half(j, i, copy=nc.scalar.copy):
            y = result(j, (i,))
            copy(out=y[:], in_=live["o", j, BOTH][:, i * DV : (i + 1) * DV])
            nc.sync.dma_start(out=out_view[j][:, i : i + 1, :], in_=y[:].rearrange("p (i d) -> p i d", d=DV))

        def copy_last(j, tiles, copy):
            first = TILES * (j % 2) + tiles[0]
            cols = slice(first * DV, (first + len(tiles)) * DV)
            copy(out=last_rows[:, cols], in_=live["o", j, tiles][:])

        def store_last(a, b):
            nc.sync.dma_start(out=out_rows[:, a * DV : b * DV], in_=last_rows[:, a * DV : b * DV])

        def copy_tile(j, i):
            cols = slice(i * DV, (i + 1) * DV)
            y = result(j, BOTH)
            nc.scalar.copy(out=y[:, cols], in_=live["o", j, BOTH][:, cols])
            if i == TILES - 1:
                nc.sync.dma_start(out=out_view[j], in_=y[:].rearrange("p (i d) -> p i d", d=DV))

        def loop_copy_o(j):
            if j not in VECTOR_COPIES:
                copy_o(j)

        def vector_copy_o(j):
            if j in VECTOR_COPIES:
                copy_o(j, BOTH, nc.vector.tensor_copy)

        def prompt_weights(j):
            if j == TAIL - 2:
                weights(j, BOTH, (0,))

        def rest_weights(j):
            weights(j, BOTH, (1,) if j == TAIL - 2 else BOTH)

        def early_bias(j):
            if j == TAIL:
                biases(j)

        def late_bias(j):
            if j != TAIL:
                biases(j)

        S = nc.scalar.copy
        A = (0,)
        B = (1,)
        spread_scales()
        repeat_scales()
        widen_sorted(0, 0)
        widen(0, E, ROW, S)
        turn_q(0, "z", A)
        turn_q(0, "z", B)
        widen_sorted(1, 0)
        widen_sorted(1, 1)
        turn_q(1, "z", A)
        copy_scales()
        sort_keys(0)
        turn_keys(0, "turn_b")
        scale_turned(0, A)
        turn_q(1, "consts", B)
        turn_keys(1, "o")
        widen(2, 0, E, S)
        product(2)
        widen(2, E, ROW, S)
        turn_q(2, "turn_q", B)
        widen(3, 0, ROW, S)
        copy_keys(0, S)
        scale_turned(0, B)
        scale_turned(1)
        turn_q(2, "turn_b", A)
        turn_q(3, "consts")
        widen(4, 0, ROW, S)
        copy_keys(1, S)
        quant_keys(0)
        quant_early(0)
        quant_keys(1)
        product(4)
        scores(0)
        scores(1)
        widen(5, 0, ROW, S)
        start_gains()
        copy_q(2)
        gate_prompts()
        widen(6, 0, ROW, S)
        scale_turned(2)
        scale_turned(3)
        open_consts()
        share_scales()
        spread_gains(0)
        maxima(0, A)
        widen(7, 0, ROW, S)
        widen(8, 0, ROW, S)
        group_values(0)
        biases(0, A)
        maxima(0, B)
        quant_early(1)
        product(5)
        group_values(2, nc.gpsimd.tensor_copy)
        turn_q(4)
        exps(0, A, A)
        biases(0, B)
        exps(0, A, B)
        maxima(1, A)
        exps(0, B)
        recips(0, A)
        maxima(1, B)
        scores(2)
        turn_keys(3, "turn_b")
        group_values(1)
        biases(1)
        copy_q(4)
        weights(0, A)
        recips(0, B)
        exps(1)
        scores(3)
        maxima(2)
        weights(0, B)
        biases(2)
        copy_keys(3, S)
        recips(1)

        step = (
            (quant, 0), (product, LEAD), (widen_gpsimd, LEAD + 1), (weights_gpsimd, -1), (turn_q, 3), (turn_b, -2),
            (outputs, -LAG), (maxima, 1), (exps, 0), (scores, 2), (scale_bytes, LEAD), (prompt_weights, -1),
            (vector_copy_o, -LAG), (rest_weights, -1), (copy_q, 3), (early_bias, 1), (copy_b, -2), (late_bias, 1),
            (recips, 0), (widen_rest, LEAD + 2), (widen_whole, LEAD + 2), (loop_copy_o, -LAG),
        )
        behind = {
            (late_bias, 3): lambda: copy_keys(2, nc.scalar.copy),
            (turn_b, 0): lambda: turn_keys(2, "o"),
            (late_bias, 4): lambda: group_values(3),
            (turn_b, PAIRS_PER_HEAD - 1): lambda: spread_gains(1),
        }
        extra_quants = {2: (quant_values, 0), 3: (quant_keys, 3), 4: (quant_keys, 2), 8: (quant_values, 1)}
        for s in range(2, TAIL):
            if s in extra_quants:
                quant_fn, which = extra_quants[s]
                quant_fn(which)
            for stage_fn, ahead in step:
                if 0 <= s + ahead < PAIRS:
                    stage_fn(s + ahead)
                if (stage_fn, s + ahead) in behind:
                    behind[stage_fn, s + ahead]()

        V = nc.vector.tensor_copy
        TQ = "turn_q"
        quant(29)
        weights_gpsimd(28)
        turn_b(27)
        outputs(25)
        exps(29)
        scores(31)
        maxima(30)
        copy_b(27)
        biases(30)
        copy_o(25)
        weights(28)
        turn_b(28, BOTH, TQ)
        exps(30)
        recips(29)
        quant_b(26)
        weights_gpsimd(29)
        maxima(31, A)
        biases(31, A)
        copy_b(28)
        maxima(31, B)
        biases(31, B)
        outputs(26, BOTH, "z")
        weights(29)
        turn_b(29)
        exps(31)
        recips(30)
        quant_b(27)
        outputs(27, BOTH, "z")
        weights(30)
        copy_b(29)
        copy_o(26)
        turn_b(30, BOTH, TQ)
        recips(31)
        quant_b(28)
        quant_b(29)
        weights(31, A)
        outputs(28, BOTH, "z")
        outputs(29, BOTH, "z")
        copy_o(27)
        copy_b(30)
        turn_b(31, A)
        weights(31, B)
        turn_b(31, B, TQ)
        copy_o(28)
        quant_b(30)
        copy_o(29, BOTH, V)
        copy_b(31, A)
        copy_b(31, B)
        outputs(30, A)
        outputs(30, B, "consts")
        quant_b(31, A)
        quant_b(31, B)
        outputs(31, A, "z")
        outputs(31, B, "z")
        copy_last(30, A, S)
        copy_last(30, B, V)
        store_last(0, 2)
        copy_last(31, A, S)
        copy_last(31, B, V)
        store_last(2, 4)
